import numpy as np
import ml_dtypes


def mxq(x, axis, fmt="e4m3"):
    dtype, down = {"e4m3": (ml_dtypes.float8_e4m3fn, 7), "e5m2": (ml_dtypes.float8_e5m2, 14)}[fmt]
    v = np.moveaxis(np.asarray(x, np.float32).astype(ml_dtypes.bfloat16).astype(np.float64), axis, -1)
    blocks = v.reshape(v.shape[:-1] + (-1, 32))
    amax = np.abs(blocks).max(-1, keepdims=True)
    byte = np.maximum(np.where(amax > 0, np.frexp(amax)[1] - 1 + 127, 0) - down, 1)
    scale = np.exp2(byte - 127.0)
    codes = (blocks / scale).astype(np.float32).astype(dtype).astype(np.float64)
    return np.moveaxis((codes * scale).reshape(v.shape), -1, axis)


WIDE = False


def mx_kscale(k):
    if not WIDE:
        return np.ones(k)
    levels = np.array([10, -10, 5, -5, 0])
    if k % 512:
        return np.exp2(np.random.permutation(np.resize(levels, k // 32))).repeat(32)
    a = np.empty((k // 512, 16))
    for p in range(k // 512):
        a[p, :8] = np.random.permutation(np.resize(levels, 8))
        for g in range(8):
            far = levels[np.abs(levels - a[p, g]) >= 10]
            a[p, g + 8] = far[np.random.randint(len(far))]
    return np.exp2(a.ravel()).repeat(32)


def f64(x):
    return np.asarray(x).astype(np.float64)


def striped(idx):
    return np.tile(idx.reshape(-1, 16).T, (8, 1)).astype(np.uint16)


def unstriped(offs):
    return offs[:16].T.reshape(-1).astype(np.int64)


def striped8(idx):
    return np.concatenate([x.reshape(-1, 16).T for x in idx]).astype(np.uint16)


def runs(offs, k):
    lists = np.stack([offs[16 * r : 16 * r + 16].T.reshape(-1) for r in range(8)]).astype(np.int64)
    return lists[np.arange(k) % 512 // 64]


def pack_weight(w):
    k, n = w.shape
    w = f64(np.asarray(w, np.float32).astype(ml_dtypes.bfloat16)).reshape(k // 32, 32, n)
    amax = np.abs(w).max(1)
    byte = np.clip(np.where(amax > 0, np.frexp(amax)[1] - 1 + 127 - 7, 1), 1, 254)
    scaled = (w * np.exp2(127.0 - byte)[:, None, :]).reshape(k, n).astype(np.float32)
    words = np.ascontiguousarray(scaled.reshape(k // 512, 128, 4, n).transpose(0, 1, 3, 2)).astype(ml_dtypes.float8_e4m3fn).view(np.uint8)
    return words, np.ascontiguousarray(byte.astype(np.uint8).reshape(k // 512, 16, n))


def unpack_weight(words, scales):
    g, p, n, _ = words.shape
    vals = np.ascontiguousarray(words).view(ml_dtypes.float8_e4m3fn).astype(np.float64) * np.repeat(np.exp2(scales.astype(np.float64) - 127.0), 8, axis=1)[..., None]
    return vals.transpose(0, 1, 3, 2).reshape(g * 512, n)


def relu(v):
    return np.maximum(v, 0.0)

def planes(y):
    n, m = y.shape
    v = y.astype(np.float32).astype(ml_dtypes.bfloat16).astype(np.float64).reshape(n // 32, 32, m)
    top = np.abs(v).max(1)
    byte = np.clip(np.where(top > 0, np.frexp(top)[1] - 1 + 127 - 7, 1), 1, 254)
    codes = (v * np.exp2(127.0 - byte)[:, None, :]).reshape(n, m).astype(np.float32).astype(ml_dtypes.float8_e4m3fn).view(np.uint8)
    words = codes.reshape(n // 512, 128, 4, m).transpose(0, 1, 3, 2)
    return np.ascontiguousarray(words), np.ascontiguousarray(byte.astype(np.uint8).reshape(n // 512, 16, m))


K, T, S, N, H = 512, 2048, 512, 512, 512


def setup_inputs():
    n = np.random.standard_normal
    s = mx_kscale(K)[:, None]
    u = mx_kscale(H)
    packed_xT = pack_weight(n((K, T)) * s)
    packed_w2 = pack_weight(n((K, H)) / np.sqrt(K) / s)
    packed_w3 = pack_weight(n((H, N)) / np.sqrt(2 * H) / u[:, None])
    packed_w4 = pack_weight(n((H, N)) / np.sqrt(2 * H) / u[:, None])
    return {
        "x_words": packed_xT[0],
        "x_scales": packed_xT[1],
        "w1": (n((K, H)) / np.sqrt(K) / s * u).astype(np.float32),
        "w2_words": packed_w2[0],
        "w2_scales": packed_w2[1],
        "w3_words": packed_w3[0],
        "w3_scales": packed_w3[1],
        "w4_words": packed_w4[0],
        "w4_scales": packed_w4[1],
        "offs": striped(np.random.permutation(T)[:S]),
        "p1": striped8(np.stack([np.random.permutation(S) for _ in range(8)])),
        "p2": striped8(np.stack([np.random.permutation(S) for _ in range(8)])),
    }


def reference(x_words, x_scales, w1, w2_words, w2_scales, w3_words, w3_scales, w4_words, w4_scales, offs, p1, p2):
    xq = unpack_weight(x_words, x_scales)[:, unstriped(offs)]
    y = mxq(f64(w1), 0, "e4m3").T @ xq
    h1 = y[np.arange(H)[:, None], runs(p1, H)]
    h2 = y[np.arange(H)[:, None], runs(p2, H)]
    z = y + h1 + h2
    c = unpack_weight(w2_words, w2_scales).T @ xq
    z2 = c * h1 + c * h2
    o = unpack_weight(w3_words, w3_scales).T @ mxq(z, 0, "e4m3") + unpack_weight(w4_words, w4_scales).T @ mxq(z2, 0, "e4m3")
    out_0 = relu(o)
    return (out_0,) + planes(out_0)

@@ -1,0 +1,234 @@
+from contextlib import ExitStack
+
+import concourse.mybir as mybir
+
+K, T, S, N, H = 512, 2048, 512, 512, 512
+FLOPS = 2 * S * (2 * K * H + 2 * H * N)
+
+F32 = mybir.dt.float32
+BF16 = mybir.dt.bfloat16
+I32 = mybir.dt.int32
+U32 = mybir.dt.uint32
+U16 = mybir.dt.uint16
+U8 = mybir.dt.uint8
+FP8X4 = mybir.dt.float8_e4m3fn_x4
+ADD = mybir.AluOpType.add
+MULT = mybir.AluOpType.mult
+RELU = mybir.ActivationFunctionType.Relu
+
+P = 128
+PACK = 4
+HALF = 256
+BLK = 128
+LINE = 4
+W1_SPLIT = 88
+
+
+def tile_picked_ngcf8_relu_po_kernel(
+    tc, x_words, x_scales, w1, w2_words, w2_scales, w3_words, w3_scales, w4_words, w4_scales, offs, p1, p2, out_0, out_1, out_2
+):
+    nc = tc.nc
+    with ExitStack() as ctx:
+        keep = ctx.enter_context(tc.tile_pool(name="keep", bufs=1))
+        ring = ctx.enter_context(tc.tile_pool(name="ring", bufs=2))
+        psum = ctx.enter_context(tc.psum_pool(name="psum", bufs=1))
+
+        def words_of(dram):
+            return dram[0].rearrange("p n t -> p (n t)").bitcast(I32)
+
+        def load_scale_rows(queues, plane, first, dram):
+            for q, queue in enumerate(queues):
+                queue.dma_start(
+                    out=plane[32 * q + first : 32 * q + first + 4, :].bitcast(I32),
+                    in_=dram[0, 4 * q : 4 * q + 4, :].bitcast(I32),
+                )
+
+        offs_sb = keep.tile([P, S // 16], U16, name="offs_sb")
+        p1_sb = keep.tile([P, S // 16], U16, name="p1_sb")
+        p2_sb = keep.tile([P, S // 16], U16, name="p2_sb")
+        x_table = keep.tile([P, T], U32, name="x_table", tag="x_table", align_bytes=64)
+        x_scale_table = keep.tile([P, T], U8, name="x_scale_table", align_bytes=64)
+        w1_raw = keep.tile([P, PACK, H], F32, name="w1_raw", tag="w1_raw", align_bytes=64)
+
+        nc.gpsimd.memset(x_scale_table[:].bitcast(I32), 0)
+
+        nc.sync.dma_start(offs_sb[:], offs)
+        nc.sync.dma_start(out=w1_raw[:], in_=w1.rearrange("(p j) c -> p j c", j=PACK))
+        load_scale_rows((nc.scalar,) * 4, x_scale_table, 0, x_scales)
+        nc.sync.dma_start(p1_sb[:], p1)
+        nc.sync.dma_start(p2_sb[:], p2)
+        nc.sync.dma_start(out=x_table[:].bitcast(I32), in_=words_of(x_words))
+
+        w1_bf = keep.tile([P, PACK, P, PACK], BF16, name="w1_bf", tag="w1_bf", align_bytes=64)
+        for copy, lo, hi in ((nc.vector.tensor_copy, 0, W1_SPLIT), (nc.scalar.copy, W1_SPLIT, P)):
+            copy(
+                out=w1_bf[:, :, lo:hi, :].rearrange("p t m j -> p m j t"),
+                in_=w1_raw[:, :, PACK * lo : PACK * hi].rearrange("p j (m t) -> p m j t", t=PACK),
+            )
+        x_scale_picked = keep.tile([P, S], U8, name="x_scale_picked", align_bytes=64)
+        nc.vector.tensor_copy(out=x_scale_picked[:], in_=x_scale_table[:].indirect(offs_sb[:]))
+        w1_codes = keep.tile([P, H], U32, name="w1_codes", align_bytes=64)
+        w1_scales = keep.tile([P, H], U8, name="w1_scales", align_bytes=64)
+        nc.vector.quantize_mx(out=w1_codes[:].bitcast(FP8X4), scales=w1_scales[:], in_=w1_bf[:].rearrange("p t m j -> p (t m j)"))
+
+        w_raw = keep.tile([P, 3, H], I32, name="w_raw", tag="w1_raw", align_bytes=64)
+        for i, words in enumerate((w2_words, w3_words, w4_words)):
+            nc.sync.dma_start(out=w_raw[:, i, :], in_=words_of(words))
+        w_scales_raw = keep.tile([P, H], U8, name="w_scales_raw", tag="w1_bf", align_bytes=64)
+        nc.gpsimd.memset(w_scales_raw[:].bitcast(I32), 0)
+        for i, scales in enumerate((w2_scales, w3_scales, w4_scales)):
+            load_scale_rows((nc.sync,) * 4, w_scales_raw, 4 * i, scales)
+
+        x_picked = [keep.tile([P, HALF], U32, name=f"x_picked{h}", align_bytes=64) for h in range(2)]
+        for h in range(2):
+            nc.vector.tensor_copy(out=x_picked[h][:], in_=x_table[:].indirect(offs_sb[:, h * HALF // 16 : (h + 1) * HALF // 16]))
+
+        y_bank = [psum.tile([P, S], F32, name=f"y_bank{t}", tag=f"bank{t}") for t in range(PACK)]
+        y_window = [keep.tile([P, S], F32, name=f"y_window{t}") for t in range(PACK)]
+        y_plain = keep.tile([P, PACK, S], F32, name="y_plain")
+        for t in range(PACK):
+            for h in range(2):
+                cols = slice(h * HALF, (h + 1) * HALF)
+                nc.tensor.matmul_mx(
+                    out=y_bank[t][:, cols],
+                    lhsT=w1_codes[:, t * P : (t + 1) * P].bitcast(FP8X4),
+                    lhsT_scale=w1_scales[:, t * P : (t + 1) * P],
+                    rhs=x_picked[h][:].bitcast(FP8X4),
+                    rhs_scale=x_scale_picked[:, cols],
+                    start=True,
+                    stop=True,
+                )
+                if t == 0:
+                    nc.scalar.copy(out=y_window[t][:, cols], in_=y_bank[t][:, cols])
+            if t > 0:
+                nc.scalar.copy(out=y_window[t][:], in_=y_bank[t][:])
+        for t in range(PACK):
+            nc.scalar.copy(out=y_plain[:, t, :], in_=y_bank[t][:])
+
+        w_dealt = {}
+
+        def deal(key, raw, dtype, tag):
+            dealt = keep.tile([P, H], dtype, name=f"dealt_{key}", tag=tag, align_bytes=64)
+            w_dealt[key] = dealt
+            nc.vector.tensor_copy(out=dealt[:].rearrange("p (t m) -> p m t", t=PACK), in_=raw.rearrange("p (m t) -> p m t", t=PACK))
+
+        def weight(i, t):
+            cols = slice(t * P, (t + 1) * P)
+            return dict(lhsT=w_dealt[i][:, cols].bitcast(FP8X4), lhsT_scale=w_dealt["scales"][4 * i :, cols])
+
+        first = {}
+        both = {}
+
+        def gather_first(h, t):
+            first[h, t] = keep.tile([P, HALF], F32, name=f"first{h}{t}", tag=f"first{h}{t}", align_bytes=64)
+            nc.vector.tensor_copy(out=first[h, t][:], in_=y_window[t][:].indirect(p1_sb[:, h * HALF // 16 : (h + 1) * HALF // 16]))
+
+        def gather_second(h, t):
+            if t == 0:
+                both[h] = keep.tile([P, PACK, HALF], F32, name=f"both{h}", tag="both")
+            nc.vector.tensor_tensor(both[h][:, t, :], y_window[t][:].indirect(p2_sb[:, h * HALF // 16 : (h + 1) * HALF // 16]), first[h, t][:], ADD)
+
+        def gathers(h, fill):
+            gather_first(h, 0)
+            for t in range(1, PACK):
+                gather_first(h, t)
+                gather_second(h, t - 1)
+                fill(t - 1)
+            gather_second(h, PACK - 1)
+
+        late_deals = ((1, w_raw[:, 1, :], I32), ("scales", w_scales_raw[:], U8), (2, w_raw[:, 2, :], I32))
+        deal(0, w_raw[:, 0, :], I32, "x_table")
+        gathers(0, lambda t: deal(*late_deals[t], f"first0{t}"))
+
+        c_bank = [psum.tile([P, PACK, BLK], F32, name=f"c_bank{b}", tag=f"bank{PACK + b}") for b in range(S // BLK)]
+        for b in range(S // BLK):
+            h, inner = divmod(b * BLK, HALF)
+            for t in range(PACK):
+                nc.tensor.matmul_mx(
+                    out=c_bank[b][:, t, :],
+                    **weight(0, t),
+                    rhs=x_picked[h][:, inner : inner + BLK].bitcast(FP8X4),
+                    rhs_scale=x_scale_picked[:, b * BLK : (b + 1) * BLK],
+                    start=True,
+                    stop=True,
+                )
+
+        out_scales = keep.tile([P, S], U8, name="out_scales", align_bytes=64)
+        out_rows = out_0.rearrange("(p t) j -> p t j", t=PACK)
+        out_words = words_of(out_1)
+        by_lines = "p t (c i) -> p c t i"
+        z_bf = {}
+        z_q = {}
+        o_bf = {}
+
+        def mix(b):
+            h, inner = divmod(b * BLK, HALF)
+            zz = ring.tile([P, 2, BLK, PACK], BF16, name="zz", align_bytes=64)
+            s = both[h][:, :, inner : inner + BLK].rearrange(by_lines, i=LINE)
+            nc.vector.tensor_tensor(
+                zz[:, 1].rearrange("p (c i) t -> p c t i", i=LINE), s, c_bank[b][:].rearrange(by_lines, i=LINE), MULT
+            )
+            nc.vector.tensor_tensor(
+                zz[:, 0].rearrange("p (c i) t -> p c t i", i=LINE), s, y_plain[:, :, b * BLK : (b + 1) * BLK].rearrange(by_lines, i=LINE), ADD
+            )
+            z_bf[b] = zz
+
+        def quantise_z(b):
+            codes = ring.tile([P, 2 * BLK], U32, name="z_codes", align_bytes=64)
+            scales = ring.tile([P, 2 * BLK], U8, name="z_scales", align_bytes=64)
+            nc.vector.quantize_mx(out=codes[:].bitcast(FP8X4), scales=scales[:], in_=z_bf[b][:].rearrange("p z j t -> p (z j t)"))
+            z_q[b] = (codes, scales)
+
+        def second_product(b, banks):
+            codes, scales = z_q[b]
+            o32 = ring.tile([P, PACK, BLK], F32, name="o32")
+            ob = ring.tile([P, BLK, PACK], BF16, name="ob", align_bytes=64)
+            per_bank = PACK // len(banks)
+            for part, bank in enumerate(banks):
+                o_bank = psum.tile([P, per_bank, BLK], F32, name="o_bank", tag=f"bank{bank}")
+                ts = slice(part * per_bank, (part + 1) * per_bank)
+                for t in range(per_bank):
+                    for z in range(2):
+                        cols = slice(z * BLK, (z + 1) * BLK)
+                        nc.tensor.matmul_mx(
+                            out=o_bank[:, t, :],
+                            **weight(1 + z, part * per_bank + t),
+                            rhs=codes[:, cols].bitcast(FP8X4),
+                            rhs_scale=scales[:, cols],
+                            start=(z == 0),
+                            stop=(z == 1),
+                        )
+                ob_view = ob[:, :, ts].rearrange("p (c i) t -> p c t i", i=LINE)
+                if len(banks) == 1:
+                    nc.scalar.activation(ob_view, o_bank[:].rearrange(by_lines, i=LINE), RELU)
+                nc.scalar.activation(o32[:, ts, :], o_bank[:], RELU)
+                if len(banks) > 1:
+                    nc.vector.tensor_copy(out=ob_view, in_=o32[:, ts, :].rearrange(by_lines, i=LINE))
+                nc.sync.dma_start(out=out_rows[:, ts, b * BLK : (b + 1) * BLK], in_=o32[:, ts, :])
+            o_bf[b] = ob
+
+        def quantise_out(b):
+            cols = slice(b * BLK, (b + 1) * BLK)
+            codes = ring.tile([P, BLK], U32, name="out_codes", align_bytes=64)
+            nc.vector.quantize_mx(out=codes[:].bitcast(FP8X4), scales=out_scales[:, cols], in_=o_bf[b][:].rearrange("p j t -> p (j t)"))
+            nc.sync.dma_start(out=out_words[:, cols], in_=codes[:].bitcast(I32))
+
+        mix(0)
+        mix(1)
+        quantise_z(0)
+        quantise_z(1)
+        second_product(0, [0])
+        second_product(1, [1])
+        gathers(1, lambda t: None)
+        mix(2)
+        quantise_out(0)
+        quantise_z(2)
+        second_product(2, [2])
+        mix(3)
+        quantise_out(1)
+        quantise_z(3)
+        quantise_out(2)
+        second_product(3, [3, 0])
+        quantise_out(3)
+        for q, queue in enumerate((nc.sync, nc.scalar, nc.sync, nc.scalar)):
+            queue.dma_start(out=out_2[0, 4 * q : 4 * q + 4, :].bitcast(I32), in_=out_scales[32 * q : 32 * q + 4, :].bitcast(I32))

@@ -30,7 +30,8 @@ def tile_picked_ngcf8_relu_po_kernel(
     nc = tc.nc
     with ExitStack() as ctx:
         keep = ctx.enter_context(tc.tile_pool(name="keep", bufs=1))
-        ring = ctx.enter_context(tc.tile_pool(name="ring", bufs=2))
+        ring = ctx.enter_context(tc.tile_pool(name="ring", bufs=4))
+        reuse = ctx.enter_context(tc.tile_pool(name="reuse", bufs=1))
         psum = ctx.enter_context(tc.psum_pool(name="psum", bufs=1))
 
         def words_of(dram):
@@ -46,7 +47,7 @@ def tile_picked_ngcf8_relu_po_kernel(
         offs_sb = keep.tile([P, S // 16], U16, name="offs_sb")
         p1_sb = keep.tile([P, S // 16], U16, name="p1_sb")
         p2_sb = keep.tile([P, S // 16], U16, name="p2_sb")
-        x_table = keep.tile([P, T], U32, name="x_table", tag="x_table", align_bytes=64)
+        x_table = reuse.tile([P, T], U32, name="x_table", align_bytes=64, offset=0)
         x_scale_table = keep.tile([P, T], U8, name="x_scale_table", align_bytes=64)
         w1_raw = keep.tile([P, PACK, H], F32, name="w1_raw", tag="w1_raw", align_bytes=64)
 
@@ -84,7 +85,9 @@ def tile_picked_ngcf8_relu_po_kernel(
             nc.vector.tensor_copy(out=x_picked[h][:], in_=x_table[:].indirect(offs_sb[:, h * HALF // 16 : (h + 1) * HALF // 16]))
 
         y_bank = [psum.tile([P, S], F32, name=f"y_bank{t}", tag=f"bank{t}") for t in range(PACK)]
-        y_window = [keep.tile([P, S], F32, name=f"y_window{t}") for t in range(PACK)]
+        y_window = [keep.tile([P, 2 * S], F32, name=f"y_window{t}") for t in range(PACK)]
+        for t in range(PACK):
+            nc.gpsimd.memset(y_window[t][:, S:], 0.0)
         y_plain = keep.tile([P, PACK, S], F32, name="y_plain")
         for t in range(PACK):
             for h in range(2):
@@ -101,14 +104,14 @@ def tile_picked_ngcf8_relu_po_kernel(
                 if t == 0:
                     nc.scalar.copy(out=y_window[t][:, cols], in_=y_bank[t][:, cols])
             if t > 0:
-                nc.scalar.copy(out=y_window[t][:], in_=y_bank[t][:])
+                nc.scalar.copy(out=y_window[t][:, :S], in_=y_bank[t][:])
         for t in range(PACK):
             nc.scalar.copy(out=y_plain[:, t, :], in_=y_bank[t][:])
 
         w_dealt = {}
 
-        def deal(key, raw, dtype, tag):
-            dealt = keep.tile([P, H], dtype, name=f"dealt_{key}", tag=tag, align_bytes=64)
+        def deal(key, raw, dtype, pool, **place):
+            dealt = pool.tile([P, H], dtype, name=f"dealt_{key}", align_bytes=64, **place)
             w_dealt[key] = dealt
             nc.vector.tensor_copy(out=dealt[:].rearrange("p (t m) -> p m t", t=PACK), in_=raw.rearrange("p (m t) -> p m t", t=PACK))
 
@@ -116,29 +119,18 @@ def tile_picked_ngcf8_relu_po_kernel(
             cols = slice(t * P, (t + 1) * P)
             return dict(lhsT=w_dealt[i][:, cols].bitcast(FP8X4), lhsT_scale=w_dealt["scales"][4 * i :, cols])
 
-        first = {}
-        both = {}
-
-        def gather_first(h, t):
-            first[h, t] = keep.tile([P, HALF], F32, name=f"first{h}{t}", tag=f"first{h}{t}", align_bytes=64)
-            nc.vector.tensor_copy(out=first[h, t][:], in_=y_window[t][:].indirect(p1_sb[:, h * HALF // 16 : (h + 1) * HALF // 16]))
-
-        def gather_second(h, t):
-            if t == 0:
-                both[h] = keep.tile([P, PACK, HALF], F32, name=f"both{h}", tag="both")
-            nc.vector.tensor_tensor(both[h][:, t, :], y_window[t][:].indirect(p2_sb[:, h * HALF // 16 : (h + 1) * HALF // 16]), first[h, t][:], ADD)
-
-        def gathers(h, fill):
-            gather_first(h, 0)
-            for t in range(1, PACK):
-                gather_first(h, t)
-                gather_second(h, t - 1)
-                fill(t - 1)
-            gather_second(h, PACK - 1)
-
-        late_deals = ((1, w_raw[:, 1, :], I32), ("scales", w_scales_raw[:], U8), (2, w_raw[:, 2, :], I32))
-        deal(0, w_raw[:, 0, :], I32, "x_table")
-        gathers(0, lambda t: deal(*late_deals[t], f"first0{t}"))
+        first = [keep.tile([P, S], F32, name=f"first{t}", tag=f"first{t}", align_bytes=64) for t in range(PACK)]
+        both = keep.tile([P, PACK, S], F32, name="both")
+        late_deals = ((2, w_raw[:, 2, :], I32), ("scales", w_scales_raw[:], U8))
+        for i in range(2):
+            deal(i, w_raw[:, i, :], I32, reuse, offset=4 * H * i)
+        nc.vector.tensor_copy(out=first[0][:], in_=y_window[0][:].indirect(p1_sb[:]))
+        for t in range(PACK):
+            if t + 1 < PACK:
+                nc.vector.tensor_copy(out=first[t + 1][:], in_=y_window[t + 1][:].indirect(p1_sb[:]))
+            nc.vector.tensor_tensor(both[:, t, :], y_window[t][:].indirect(p2_sb[:]), first[t][:], ADD)
+            if t < len(late_deals):
+                deal(*late_deals[t], keep, tag=f"first{t}")
 
         c_bank = [psum.tile([P, PACK, BLK], F32, name=f"c_bank{b}", tag=f"bank{PACK + b}") for b in range(S // BLK)]
         for b in range(S // BLK):
@@ -157,55 +149,55 @@ def tile_picked_ngcf8_relu_po_kernel(
         out_rows = out_0.rearrange("(p t) j -> p t j", t=PACK)
         out_words = words_of(out_1)
         by_lines = "p t (c i) -> p c t i"
+        last = S // BLK - 1
         z_bf = {}
         z_q = {}
         o_bf = {}
+        o_f32 = {}
 
-        def mix(b):
-            h, inner = divmod(b * BLK, HALF)
-            zz = ring.tile([P, 2, BLK, PACK], BF16, name="zz", align_bytes=64)
-            s = both[h][:, :, inner : inner + BLK].rearrange(by_lines, i=LINE)
+        def mix(b, z):
+            if z == 1:
+                z_bf[b] = ring.tile([P, 2, BLK, PACK], BF16, name="zz", align_bytes=64)
+            cols = slice(b * BLK, (b + 1) * BLK)
+            other, op = ((y_plain[:, :, cols], ADD), (c_bank[b][:], MULT))[z]
             nc.vector.tensor_tensor(
-                zz[:, 1].rearrange("p (c i) t -> p c t i", i=LINE), s, c_bank[b][:].rearrange(by_lines, i=LINE), MULT
+                z_bf[b][:, z].rearrange("p (c i) t -> p c t i", i=LINE),
+                both[:, :, cols].rearrange(by_lines, i=LINE),
+                other.rearrange(by_lines, i=LINE),
+                op,
             )
-            nc.vector.tensor_tensor(
-                zz[:, 0].rearrange("p (c i) t -> p c t i", i=LINE), s, y_plain[:, :, b * BLK : (b + 1) * BLK].rearrange(by_lines, i=LINE), ADD
-            )
-            z_bf[b] = zz
 
-        def quantise_z(b):
-            codes = ring.tile([P, 2 * BLK], U32, name="z_codes", align_bytes=64)
-            scales = ring.tile([P, 2 * BLK], U8, name="z_scales", align_bytes=64)
-            nc.vector.quantize_mx(out=codes[:].bitcast(FP8X4), scales=scales[:], in_=z_bf[b][:].rearrange("p z j t -> p (z j t)"))
-            z_q[b] = (codes, scales)
+        def quantise(values, name):
+            width = values.shape[1] // PACK
+            codes = ring.tile([P, width], U32, name=f"{name}_codes", align_bytes=64)
+            scales = ring.tile([P, width], U8, name=f"{name}_scales", align_bytes=64)
+            nc.vector.quantize_mx(out=codes[:].bitcast(FP8X4), scales=scales[:], in_=values)
+            return codes, scales
 
-        def second_product(b, banks):
-            codes, scales = z_q[b]
+        def second_product(b):
+            codes, scales = quantise(z_bf[b][:].rearrange("p z j t -> p (z j t)"), "zz")
             o32 = ring.tile([P, PACK, BLK], F32, name="o32")
-            ob = ring.tile([P, BLK, PACK], BF16, name="ob", align_bytes=64)
-            per_bank = PACK // len(banks)
-            for part, bank in enumerate(banks):
-                o_bank = psum.tile([P, per_bank, BLK], F32, name="o_bank", tag=f"bank{bank}")
-                ts = slice(part * per_bank, (part + 1) * per_bank)
-                for t in range(per_bank):
-                    for z in range(2):
-                        cols = slice(z * BLK, (z + 1) * BLK)
-                        nc.tensor.matmul_mx(
-                            out=o_bank[:, t, :],
-                            **weight(1 + z, part * per_bank + t),
-                            rhs=codes[:, cols].bitcast(FP8X4),
-                            rhs_scale=scales[:, cols],
-                            start=(z == 0),
-                            stop=(z == 1),
-                        )
-                ob_view = ob[:, :, ts].rearrange("p (c i) t -> p c t i", i=LINE)
-                if len(banks) == 1:
-                    nc.scalar.activation(ob_view, o_bank[:].rearrange(by_lines, i=LINE), RELU)
-                nc.scalar.activation(o32[:, ts, :], o_bank[:], RELU)
-                if len(banks) > 1:
-                    nc.vector.tensor_copy(out=ob_view, in_=o32[:, ts, :].rearrange(by_lines, i=LINE))
-                nc.sync.dma_start(out=out_rows[:, ts, b * BLK : (b + 1) * BLK], in_=o32[:, ts, :])
-            o_bf[b] = ob
+            o_bf[b] = keep.tile([P, BLK, PACK], BF16, name=f"o_bf{b}", align_bytes=64)
+            o_bank = psum.tile([P, PACK, BLK], F32, name="o_bank", tag=f"bank{b}")
+            for t in range(PACK):
+                for z in range(2):
+                    cols = slice(z * BLK, (z + 1) * BLK)
+                    nc.tensor.matmul_mx(
+                        out=o_bank[:, t, :],
+                        **weight(1 + z, t),
+                        rhs=codes[:, cols].bitcast(FP8X4),
+                        rhs_scale=scales[:, cols],
+                        start=(z == 0),
+                        stop=(z == 1),
+                    )
+            if b < last - 1:
+                nc.scalar.activation(o_bf[b][:], o_bank[:].rearrange("p t j -> p j t"), RELU)
+            nc.scalar.activation(o32[:], o_bank[:], RELU)
+            o_f32[b] = o32
+            nc.sync.dma_start(out=out_rows[:, :, b * BLK : (b + 1) * BLK], in_=o32[:])
+
+        def round_out(b):
+            nc.vector.tensor_copy(out=o_bf[b][:].rearrange("p (c i) t -> p c t i", i=LINE), in_=o_f32[b][:].rearrange(by_lines, i=LINE))
 
         def quantise_out(b):
             cols = slice(b * BLK, (b + 1) * BLK)
@@ -213,22 +205,37 @@ def tile_picked_ngcf8_relu_po_kernel(
             nc.vector.quantize_mx(out=codes[:].bitcast(FP8X4), scales=out_scales[:, cols], in_=o_bf[b][:].rearrange("p j t -> p (j t)"))
             nc.sync.dma_start(out=out_words[:, cols], in_=codes[:].bitcast(I32))
 
-        mix(0)
-        mix(1)
-        quantise_z(0)
-        quantise_z(1)
-        second_product(0, [0])
-        second_product(1, [1])
-        gathers(1, lambda t: None)
-        mix(2)
+        o_banks = [psum.tile([P, BLK], F32, name=f"o_last{t}", tag=f"bank{last + t}") for t in range(PACK)]
+
+        def last_passes(z):
+            codes, scales = quantise(z_bf[last][:, z].rearrange("p j t -> p (j t)"), "last")
+            for t in range(PACK):
+                nc.tensor.matmul_mx(
+                    out=o_banks[t][:], **weight(1 + z, t), rhs=codes[:].bitcast(FP8X4), rhs_scale=scales[:], start=(z == 1), stop=(z == 0)
+                )
+
+        mix(0, 1)
+        for b in range(last):
+            mix(b, 0)
+            mix(b + 1, 1)
+            second_product(b)
+        last_passes(1)
+        mix(last, 0)
         quantise_out(0)
-        quantise_z(2)
-        second_product(2, [2])
-        mix(3)
+        last_passes(0)
         quantise_out(1)
-        quantise_z(3)
+        round_out(2)
         quantise_out(2)
-        second_product(3, [3, 0])
-        quantise_out(3)
+        o32 = ring.tile([P, PACK, BLK], F32, name="o32")
+        for t in range(PACK):
+            if t % 2 == 0:
+                nc.scalar.activation(o32[:, t, :], o_banks[t][:], RELU)
+            else:
+                nc.vector.tensor_scalar_max(o32[:, t, :], o_banks[t][:], 0.0)
+                nc.sync.dma_start(out=out_rows[:, t - 1 : t + 1, last * BLK :], in_=o32[:, t - 1 : t + 1, :])
+        o_bf[last] = keep.tile([P, BLK, PACK], BF16, name="o_bf_last", align_bytes=64)
+        o_f32[last] = o32
+        round_out(last)
+        quantise_out(last)
         for q, queue in enumerate((nc.sync, nc.scalar, nc.sync, nc.scalar)):
             queue.dma_start(out=out_2[0, 4 * q : 4 * q + 4, :].bitcast(I32), in_=out_scales[32 * q : 32 * q + 4, :].bitcast(I32))

@@ -1,6 +1,7 @@
 from contextlib import ExitStack
 
 import concourse.mybir as mybir
+from concourse.masks import make_identity
 
 K, T, S, N, H = 512, 2048, 512, 512, 512
 FLOPS = 2 * S * (2 * K * H + 2 * H * N)
@@ -18,10 +19,17 @@ RELU = mybir.ActivationFunctionType.Relu
 
 P = 128
 PACK = 4
-HALF = 256
+QUADRANT = 32
+SCALE_ROWS = 4
+LIST_ROWS = 16
+HALF = S // 2
 BLK = 128
+BLOCKS = S // BLK
+LAST = BLOCKS - 1
 LINE = 4
 W1_SPLIT = 88
+W2, W3, W4 = 0, 1, 2
+Z, Z2 = 0, 1
 
 
 def tile_picked_ngcf8_relu_po_kernel(
@@ -30,37 +38,46 @@ def tile_picked_ngcf8_relu_po_kernel(
     nc = tc.nc
     with ExitStack() as ctx:
         keep = ctx.enter_context(tc.tile_pool(name="keep", bufs=1))
-        ring = ctx.enter_context(tc.tile_pool(name="ring", bufs=4))
+        ring = ctx.enter_context(tc.tile_pool(name="ring", bufs=BLOCKS))
         reuse = ctx.enter_context(tc.tile_pool(name="reuse", bufs=1))
         psum = ctx.enter_context(tc.psum_pool(name="psum", bufs=1))
 
         def words_of(dram):
             return dram[0].rearrange("p n t -> p (n t)").bitcast(I32)
 
-        def load_scale_rows(queues, plane, first, dram):
-            for q, queue in enumerate(queues):
+        def load_scale_rows(queue, tile, shift, dram):
+            for q in range(P // QUADRANT):
                 queue.dma_start(
-                    out=plane[32 * q + first : 32 * q + first + 4, :].bitcast(I32),
-                    in_=dram[0, 4 * q : 4 * q + 4, :].bitcast(I32),
+                    out=tile[QUADRANT * q + shift : QUADRANT * q + shift + SCALE_ROWS, :].bitcast(I32),
+                    in_=dram[0, SCALE_ROWS * q : SCALE_ROWS * (q + 1), :].bitcast(I32),
                 )
 
-        offs_sb = keep.tile([P, S // 16], U16, name="offs_sb")
-        p1_sb = keep.tile([P, S // 16], U16, name="p1_sb")
-        p2_sb = keep.tile([P, S // 16], U16, name="p2_sb")
+        def block_cols(b):
+            return slice(b * BLK, (b + 1) * BLK)
+
+        offs_sb = keep.tile([P, S // LIST_ROWS], U16, name="offs_sb")
+        p1_sb = keep.tile([P, S // LIST_ROWS], U16, name="p1_sb")
+        p2_sb = keep.tile([P, S // LIST_ROWS], U16, name="p2_sb")
         x_table = reuse.tile([P, T], U32, name="x_table", align_bytes=64, offset=0)
         x_scale_table = keep.tile([P, T], U8, name="x_scale_table", align_bytes=64)
-        w1_raw = keep.tile([P, PACK, H], F32, name="w1_raw", tag="w1_raw", align_bytes=64)
+        w1_raw = keep.tile([P, PACK, H], F32, name="w1_raw", tag="raw_weights", align_bytes=64)
 
         nc.gpsimd.memset(x_scale_table[:].bitcast(I32), 0)
 
+        y_window = [keep.tile([P, 2 * S], F32, name=f"y_window{t}") for t in range(PACK)]
+        for t in range(PACK):
+            nc.gpsimd.memset(y_window[t][:, S:], 0.0)
+        identity = keep.tile([P, P], F32, name="identity")
+        make_identity(nc, identity[:])
+
         nc.sync.dma_start(offs_sb[:], offs)
         nc.sync.dma_start(out=w1_raw[:], in_=w1.rearrange("(p j) c -> p j c", j=PACK))
-        load_scale_rows((nc.scalar,) * 4, x_scale_table, 0, x_scales)
+        load_scale_rows(nc.scalar, x_scale_table, 0, x_scales)
         nc.sync.dma_start(p1_sb[:], p1)
         nc.sync.dma_start(p2_sb[:], p2)
         nc.sync.dma_start(out=x_table[:].bitcast(I32), in_=words_of(x_words))
 
-        w1_bf = keep.tile([P, PACK, P, PACK], BF16, name="w1_bf", tag="w1_bf", align_bytes=64)
+        w1_bf = keep.tile([P, PACK, P, PACK], BF16, name="w1_bf", tag="chain", align_bytes=64)
         for copy, lo, hi in ((nc.vector.tensor_copy, 0, W1_SPLIT), (nc.scalar.copy, W1_SPLIT, P)):
             copy(
                 out=w1_bf[:, :, lo:hi, :].rearrange("p t m j -> p m j t"),
@@ -72,23 +89,21 @@ def tile_picked_ngcf8_relu_po_kernel(
         w1_scales = keep.tile([P, H], U8, name="w1_scales", align_bytes=64)
         nc.vector.quantize_mx(out=w1_codes[:].bitcast(FP8X4), scales=w1_scales[:], in_=w1_bf[:].rearrange("p t m j -> p (t m j)"))
 
-        w_raw = keep.tile([P, 3, H], I32, name="w_raw", tag="w1_raw", align_bytes=64)
+        w_raw = keep.tile([P, 3, H], I32, name="w_raw", tag="raw_weights", align_bytes=64)
         for i, words in enumerate((w2_words, w3_words, w4_words)):
             nc.sync.dma_start(out=w_raw[:, i, :], in_=words_of(words))
-        w_scales_raw = keep.tile([P, H], U8, name="w_scales_raw", tag="w1_bf", align_bytes=64)
+        w_scales_raw = keep.tile([P, H], U8, name="w_scales_raw", tag="chain", align_bytes=64)
         nc.gpsimd.memset(w_scales_raw[:].bitcast(I32), 0)
         for i, scales in enumerate((w2_scales, w3_scales, w4_scales)):
-            load_scale_rows((nc.sync,) * 4, w_scales_raw, 4 * i, scales)
+            load_scale_rows(nc.sync, w_scales_raw, SCALE_ROWS * i, scales)
 
         x_picked = [keep.tile([P, HALF], U32, name=f"x_picked{h}", align_bytes=64) for h in range(2)]
         for h in range(2):
-            nc.vector.tensor_copy(out=x_picked[h][:], in_=x_table[:].indirect(offs_sb[:, h * HALF // 16 : (h + 1) * HALF // 16]))
+            entries = offs_sb[:, h * HALF // LIST_ROWS : (h + 1) * HALF // LIST_ROWS]
+            nc.vector.tensor_copy(out=x_picked[h][:], in_=x_table[:].indirect(entries))
 
         y_bank = [psum.tile([P, S], F32, name=f"y_bank{t}", tag=f"bank{t}") for t in range(PACK)]
-        y_window = [keep.tile([P, 2 * S], F32, name=f"y_window{t}") for t in range(PACK)]
-        for t in range(PACK):
-            nc.gpsimd.memset(y_window[t][:, S:], 0.0)
-        y_plain = keep.tile([P, PACK, S], F32, name="y_plain")
+        y_plain = keep.tile([P, 2, S], F32, name="y_plain")
         for t in range(PACK):
             for h in range(2):
                 cols = slice(h * HALF, (h + 1) * HALF)
@@ -105,42 +120,48 @@ def tile_picked_ngcf8_relu_po_kernel(
                     nc.scalar.copy(out=y_window[t][:, cols], in_=y_bank[t][:, cols])
             if t > 0:
                 nc.scalar.copy(out=y_window[t][:, :S], in_=y_bank[t][:])
-        for t in range(PACK):
-            nc.scalar.copy(out=y_plain[:, t, :], in_=y_bank[t][:])
+        for e in range(2):
+            nc.scalar.copy(out=y_plain[:, e, :], in_=y_bank[2 + e][:])
 
-        w_dealt = {}
+        dealt = {}
 
         def deal(key, raw, dtype, pool, **place):
-            dealt = pool.tile([P, H], dtype, name=f"dealt_{key}", align_bytes=64, **place)
-            w_dealt[key] = dealt
-            nc.vector.tensor_copy(out=dealt[:].rearrange("p (t m) -> p m t", t=PACK), in_=raw.rearrange("p (m t) -> p m t", t=PACK))
+            dealt[key] = pool.tile([P, H], dtype, name=f"dealt_{key}", align_bytes=64, **place)
+            nc.vector.tensor_copy(out=dealt[key][:].rearrange("p (t m) -> p m t", t=PACK), in_=raw.rearrange("p (m t) -> p m t", t=PACK))
 
         def weight(i, t):
             cols = slice(t * P, (t + 1) * P)
-            return dict(lhsT=w_dealt[i][:, cols].bitcast(FP8X4), lhsT_scale=w_dealt["scales"][4 * i :, cols])
+            return dict(lhsT=dealt[i][:, cols].bitcast(FP8X4), lhsT_scale=dealt["scales"][SCALE_ROWS * i :, cols])
 
-        first = [keep.tile([P, S], F32, name=f"first{t}", tag=f"first{t}", align_bytes=64) for t in range(PACK)]
-        both = keep.tile([P, PACK, S], F32, name="both")
-        late_deals = ((2, w_raw[:, 2, :], I32), ("scales", w_scales_raw[:], U8))
-        for i in range(2):
+        h_sum = keep.tile([P, PACK, S], F32, name="h_sum")
+        for i in (W2, W3):
             deal(i, w_raw[:, i, :], I32, reuse, offset=4 * H * i)
-        nc.vector.tensor_copy(out=first[0][:], in_=y_window[0][:].indirect(p1_sb[:]))
+
+        h1_tags = ("h1_0", "h1_1", "h1_2", "chain")
+        late_deals = {1: ("scales", w_scales_raw[:], U8), 3: (W4, w_raw[:, W4, :], I32)}
+        h1 = {}
+
+        def gather_h1(t):
+            h1[t] = keep.tile([P, S], F32, name=f"h1_{t}", tag=h1_tags[t], align_bytes=64)
+            nc.vector.tensor_copy(out=h1[t][:], in_=y_window[t][:].indirect(p1_sb[:]))
+
+        gather_h1(0)
         for t in range(PACK):
             if t + 1 < PACK:
-                nc.vector.tensor_copy(out=first[t + 1][:], in_=y_window[t + 1][:].indirect(p1_sb[:]))
-            nc.vector.tensor_tensor(both[:, t, :], y_window[t][:].indirect(p2_sb[:]), first[t][:], ADD)
-            if t < len(late_deals):
-                deal(*late_deals[t], keep, tag=f"first{t}")
+                gather_h1(t + 1)
+            nc.vector.tensor_tensor(h_sum[:, t, :], y_window[t][:].indirect(p2_sb[:]), h1[t][:], ADD)
+            if t in late_deals:
+                deal(*late_deals[t], keep, tag=h1_tags[t])
 
-        c_bank = [psum.tile([P, PACK, BLK], F32, name=f"c_bank{b}", tag=f"bank{PACK + b}") for b in range(S // BLK)]
-        for b in range(S // BLK):
+        c_bank = [psum.tile([P, PACK, BLK], F32, name=f"c_bank{b}", tag=f"bank{PACK + b}") for b in range(BLOCKS)]
+        for b in range(BLOCKS):
             h, inner = divmod(b * BLK, HALF)
             for t in range(PACK):
                 nc.tensor.matmul_mx(
                     out=c_bank[b][:, t, :],
-                    **weight(0, t),
+                    **weight(W2, t),
                     rhs=x_picked[h][:, inner : inner + BLK].bitcast(FP8X4),
-                    rhs_scale=x_scale_picked[:, b * BLK : (b + 1) * BLK],
+                    rhs_scale=x_scale_picked[:, block_cols(b)],
                     start=True,
                     stop=True,
                 )
@@ -149,20 +170,33 @@ def tile_picked_ngcf8_relu_po_kernel(
         out_rows = out_0.rearrange("(p t) j -> p t j", t=PACK)
         out_words = words_of(out_1)
         by_lines = "p t (c i) -> p c t i"
-        last = S // BLK - 1
-        z_bf = {}
-        z_q = {}
+
+        z_bf = [keep.tile([P, 2, BLK, PACK], BF16, name=f"z_bf{b}", align_bytes=64) for b in range(BLOCKS)]
+        back = psum.tile([P, BLOCKS, BLK], F32, name="back", tag="bank2")
+        for h in range(2):
+            turned = psum.tile([P, 2, 2, P], F32, name="turned", tag=f"bank{h}")
+            for i in range(2):
+                cols = block_cols(2 * h + i)
+                for e in range(2):
+                    nc.tensor.matmul(turned[:, i, e, :], y_window[e][:, cols], identity[:], is_transpose=True, start=True, stop=False)
+                    nc.tensor.matmul(turned[:, i, e, :], h_sum[:, e, cols], identity[:], is_transpose=True, start=False, stop=True)
+            turned_bf = ring.tile([P, 2, P, 2], BF16, name="turned_bf", align_bytes=64)
+            nc.scalar.copy(out=turned_bf[:], in_=turned[:].rearrange("j i e p -> j i p e"))
+            turned_pairs = turned_bf[:].rearrange("j i p e -> j i (p e)").bitcast(F32)
+            for i in range(2):
+                nc.tensor.transpose(back[:, 2 * h + i, :], turned_pairs[:, i, :], identity[:])
+        for b in range(BLOCKS):
+            z_pairs = z_bf[b][:, Z].rearrange("p j t -> p (j t)").bitcast(F32).rearrange("p (j u) -> p j u", u=2)
+            nc.scalar.copy(out=z_pairs[:, :, 0], in_=back[:, b, :])
         o_bf = {}
         o_f32 = {}
 
-        def mix(b, z):
-            if z == 1:
-                z_bf[b] = ring.tile([P, 2, BLK, PACK], BF16, name="zz", align_bytes=64)
-            cols = slice(b * BLK, (b + 1) * BLK)
-            other, op = ((y_plain[:, :, cols], ADD), (c_bank[b][:], MULT))[z]
+        def mix(b, which):
+            cols = block_cols(b)
+            planes, other, op = ((slice(2, PACK), y_plain[:, :, cols], ADD), (slice(0, PACK), c_bank[b][:], MULT))[which]
             nc.vector.tensor_tensor(
-                z_bf[b][:, z].rearrange("p (c i) t -> p c t i", i=LINE),
-                both[:, :, cols].rearrange(by_lines, i=LINE),
+                z_bf[b][:, which, :, planes].rearrange("p (c i) t -> p c t i", i=LINE),
+                h_sum[:, planes, cols].rearrange(by_lines, i=LINE),
                 other.rearrange(by_lines, i=LINE),
                 op,
             )
@@ -175,67 +209,74 @@ def tile_picked_ngcf8_relu_po_kernel(
             return codes, scales
 
         def second_product(b):
-            codes, scales = quantise(z_bf[b][:].rearrange("p z j t -> p (z j t)"), "zz")
-            o32 = ring.tile([P, PACK, BLK], F32, name="o32")
+            codes, scales = quantise(z_bf[b][:].rearrange("p z j t -> p (z j t)"), "both")
+            o_f32[b] = ring.tile([P, PACK, BLK], F32, name="o_f32")
             o_bf[b] = keep.tile([P, BLK, PACK], BF16, name=f"o_bf{b}", align_bytes=64)
             o_bank = psum.tile([P, PACK, BLK], F32, name="o_bank", tag=f"bank{b}")
             for t in range(PACK):
-                for z in range(2):
-                    cols = slice(z * BLK, (z + 1) * BLK)
+                for which in (Z, Z2):
                     nc.tensor.matmul_mx(
                         out=o_bank[:, t, :],
-                        **weight(1 + z, t),
-                        rhs=codes[:, cols].bitcast(FP8X4),
-                        rhs_scale=scales[:, cols],
-                        start=(z == 0),
-                        stop=(z == 1),
+                        **weight(W3 + which, t),
+                        rhs=codes[:, block_cols(which)].bitcast(FP8X4),
+                        rhs_scale=scales[:, block_cols(which)],
+                        start=(which == Z),
+                        stop=(which == Z2),
                     )
-            if b < last - 1:
+            if b < LAST - 1:
                 nc.scalar.activation(o_bf[b][:], o_bank[:].rearrange("p t j -> p j t"), RELU)
-            nc.scalar.activation(o32[:], o_bank[:], RELU)
-            o_f32[b] = o32
-            nc.sync.dma_start(out=out_rows[:, :, b * BLK : (b + 1) * BLK], in_=o32[:])
+            nc.scalar.activation(o_f32[b][:], o_bank[:], RELU)
+            nc.sync.dma_start(out=out_rows[:, :, block_cols(b)], in_=o_f32[b][:])
 
         def round_out(b):
             nc.vector.tensor_copy(out=o_bf[b][:].rearrange("p (c i) t -> p c t i", i=LINE), in_=o_f32[b][:].rearrange(by_lines, i=LINE))
 
         def quantise_out(b):
-            cols = slice(b * BLK, (b + 1) * BLK)
+            cols = block_cols(b)
             codes = ring.tile([P, BLK], U32, name="out_codes", align_bytes=64)
             nc.vector.quantize_mx(out=codes[:].bitcast(FP8X4), scales=out_scales[:, cols], in_=o_bf[b][:].rearrange("p j t -> p (j t)"))
             nc.sync.dma_start(out=out_words[:, cols], in_=codes[:].bitcast(I32))
 
-        o_banks = [psum.tile([P, BLK], F32, name=f"o_last{t}", tag=f"bank{last + t}") for t in range(PACK)]
+        last_banks = [psum.tile([P, BLK], F32, name=f"o_last{t}", tag=f"bank{LAST + t}") for t in range(PACK)]
 
-        def last_passes(z):
-            codes, scales = quantise(z_bf[last][:, z].rearrange("p j t -> p (j t)"), "last")
+        def last_passes(which):
+            codes, scales = quantise(z_bf[LAST][:, which].rearrange("p j t -> p (j t)"), "last")
             for t in range(PACK):
                 nc.tensor.matmul_mx(
-                    out=o_banks[t][:], **weight(1 + z, t), rhs=codes[:].bitcast(FP8X4), rhs_scale=scales[:], start=(z == 1), stop=(z == 0)
+                    out=last_banks[t][:],
+                    **weight(W3 + which, t),
+                    rhs=codes[:].bitcast(FP8X4),
+                    rhs_scale=scales[:],
+                    start=(which == Z2),
+                    stop=(which == Z),
                 )
 
-        mix(0, 1)
-        for b in range(last):
-            mix(b, 0)
-            mix(b + 1, 1)
+        mix(0, Z2)
+        for b in range(LAST):
+            mix(b, Z)
+            mix(b + 1, Z2)
             second_product(b)
-        last_passes(1)
-        mix(last, 0)
+        last_passes(Z2)
+        mix(LAST, Z)
         quantise_out(0)
-        last_passes(0)
+        last_passes(Z)
         quantise_out(1)
-        round_out(2)
-        quantise_out(2)
-        o32 = ring.tile([P, PACK, BLK], F32, name="o32")
+        round_out(LAST - 1)
+        quantise_out(LAST - 1)
+
+        o_f32[LAST] = ring.tile([P, PACK, BLK], F32, name="o_f32")
         for t in range(PACK):
             if t % 2 == 0:
-                nc.scalar.activation(o32[:, t, :], o_banks[t][:], RELU)
+                nc.scalar.activation(o_f32[LAST][:, t, :], last_banks[t][:], RELU)
             else:
-                nc.vector.tensor_scalar_max(o32[:, t, :], o_banks[t][:], 0.0)
-                nc.sync.dma_start(out=out_rows[:, t - 1 : t + 1, last * BLK :], in_=o32[:, t - 1 : t + 1, :])
-        o_bf[last] = keep.tile([P, BLK, PACK], BF16, name="o_bf_last", align_bytes=64)
-        o_f32[last] = o32
-        round_out(last)
-        quantise_out(last)
+                nc.vector.tensor_scalar_max(o_f32[LAST][:, t, :], last_banks[t][:], 0.0)
+                nc.sync.dma_start(out=out_rows[:, t - 1 : t + 1, block_cols(LAST)], in_=o_f32[LAST][:, t - 1 : t + 1, :])
+        o_bf[LAST] = keep.tile([P, BLK, PACK], BF16, name="o_bf_last", align_bytes=64)
+        round_out(LAST)
+        quantise_out(LAST)
+
         for q, queue in enumerate((nc.sync, nc.scalar, nc.sync, nc.scalar)):
-            queue.dma_start(out=out_2[0, 4 * q : 4 * q + 4, :].bitcast(I32), in_=out_scales[32 * q : 32 * q + 4, :].bitcast(I32))
+            queue.dma_start(
+                out=out_2[0, SCALE_ROWS * q : SCALE_ROWS * (q + 1), :].bitcast(I32),
+                in_=out_scales[QUADRANT * q : QUADRANT * q + SCALE_ROWS, :].bitcast(I32),
+            )

@@ -26,8 +26,8 @@ HALF = S // 2
 BLK = 128
 BLOCKS = S // BLK
 LAST = BLOCKS - 1
-LINE = 4
-W1_SPLIT = 88
+LINE = 2
+W1_SPLIT = 40
 W2, W3, W4 = 0, 1, 2
 Z, Z2 = 0, 1
 
@@ -40,6 +40,7 @@ def tile_picked_ngcf8_relu_po_kernel(
         keep = ctx.enter_context(tc.tile_pool(name="keep", bufs=1))
         ring = ctx.enter_context(tc.tile_pool(name="ring", bufs=BLOCKS))
         reuse = ctx.enter_context(tc.tile_pool(name="reuse", bufs=1))
+        late = ctx.enter_context(tc.tile_pool(name="late", bufs=1))
         psum = ctx.enter_context(tc.psum_pool(name="psum", bufs=1))
 
         def words_of(dram):
@@ -60,13 +61,15 @@ def tile_picked_ngcf8_relu_po_kernel(
         p2_sb = keep.tile([P, S // LIST_ROWS], U16, name="p2_sb")
         x_table = reuse.tile([P, T], U32, name="x_table", align_bytes=64, offset=0)
         x_scale_table = keep.tile([P, T], U8, name="x_scale_table", align_bytes=64)
-        w1_raw = keep.tile([P, PACK, H], F32, name="w1_raw", tag="raw_weights", align_bytes=64)
+        w1_raw = keep.tile([P, PACK, H], F32, name="w1_raw", align_bytes=64)
+        w_tags = ("w2_raw", "w3_raw", "h1_0")
+        w_raw = [keep.tile([P, H], I32, name=f"w_raw{i}", tag=w_tags[i], align_bytes=64) for i in range(3)]
+        w_scales_room = late.tile([P, 3 * 4 * HALF], U8, name="w_scales_room", align_bytes=64, offset=0)
+        w_scales_raw = w_scales_room[:, :H]
 
         nc.gpsimd.memset(x_scale_table[:].bitcast(I32), 0)
-
-        y_window = [keep.tile([P, 2 * S], F32, name=f"y_window{t}") for t in range(PACK)]
-        for t in range(PACK):
-            nc.gpsimd.memset(y_window[t][:, S:], 0.0)
+        nc.gpsimd.memset(w_scales_raw.bitcast(I32), 0)
+        y_window = [keep.tile([P, S], F32, name=f"y_window{t}") for t in range(PACK)]
         identity = keep.tile([P, P], F32, name="identity")
         make_identity(nc, identity[:])
 
@@ -76,52 +79,54 @@ def tile_picked_ngcf8_relu_po_kernel(
         nc.sync.dma_start(p1_sb[:], p1)
         nc.sync.dma_start(p2_sb[:], p2)
         nc.sync.dma_start(out=x_table[:].bitcast(I32), in_=words_of(x_words))
+        for i, words in enumerate((w2_words, w3_words, w4_words)):
+            nc.sync.dma_start(out=w_raw[i][:], in_=words_of(words))
+        for i, scales in enumerate((w2_scales, w3_scales, w4_scales)):
+            load_scale_rows(nc.sync, w_scales_raw, SCALE_ROWS * i, scales)
 
-        w1_bf = keep.tile([P, PACK, P, PACK], BF16, name="w1_bf", tag="chain", align_bytes=64)
+        def half_cols(h):
+            return slice(h * HALF, (h + 1) * HALF)
+
+        def entries(tile, h):
+            return tile[:, h * HALF // LIST_ROWS : (h + 1) * HALF // LIST_ROWS]
+
+        x_scale_picked = keep.tile([P, S], U8, name="x_scale_picked", align_bytes=64)
+        nc.vector.tensor_copy(out=x_scale_picked[:], in_=x_scale_table[:].indirect(offs_sb[:]))
+        w1_bf = keep.tile([P, PACK, P, PACK], BF16, name="w1_bf", align_bytes=64)
         for copy, lo, hi in ((nc.vector.tensor_copy, 0, W1_SPLIT), (nc.scalar.copy, W1_SPLIT, P)):
             copy(
                 out=w1_bf[:, :, lo:hi, :].rearrange("p t m j -> p m j t"),
                 in_=w1_raw[:, :, PACK * lo : PACK * hi].rearrange("p j (m t) -> p m j t", t=PACK),
             )
-        x_scale_picked = keep.tile([P, S], U8, name="x_scale_picked", align_bytes=64)
-        nc.vector.tensor_copy(out=x_scale_picked[:], in_=x_scale_table[:].indirect(offs_sb[:]))
         w1_codes = keep.tile([P, H], U32, name="w1_codes", align_bytes=64)
         w1_scales = keep.tile([P, H], U8, name="w1_scales", align_bytes=64)
-        nc.vector.quantize_mx(out=w1_codes[:].bitcast(FP8X4), scales=w1_scales[:], in_=w1_bf[:].rearrange("p t m j -> p (t m j)"))
 
-        w_raw = keep.tile([P, 3, H], I32, name="w_raw", tag="raw_weights", align_bytes=64)
-        for i, words in enumerate((w2_words, w3_words, w4_words)):
-            nc.sync.dma_start(out=w_raw[:, i, :], in_=words_of(words))
-        w_scales_raw = keep.tile([P, H], U8, name="w_scales_raw", tag="chain", align_bytes=64)
-        nc.gpsimd.memset(w_scales_raw[:].bitcast(I32), 0)
-        for i, scales in enumerate((w2_scales, w3_scales, w4_scales)):
-            load_scale_rows(nc.sync, w_scales_raw, SCALE_ROWS * i, scales)
+        def quantise_w1(planes):
+            cols = slice(planes.start * P, planes.stop * P)
+            nc.vector.quantize_mx(out=w1_codes[:, cols].bitcast(FP8X4), scales=w1_scales[:, cols], in_=w1_bf[:, planes].rearrange("p t m j -> p (t m j)"))
 
-        x_picked = [keep.tile([P, HALF], U32, name=f"x_picked{h}", align_bytes=64) for h in range(2)]
+        quantise_w1(slice(0, 2))
+        x_picked = keep.tile([P, S], U32, name="x_picked", align_bytes=64)
         for h in range(2):
-            entries = offs_sb[:, h * HALF // LIST_ROWS : (h + 1) * HALF // LIST_ROWS]
-            nc.vector.tensor_copy(out=x_picked[h][:], in_=x_table[:].indirect(entries))
+            nc.vector.tensor_copy(out=x_picked[:, half_cols(h)], in_=x_table[:].indirect(entries(offs_sb, h)))
+        quantise_w1(slice(2, PACK))
 
         y_bank = [psum.tile([P, S], F32, name=f"y_bank{t}", tag=f"bank{t}") for t in range(PACK)]
-        y_plain = keep.tile([P, 2, S], F32, name="y_plain")
+        y_first = psum.tile([P, HALF], F32, name="y_first", tag=f"bank{PACK}")
         for t in range(PACK):
-            for h in range(2):
-                cols = slice(h * HALF, (h + 1) * HALF)
+            for h in range(2) if t == 0 else (None,):
+                cols = slice(0, S) if h is None else half_cols(h)
+                bank = y_first[:] if h == 0 else y_bank[t][:, cols]
                 nc.tensor.matmul_mx(
-                    out=y_bank[t][:, cols],
-                    lhsT=w1_codes[:, t * P : (t + 1) * P].bitcast(FP8X4),
-                    lhsT_scale=w1_scales[:, t * P : (t + 1) * P],
-                    rhs=x_picked[h][:].bitcast(FP8X4),
+                    out=bank,
+                    lhsT=w1_codes[:, block_cols(t)].bitcast(FP8X4),
+                    lhsT_scale=w1_scales[:, block_cols(t)],
+                    rhs=x_picked[:, cols].bitcast(FP8X4),
                     rhs_scale=x_scale_picked[:, cols],
                     start=True,
                     stop=True,
                 )
-                if t == 0:
-                    nc.scalar.copy(out=y_window[t][:, cols], in_=y_bank[t][:, cols])
-            if t > 0:
-                nc.scalar.copy(out=y_window[t][:, :S], in_=y_bank[t][:])
-        for e in range(2):
-            nc.scalar.copy(out=y_plain[:, e, :], in_=y_bank[2 + e][:])
+                nc.scalar.copy(out=y_window[t][:, cols], in_=bank)
 
         dealt = {}
 
@@ -133,147 +138,152 @@ def tile_picked_ngcf8_relu_po_kernel(
             cols = slice(t * P, (t + 1) * P)
             return dict(lhsT=dealt[i][:, cols].bitcast(FP8X4), lhsT_scale=dealt["scales"][SCALE_ROWS * i :, cols])
 
-        h_sum = keep.tile([P, PACK, S], F32, name="h_sum")
-        for i in (W2, W3):
-            deal(i, w_raw[:, i, :], I32, reuse, offset=4 * H * i)
+        for i in (W2, W3, W4):
+            deal(i, w_raw[i][:], I32, reuse, offset=4 * H * i)
 
-        h1_tags = ("h1_0", "h1_1", "h1_2", "chain")
-        late_deals = {1: ("scales", w_scales_raw[:], U8), 3: (W4, w_raw[:, W4, :], I32)}
-        h1 = {}
-
-        def gather_h1(t):
-            h1[t] = keep.tile([P, S], F32, name=f"h1_{t}", tag=h1_tags[t], align_bytes=64)
-            nc.vector.tensor_copy(out=h1[t][:], in_=y_window[t][:].indirect(p1_sb[:]))
-
-        gather_h1(0)
+        turned = [psum.tile([P, 2, 2, P], F32, name=f"turned{u}", tag=f"bank{2 * u}") for u in range(2)]
+        for u in range(2):
+            for e in range(2):
+                for i in range(2):
+                    nc.tensor.matmul(
+                        turned[u][:, i, e, :], y_window[2 * u + e][:, block_cols(i)], identity[:],
+                        is_transpose=True, start=(e == 0 and i == 0), stop=False,
+                    )
+        y_plain = keep.tile([P, PACK, HALF], F32, name="y_plain")
         for t in range(PACK):
-            if t + 1 < PACK:
-                gather_h1(t + 1)
-            nc.vector.tensor_tensor(h_sum[:, t, :], y_window[t][:].indirect(p2_sb[:]), h1[t][:], ADD)
-            if t in late_deals:
-                deal(*late_deals[t], keep, tag=h1_tags[t])
+            nc.scalar.copy(out=y_plain[:, t, :], in_=y_window[t][:, half_cols(1)])
 
+        h_sum = keep.tile([P, PACK, S], F32, name="h_sum")
+        h1 = {}
+        z_half = [keep.tile([P, HALF, PACK], BF16, name=f"z_half{w}", tag=f"z_half{w}", align_bytes=64) for w in (Z, Z2)]
+        z_block = {b: keep.tile([P, 2, BLK, PACK], BF16, name=f"z_block{b}", align_bytes=64) for b in (2, 3)}
+
+        def gather_h1(t, h, pool, **place):
+            h1[t, h] = pool.tile([P, S if h is None else HALF], F32, name=f"h1_{t}{h}", align_bytes=64, **place)
+            nc.vector.tensor_copy(out=h1[t, h][:], in_=y_window[t][:].indirect(p1_sb[:] if h is None else entries(p1_sb, h)))
+
+        def gather_h2(t, h):
+            cols = slice(0, S) if h is None else half_cols(h)
+            nc.vector.tensor_tensor(h_sum[:, t, cols], y_window[t][:].indirect(p2_sb[:] if h is None else entries(p2_sb, h)), h1[t, h][:], ADD)
+            u, e = divmod(t, 2)
+            if h != 1:
+                for i in range(2):
+                    nc.tensor.matmul(
+                        turned[u][:, i, e, :], h_sum[:, t, block_cols(i)], identity[:],
+                        is_transpose=True, start=False, stop=(e == 1 and i == 1),
+                    )
+
+        back = psum.tile([P, 2, 2, BLK], F32, name="back", tag="bank1")
+
+        def turn_back(u):
+            turned_bf = keep.tile([P, 2, P, 2], BF16, name=f"turned_bf{u}", tag=f"turned_bf{u}", align_bytes=64)
+            nc.scalar.copy(out=turned_bf[:], in_=turned[u][:].rearrange("j i e p -> j i p e"))
+            pairs = turned_bf[:].rearrange("j i p e -> j i (p e)").bitcast(F32)
+            for i in range(2):
+                nc.tensor.transpose(back[:, i, u, :], pairs[:, i, :], identity[:])
+
+        gather_h1(0, 0, keep, tag="h1_0")
+        deal("scales", w_scales_raw, U8, keep)
         c_bank = [psum.tile([P, PACK, BLK], F32, name=f"c_bank{b}", tag=f"bank{PACK + b}") for b in range(BLOCKS)]
         for b in range(BLOCKS):
-            h, inner = divmod(b * BLK, HALF)
             for t in range(PACK):
                 nc.tensor.matmul_mx(
                     out=c_bank[b][:, t, :],
                     **weight(W2, t),
-                    rhs=x_picked[h][:, inner : inner + BLK].bitcast(FP8X4),
+                    rhs=x_picked[:, block_cols(b)].bitcast(FP8X4),
                     rhs_scale=x_scale_picked[:, block_cols(b)],
                     start=True,
                     stop=True,
                 )
+        gather_h1(1, 0, late, offset=0)
+        gather_h2(0, 0)
+        gather_h1(2, 0, late, offset=4 * HALF)
+        gather_h1(3, 0, late, offset=8 * HALF)
+        gather_h2(1, 0)
+        turn_back(0)
+        gather_h2(2, 0)
+        gather_h2(3, 0)
+        turn_back(1)
+        z_words = z_half[Z][:].rearrange("p j t -> p (j t)").bitcast(F32).rearrange("p (i j u) -> p i j u", i=2, u=2)
+        nc.scalar.copy(out=z_words, in_=back[:].rearrange("p i u j -> p i j u"))
 
         out_scales = keep.tile([P, S], U8, name="out_scales", align_bytes=64)
         out_rows = out_0.rearrange("(p t) j -> p t j", t=PACK)
         out_words = words_of(out_1)
         by_lines = "p t (c i) -> p c t i"
+        o_bank, o_f32, o_bf = {}, {}, {}
 
-        z_bf = [keep.tile([P, 2, BLK, PACK], BF16, name=f"z_bf{b}", align_bytes=64) for b in range(BLOCKS)]
-        back = psum.tile([P, BLOCKS, BLK], F32, name="back", tag="bank2")
-        for h in range(2):
-            turned = psum.tile([P, 2, 2, P], F32, name="turned", tag=f"bank{h}")
-            for i in range(2):
-                cols = block_cols(2 * h + i)
-                for e in range(2):
-                    nc.tensor.matmul(turned[:, i, e, :], y_window[e][:, cols], identity[:], is_transpose=True, start=True, stop=False)
-                    nc.tensor.matmul(turned[:, i, e, :], h_sum[:, e, cols], identity[:], is_transpose=True, start=False, stop=True)
-            turned_bf = ring.tile([P, 2, P, 2], BF16, name="turned_bf", align_bytes=64)
-            nc.scalar.copy(out=turned_bf[:], in_=turned[:].rearrange("j i e p -> j i p e"))
-            turned_pairs = turned_bf[:].rearrange("j i p e -> j i (p e)").bitcast(F32)
-            for i in range(2):
-                nc.tensor.transpose(back[:, 2 * h + i, :], turned_pairs[:, i, :], identity[:])
-        for b in range(BLOCKS):
-            z_pairs = z_bf[b][:, Z].rearrange("p j t -> p (j t)").bitcast(F32).rearrange("p (j u) -> p j u", u=2)
-            nc.scalar.copy(out=z_pairs[:, :, 0], in_=back[:, b, :])
-        o_bf = {}
-        o_f32 = {}
+        def z_values(b, which):
+            return z_half[which][:, block_cols(b), :] if b < 2 else z_block[b][:, which]
 
         def mix(b, which):
-            cols = block_cols(b)
-            planes, other, op = ((slice(2, PACK), y_plain[:, :, cols], ADD), (slice(0, PACK), c_bank[b][:], MULT))[which]
+            other, op = (c_bank[b][:], MULT) if which == Z2 else (y_plain[:, :, block_cols(b - 2)], ADD)
             nc.vector.tensor_tensor(
-                z_bf[b][:, which, :, planes].rearrange("p (c i) t -> p c t i", i=LINE),
-                h_sum[:, planes, cols].rearrange(by_lines, i=LINE),
+                z_values(b, which).rearrange("p (c i) t -> p c t i", i=LINE),
+                h_sum[:, :, block_cols(b)].rearrange(by_lines, i=LINE),
                 other.rearrange(by_lines, i=LINE),
                 op,
             )
 
-        def quantise(values, name):
-            width = values.shape[1] // PACK
-            codes = ring.tile([P, width], U32, name=f"{name}_codes", align_bytes=64)
-            scales = ring.tile([P, width], U8, name=f"{name}_scales", align_bytes=64)
+        def quantise(values, parts, **place):
+            width = BLK * len(parts)
+            codes = keep.tile([P, width], U32, name=f"codes{parts[0][0]}{parts[0][1]}", align_bytes=64, **place)
+            scales = keep.tile([P, width], U8, name=f"scales{parts[0][0]}{parts[0][1]}", align_bytes=64)
             nc.vector.quantize_mx(out=codes[:].bitcast(FP8X4), scales=scales[:], in_=values)
-            return codes, scales
-
-        def second_product(b):
-            codes, scales = quantise(z_bf[b][:].rearrange("p z j t -> p (z j t)"), "both")
-            o_f32[b] = ring.tile([P, PACK, BLK], F32, name="o_f32")
-            o_bf[b] = keep.tile([P, BLK, PACK], BF16, name=f"o_bf{b}", align_bytes=64)
-            o_bank = psum.tile([P, PACK, BLK], F32, name="o_bank", tag=f"bank{b}")
-            for t in range(PACK):
-                for which in (Z, Z2):
+            for i, (b, which) in enumerate(parts):
+                first = b not in o_bank
+                if first:
+                    o_bank[b] = psum.tile([P, PACK, BLK], F32, name=f"o_bank{b}", tag=f"bank{PACK + b}")
+                for t in range(PACK):
                     nc.tensor.matmul_mx(
-                        out=o_bank[:, t, :],
+                        out=o_bank[b][:, t, :],
                         **weight(W3 + which, t),
-                        rhs=codes[:, block_cols(which)].bitcast(FP8X4),
-                        rhs_scale=scales[:, block_cols(which)],
-                        start=(which == Z),
-                        stop=(which == Z2),
+                        rhs=codes[:, block_cols(i)].bitcast(FP8X4),
+                        rhs_scale=scales[:, block_cols(i)],
+                        start=(first and t == 0),
+                        stop=(not first and t == PACK - 1),
                     )
-            if b < LAST - 1:
-                nc.scalar.activation(o_bf[b][:], o_bank[:].rearrange("p t j -> p j t"), RELU)
-            nc.scalar.activation(o_f32[b][:], o_bank[:], RELU)
-            nc.sync.dma_start(out=out_rows[:, :, block_cols(b)], in_=o_f32[b][:])
 
-        def round_out(b):
-            nc.vector.tensor_copy(out=o_bf[b][:].rearrange("p (c i) t -> p c t i", i=LINE), in_=o_f32[b][:].rearrange(by_lines, i=LINE))
+        def empty(b):
+            o_f32[b] = ring.tile([P, PACK, BLK], F32, name="o_f32")
+            o_bf[b] = ring.tile([P, BLK, PACK], BF16, name="o_bf", align_bytes=64)
+            nc.scalar.activation(o_bf[b][:], o_bank[b][:].rearrange("p t j -> p j t"), RELU)
+            nc.scalar.activation(o_f32[b][:], o_bank[b][:], RELU)
+            nc.sync.dma_start(out=out_rows[:, :, block_cols(b)], in_=o_f32[b][:])
 
         def quantise_out(b):
             cols = block_cols(b)
-            codes = ring.tile([P, BLK], U32, name="out_codes", align_bytes=64)
-            nc.vector.quantize_mx(out=codes[:].bitcast(FP8X4), scales=out_scales[:, cols], in_=o_bf[b][:].rearrange("p j t -> p (j t)"))
-            nc.sync.dma_start(out=out_words[:, cols], in_=codes[:].bitcast(I32))
+            out_codes = ring.tile([P, BLK], U32, name="out_codes", align_bytes=64)
+            nc.vector.quantize_mx(out=out_codes[:].bitcast(FP8X4), scales=out_scales[:, cols], in_=o_bf[b][:].rearrange("p j t -> p (j t)"))
+            nc.sync.dma_start(out=out_words[:, cols], in_=out_codes[:].bitcast(I32))
 
-        last_banks = [psum.tile([P, BLK], F32, name=f"o_last{t}", tag=f"bank{LAST + t}") for t in range(PACK)]
-
-        def last_passes(which):
-            codes, scales = quantise(z_bf[LAST][:, which].rearrange("p j t -> p (j t)"), "last")
-            for t in range(PACK):
-                nc.tensor.matmul_mx(
-                    out=last_banks[t][:],
-                    **weight(W3 + which, t),
-                    rhs=codes[:].bitcast(FP8X4),
-                    rhs_scale=scales[:],
-                    start=(which == Z2),
-                    stop=(which == Z),
-                )
-
+        flat = "p j t -> p (j t)"
+        for t in range(2):
+            gather_h1(t, 1, reuse, offset=4 * H * W2 + 4 * HALF * t)
         mix(0, Z2)
-        for b in range(LAST):
-            mix(b, Z)
-            mix(b + 1, Z2)
-            second_product(b)
-        last_passes(Z2)
-        mix(LAST, Z)
+        mix(1, Z2)
+        gather_h1(2, 1, late, offset=8 * HALF)
+        quantise(z_half[Z2][:].rearrange(flat), [(0, Z2), (1, Z2)], tag="turned_bf1")
+        gather_h2(0, 1)
+        gather_h2(1, 1)
+        quantise(z_half[Z][:].rearrange(flat), [(0, Z), (1, Z)])
+        empty(0)
+        empty(1)
+        gather_h1(3, 1, keep, tag=f"z_half{Z}")
+        gather_h2(2, 1)
+        gather_h2(3, 1)
+        mix(2, Z2)
+        mix(2, Z)
+        mix(3, Z2)
+        quantise(z_block[2][:].rearrange("p z j t -> p (z j t)"), [(2, Z), (2, Z2)])
+        empty(2)
+        mix(3, Z)
+        quantise(z_block[3][:, Z2].rearrange(flat), [(3, Z2)])
         quantise_out(0)
-        last_passes(Z)
-        quantise_out(1)
-        round_out(LAST - 1)
-        quantise_out(LAST - 1)
-
-        o_f32[LAST] = ring.tile([P, PACK, BLK], F32, name="o_f32")
-        for t in range(PACK):
-            if t % 2 == 0:
-                nc.scalar.activation(o_f32[LAST][:, t, :], last_banks[t][:], RELU)
-            else:
-                nc.vector.tensor_scalar_max(o_f32[LAST][:, t, :], last_banks[t][:], 0.0)
-                nc.sync.dma_start(out=out_rows[:, t - 1 : t + 1, block_cols(LAST)], in_=o_f32[LAST][:, t - 1 : t + 1, :])
-        o_bf[LAST] = keep.tile([P, BLK, PACK], BF16, name="o_bf_last", align_bytes=64)
-        round_out(LAST)
-        quantise_out(LAST)
+        quantise(z_block[3][:, Z].rearrange(flat), [(3, Z)])
+        empty(3)
+        for b in range(1, BLOCKS):
+            quantise_out(b)
 
         for q, queue in enumerate((nc.sync, nc.scalar, nc.sync, nc.scalar)):
             queue.dma_start(

@@ -82,7 +82,7 @@ def tile_picked_ngcf8_relu_po_kernel(
         for i, words in enumerate((w2_words, w3_words, w4_words)):
             nc.sync.dma_start(out=w_raw[i][:], in_=words_of(words))
         for i, scales in enumerate((w2_scales, w3_scales, w4_scales)):
-            load_scale_rows(nc.sync, w_scales_raw, SCALE_ROWS * i, scales)
+            load_scale_rows(nc.gpsimd if i == W4 else nc.sync, w_scales_raw, SCALE_ROWS * i, scales)
 
         def half_cols(h):
             return slice(h * HALF, (h + 1) * HALF)
@@ -141,47 +141,51 @@ def tile_picked_ngcf8_relu_po_kernel(
         for i in (W2, W3, W4):
             deal(i, w_raw[i][:], I32, reuse, offset=4 * H * i)
 
-        turned = [psum.tile([P, 2, 2, P], F32, name=f"turned{u}", tag=f"bank{2 * u}") for u in range(2)]
-        for u in range(2):
-            for e in range(2):
-                for i in range(2):
-                    nc.tensor.matmul(
-                        turned[u][:, i, e, :], y_window[2 * u + e][:, block_cols(i)], identity[:],
-                        is_transpose=True, start=(e == 0 and i == 0), stop=False,
-                    )
+        turned_low = psum.tile([P, 2, 2, P], F32, name="turned_low", tag="bank0")
+        turned_high = [psum.tile([P, 2, P], F32, name=f"turned_high{i}", tag=f"bank{2 + i}") for i in range(2)]
+
+        def turn(source, t, last):
+            u, e = divmod(t, 2)
+            for i in range(2):
+                edge = e == last and (u == 1 or i == last)
+                nc.tensor.matmul(
+                    turned_high[i][:, e, :] if u else turned_low[:, i, e, :], source[:, block_cols(i)], identity[:],
+                    is_transpose=True, start=edge and not last, stop=edge and bool(last),
+                )
+
+        for t in range(PACK):
+            turn(y_window[t], t, 0)
         y_plain = keep.tile([P, PACK, HALF], F32, name="y_plain")
         for t in range(PACK):
             nc.scalar.copy(out=y_plain[:, t, :], in_=y_window[t][:, half_cols(1)])
 
-        h_sum = keep.tile([P, PACK, S], F32, name="h_sum")
+        h_sum = {0: keep.tile([P, PACK, HALF], F32, name="h_sum0")}
         h1 = {}
-        z_half = [keep.tile([P, HALF, PACK], BF16, name=f"z_half{w}", tag=f"z_half{w}", align_bytes=64) for w in (Z, Z2)]
+        z_early = [late.tile([P, HALF, PACK], BF16, name=f"z_early{w}", align_bytes=64, offset=4 * HALF * (3 + 2 * w)) for w in (Z, Z2)]
         z_block = {b: keep.tile([P, 2, BLK, PACK], BF16, name=f"z_block{b}", align_bytes=64) for b in (2, 3)}
+        by_lines = "p t (c i) -> p c t i"
+
+        def z_values(b, which):
+            return z_early[which][:, block_cols(b), :] if b < 2 else z_block[b][:, which]
 
         def gather_h1(t, h, pool, **place):
-            h1[t, h] = pool.tile([P, S if h is None else HALF], F32, name=f"h1_{t}{h}", align_bytes=64, **place)
-            nc.vector.tensor_copy(out=h1[t, h][:], in_=y_window[t][:].indirect(p1_sb[:] if h is None else entries(p1_sb, h)))
+            h1[t, h] = pool.tile([P, HALF], F32, name=f"h1_{t}{h}", align_bytes=64, **place)
+            nc.vector.tensor_copy(out=h1[t, h][:], in_=y_window[t][:].indirect(entries(p1_sb, h)))
 
         def gather_h2(t, h):
-            cols = slice(0, S) if h is None else half_cols(h)
-            nc.vector.tensor_tensor(h_sum[:, t, cols], y_window[t][:].indirect(p2_sb[:] if h is None else entries(p2_sb, h)), h1[t, h][:], ADD)
-            u, e = divmod(t, 2)
-            if h != 1:
-                for i in range(2):
-                    nc.tensor.matmul(
-                        turned[u][:, i, e, :], h_sum[:, t, block_cols(i)], identity[:],
-                        is_transpose=True, start=False, stop=(e == 1 and i == 1),
-                    )
+            nc.vector.tensor_tensor(h_sum[h][:, t, :], y_window[t][:].indirect(entries(p2_sb, h)), h1[t, h][:], ADD)
+            if h == 0:
+                turn(h_sum[0][:, t, :], t, 1)
 
-        back = psum.tile([P, 2, 2, BLK], F32, name="back", tag="bank1")
+        def mix(engine, b, other, which, line):
+            engine.tensor_tensor(
+                z_values(b, which).rearrange("p (c i) t -> p c t i", i=line),
+                h_sum[b // 2][:, :, block_cols(b % 2)].rearrange(by_lines, i=line),
+                other.rearrange(by_lines, i=line),
+                MULT if which == Z2 else ADD,
+            )
 
-        def turn_back(u):
-            turned_bf = keep.tile([P, 2, P, 2], BF16, name=f"turned_bf{u}", tag=f"turned_bf{u}", align_bytes=64)
-            nc.scalar.copy(out=turned_bf[:], in_=turned[u][:].rearrange("j i e p -> j i p e"))
-            pairs = turned_bf[:].rearrange("j i p e -> j i (p e)").bitcast(F32)
-            for i in range(2):
-                nc.tensor.transpose(back[:, i, u, :], pairs[:, i, :], identity[:])
-
+        slots = [dict(offset=4 * HALF * i) for i in range(3)]
         gather_h1(0, 0, keep, tag="h1_0")
         deal("scales", w_scales_raw, U8, keep)
         c_bank = [psum.tile([P, PACK, BLK], F32, name=f"c_bank{b}", tag=f"bank{PACK + b}") for b in range(BLOCKS)]
@@ -195,61 +199,62 @@ def tile_picked_ngcf8_relu_po_kernel(
                     start=True,
                     stop=True,
                 )
-        gather_h1(1, 0, late, offset=0)
+        c_first = keep.tile([P, PACK, BLK], F32, name="c_first")
+        nc.scalar.copy(out=c_first[:], in_=c_bank[0][:])
+        gather_h1(1, 0, late, **slots[0])
         gather_h2(0, 0)
-        gather_h1(2, 0, late, offset=4 * HALF)
-        gather_h1(3, 0, late, offset=8 * HALF)
+        gather_h1(2, 0, late, **slots[1])
         gather_h2(1, 0)
-        turn_back(0)
+        low_bf = keep.tile([P, 2, P, 2], BF16, name="low_bf", tag="low_bf", align_bytes=64)
+        nc.scalar.copy(out=low_bf[:], in_=turned_low[:].rearrange("j i e p -> j i p e"))
+        back = [psum.tile([P, 2, BLK], F32, name=f"back{i}", tag=f"bank{i}") for i in range(2)]
+        for i in range(2):
+            nc.tensor.transpose(back[i][:, 0, :], low_bf[:, i].rearrange("j p e -> j (p e)").bitcast(F32), identity[:])
+        gather_h1(3, 0, late, **slots[2])
         gather_h2(2, 0)
         gather_h2(3, 0)
-        turn_back(1)
-        z_words = z_half[Z][:].rearrange("p j t -> p (j t)").bitcast(F32).rearrange("p (i j u) -> p i j u", i=2, u=2)
-        nc.scalar.copy(out=z_words, in_=back[:].rearrange("p i u j -> p i j u"))
+        for i in range(2):
+            high_bf = keep.tile([P, P, 2], BF16, name=f"high_bf{i}", tag=f"high_bf{i}", align_bytes=64)
+            nc.scalar.copy(out=high_bf[:], in_=turned_high[i][:].rearrange("j e p -> j p e"))
+            nc.tensor.transpose(back[i][:, 1, :], high_bf[:].rearrange("j p e -> j (p e)").bitcast(F32), identity[:])
+        for i in range(2):
+            z_words = z_values(i, Z).rearrange("p j t -> p (j t)").bitcast(F32).rearrange("p (j u) -> p j u", u=2)
+            nc.scalar.copy(out=z_words, in_=back[i][:].rearrange("p u j -> p j u"))
+        mix(nc.gpsimd, 0, c_first[:], Z2, 4)
 
         out_scales = keep.tile([P, S], U8, name="out_scales", align_bytes=64)
         out_rows = out_0.rearrange("(p t) j -> p t j", t=PACK)
         out_words = words_of(out_1)
-        by_lines = "p t (c i) -> p c t i"
         o_bank, o_f32, o_bf = {}, {}, {}
-
-        def z_values(b, which):
-            return z_half[which][:, block_cols(b), :] if b < 2 else z_block[b][:, which]
-
-        def mix(b, which):
-            other, op = (c_bank[b][:], MULT) if which == Z2 else (y_plain[:, :, block_cols(b - 2)], ADD)
-            nc.vector.tensor_tensor(
-                z_values(b, which).rearrange("p (c i) t -> p c t i", i=LINE),
-                h_sum[:, :, block_cols(b)].rearrange(by_lines, i=LINE),
-                other.rearrange(by_lines, i=LINE),
-                op,
-            )
 
         def quantise(values, parts, **place):
             width = BLK * len(parts)
             codes = keep.tile([P, width], U32, name=f"codes{parts[0][0]}{parts[0][1]}", align_bytes=64, **place)
             scales = keep.tile([P, width], U8, name=f"scales{parts[0][0]}{parts[0][1]}", align_bytes=64)
             nc.vector.quantize_mx(out=codes[:].bitcast(FP8X4), scales=scales[:], in_=values)
-            for i, (b, which) in enumerate(parts):
+            for i, (b, which) in sorted(enumerate(parts), key=lambda part: part[1][0]):
                 first = b not in o_bank
+                group = 2 if b == LAST else PACK
                 if first:
-                    o_bank[b] = psum.tile([P, PACK, BLK], F32, name=f"o_bank{b}", tag=f"bank{PACK + b}")
+                    tags = (2, 3) if b == LAST else (PACK + b,)
+                    o_bank[b] = [psum.tile([P, group, BLK], F32, name=f"o_bank{b}{k}", tag=f"bank{k}") for k in tags]
                 for t in range(PACK):
                     nc.tensor.matmul_mx(
-                        out=o_bank[b][:, t, :],
+                        out=o_bank[b][t // group][:, t % group, :],
                         **weight(W3 + which, t),
                         rhs=codes[:, block_cols(i)].bitcast(FP8X4),
                         rhs_scale=scales[:, block_cols(i)],
-                        start=(first and t == 0),
-                        stop=(not first and t == PACK - 1),
+                        start=(first and t % group == 0),
+                        stop=(not first and t % group == group - 1),
                     )
 
         def empty(b):
             o_f32[b] = ring.tile([P, PACK, BLK], F32, name="o_f32")
             o_bf[b] = ring.tile([P, BLK, PACK], BF16, name="o_bf", align_bytes=64)
-            nc.scalar.activation(o_bf[b][:], o_bank[b][:].rearrange("p t j -> p j t"), RELU)
-            nc.scalar.activation(o_f32[b][:], o_bank[b][:], RELU)
+            nc.scalar.activation(o_f32[b][:], o_bank[b][0][:], RELU)
             nc.sync.dma_start(out=out_rows[:, :, block_cols(b)], in_=o_f32[b][:])
+            if b < 2:
+                nc.scalar.activation(o_bf[b][:], o_bank[b][0][:].rearrange("p t j -> p j t"), RELU)
 
         def quantise_out(b):
             cols = block_cols(b)
@@ -258,32 +263,40 @@ def tile_picked_ngcf8_relu_po_kernel(
             nc.sync.dma_start(out=out_words[:, cols], in_=out_codes[:].bitcast(I32))
 
         flat = "p j t -> p (j t)"
-        for t in range(2):
-            gather_h1(t, 1, reuse, offset=4 * H * W2 + 4 * HALF * t)
-        mix(0, Z2)
-        mix(1, Z2)
-        gather_h1(2, 1, late, offset=8 * HALF)
-        quantise(z_half[Z2][:].rearrange(flat), [(0, Z2), (1, Z2)], tag="turned_bf1")
-        gather_h2(0, 1)
-        gather_h2(1, 1)
-        quantise(z_half[Z][:].rearrange(flat), [(0, Z), (1, Z)])
+        gather_h1(0, 1, late, **slots[1])
+        gather_h1(1, 1, late, **slots[2])
+        gather_h1(2, 1, reuse, offset=4 * H * W2)
+        mix(nc.vector, 1, c_bank[1][:], Z2, LINE)
+        gather_h1(3, 1, reuse, offset=4 * H * W2 + 4 * HALF)
+        quantise(z_early[Z2][:].rearrange(flat), [(0, Z2), (1, Z2)], tag="high_bf1")
+        quantise(z_early[Z][:].rearrange(flat), [(0, Z), (1, Z)])
         empty(0)
         empty(1)
-        gather_h1(3, 1, keep, tag=f"z_half{Z}")
-        gather_h2(2, 1)
-        gather_h2(3, 1)
-        mix(2, Z2)
-        mix(2, Z)
-        mix(3, Z2)
+        h_sum[1] = late.tile([P, PACK, HALF], F32, name="h_sum1", align_bytes=64, offset=4 * HALF * 3)
+        for t in range(PACK):
+            gather_h2(t, 1)
+        mix(nc.vector, 2, c_bank[2][:], Z2, LINE)
+        mix(nc.vector, 2, y_plain[:, :, block_cols(0)], Z, LINE)
+        mix(nc.vector, 3, c_bank[3][:], Z2, LINE)
         quantise(z_block[2][:].rearrange("p z j t -> p (z j t)"), [(2, Z), (2, Z2)])
         empty(2)
-        mix(3, Z)
-        quantise(z_block[3][:, Z2].rearrange(flat), [(3, Z2)])
+        mix(nc.vector, 3, y_plain[:, :, block_cols(1)], Z, LINE)
+        quantise(z_values(3, Z2).rearrange(flat), [(3, Z2)])
         quantise_out(0)
-        quantise(z_block[3][:, Z].rearrange(flat), [(3, Z)])
-        empty(3)
-        for b in range(1, BLOCKS):
-            quantise_out(b)
+        quantise(z_values(3, Z).rearrange(flat), [(3, Z)])
+        quantise_out(1)
+        nc.vector.tensor_copy(out=o_bf[2][:].rearrange("p (c i) t -> p c t i", i=4), in_=o_f32[2][:].rearrange(by_lines, i=4))
+        low, high = o_bank[LAST]
+        last_f32 = [keep.tile([P, 2, BLK], F32, name=f"last_f32{u}") for u in range(2)]
+        o_bf[LAST] = keep.tile([P, BLK, PACK], BF16, name="last_bf", align_bytes=64)
+        nc.scalar.activation(last_f32[0][:], low[:], RELU)
+        nc.sync.dma_start(out=out_rows[:, 0:2, block_cols(LAST)], in_=last_f32[0][:])
+        nc.vector.tensor_scalar_max(o_bf[LAST][:, :, 2:], high[:].rearrange("p e j -> p j e"), 0.0)
+        quantise_out(2)
+        nc.scalar.activation(o_bf[LAST][:, :, :2], low[:].rearrange("p e j -> p j e"), RELU)
+        nc.vector.tensor_scalar_max(last_f32[1][:], high[:], 0.0)
+        nc.sync.dma_start(out=out_rows[:, 2:, block_cols(LAST)], in_=last_f32[1][:])
+        quantise_out(LAST)
 
         for q, queue in enumerate((nc.sync, nc.scalar, nc.sync, nc.scalar)):
             queue.dma_start(

@@ -27,7 +27,7 @@ BLK = 128
 BLOCKS = S // BLK
 LAST = BLOCKS - 1
 LINE = 2
-W1_SPLIT = 40
+W1_SPLIT = 60
 W2, W3, W4 = 0, 1, 2
 Z, Z2 = 0, 1
 
@@ -186,7 +186,7 @@ def tile_picked_ngcf8_relu_po_kernel(
             )
 
         slots = [dict(offset=4 * HALF * i) for i in range(3)]
-        gather_h1(0, 0, keep, tag="h1_0")
+        gather_h1(0, 0, keep)
         deal("scales", w_scales_raw, U8, keep)
         c_bank = [psum.tile([P, PACK, BLK], F32, name=f"c_bank{b}", tag=f"bank{PACK + b}") for b in range(BLOCKS)]
         for b in range(BLOCKS):
@@ -225,7 +225,7 @@ def tile_picked_ngcf8_relu_po_kernel(
         out_scales = keep.tile([P, S], U8, name="out_scales", align_bytes=64)
         out_rows = out_0.rearrange("(p t) j -> p t j", t=PACK)
         out_words = words_of(out_1)
-        o_bank, o_f32, o_bf = {}, {}, {}
+        o_bank = {}
 
         def quantise(values, parts, **place):
             width = BLK * len(parts)
@@ -248,19 +248,19 @@ def tile_picked_ngcf8_relu_po_kernel(
                         stop=(not first and t % group == group - 1),
                     )
 
-        def empty(b):
-            o_f32[b] = ring.tile([P, PACK, BLK], F32, name="o_f32")
-            o_bf[b] = ring.tile([P, BLK, PACK], BF16, name="o_bf", align_bytes=64)
-            nc.scalar.activation(o_f32[b][:], o_bank[b][0][:], RELU)
-            nc.sync.dma_start(out=out_rows[:, :, block_cols(b)], in_=o_f32[b][:])
-            if b < 2:
-                nc.scalar.activation(o_bf[b][:], o_bank[b][0][:].rearrange("p t j -> p j t"), RELU)
+        early_f32 = keep.tile([P, PACK, HALF], F32, name="early_f32")
+        out_bf = [keep.tile([P, HALF, PACK], BF16, name=f"out_bf{h}", align_bytes=64) for h in range(2)]
+        out_codes = [keep.tile([P, HALF], U32, name=f"out_codes{h}", align_bytes=64) for h in range(2)]
 
-        def quantise_out(b):
-            cols = block_cols(b)
-            out_codes = ring.tile([P, BLK], U32, name="out_codes", align_bytes=64)
-            nc.vector.quantize_mx(out=out_codes[:].bitcast(FP8X4), scales=out_scales[:, cols], in_=o_bf[b][:].rearrange("p j t -> p (j t)"))
-            nc.sync.dma_start(out=out_words[:, cols], in_=out_codes[:].bitcast(I32))
+        def empty_early(b):
+            nc.scalar.activation(early_f32[:, :, block_cols(b)], o_bank[b][0][:], RELU)
+            nc.scalar.activation(out_bf[0][:, block_cols(b), :], o_bank[b][0][:].rearrange("p t j -> p j t"), RELU)
+
+        def quantise_out(h, inner):
+            cols = slice(h * HALF + inner.start, h * HALF + inner.stop)
+            nc.vector.quantize_mx(out=out_codes[h][:, inner].bitcast(FP8X4), scales=out_scales[:, cols], in_=out_bf[h][:, inner, :].rearrange("p j t -> p (j t)"))
+            if inner.stop == HALF:
+                nc.sync.dma_start(out=out_words[:, half_cols(h)], in_=out_codes[h][:].bitcast(I32))
 
         flat = "p j t -> p (j t)"
         gather_h1(0, 1, late, **slots[1])
@@ -270,33 +270,36 @@ def tile_picked_ngcf8_relu_po_kernel(
         gather_h1(3, 1, reuse, offset=4 * H * W2 + 4 * HALF)
         quantise(z_early[Z2][:].rearrange(flat), [(0, Z2), (1, Z2)], tag="high_bf1")
         quantise(z_early[Z][:].rearrange(flat), [(0, Z), (1, Z)])
-        empty(0)
-        empty(1)
+        empty_early(0)
+        empty_early(1)
+        nc.sync.dma_start(out=out_rows[:, :, half_cols(0)], in_=early_f32[:])
         h_sum[1] = late.tile([P, PACK, HALF], F32, name="h_sum1", align_bytes=64, offset=4 * HALF * 3)
         for t in range(PACK):
             gather_h2(t, 1)
         mix(nc.vector, 2, c_bank[2][:], Z2, LINE)
         mix(nc.vector, 2, y_plain[:, :, block_cols(0)], Z, LINE)
+        quantise(z_values(2, Z2).rearrange(flat), [(2, Z2)])
         mix(nc.vector, 3, c_bank[3][:], Z2, LINE)
-        quantise(z_block[2][:].rearrange("p z j t -> p (z j t)"), [(2, Z), (2, Z2)])
-        empty(2)
-        mix(nc.vector, 3, y_plain[:, :, block_cols(1)], Z, LINE)
+        quantise(z_values(2, Z).rearrange(flat), [(2, Z)])
+        third_f32 = keep.tile([P, PACK, BLK], F32, name="third_f32")
+        nc.scalar.activation(third_f32[:], o_bank[2][0][:], RELU)
+        nc.sync.dma_start(out=out_rows[:, :, block_cols(2)], in_=third_f32[:])
         quantise(z_values(3, Z2).rearrange(flat), [(3, Z2)])
-        quantise_out(0)
+        mix(nc.vector, 3, y_plain[:, :, block_cols(1)], Z, LINE)
+        quantise_out(0, half_cols(0))
         quantise(z_values(3, Z).rearrange(flat), [(3, Z)])
-        quantise_out(1)
-        nc.vector.tensor_copy(out=o_bf[2][:].rearrange("p (c i) t -> p c t i", i=4), in_=o_f32[2][:].rearrange(by_lines, i=4))
+        nc.vector.tensor_copy(out=out_bf[1][:, block_cols(0), :].rearrange("p (c i) t -> p c t i", i=4), in_=third_f32[:].rearrange(by_lines, i=4))
         low, high = o_bank[LAST]
         last_f32 = [keep.tile([P, 2, BLK], F32, name=f"last_f32{u}") for u in range(2)]
-        o_bf[LAST] = keep.tile([P, BLK, PACK], BF16, name="last_bf", align_bytes=64)
+        last_bf = out_bf[1][:, block_cols(1), :]
         nc.scalar.activation(last_f32[0][:], low[:], RELU)
         nc.sync.dma_start(out=out_rows[:, 0:2, block_cols(LAST)], in_=last_f32[0][:])
-        nc.vector.tensor_scalar_max(o_bf[LAST][:, :, 2:], high[:].rearrange("p e j -> p j e"), 0.0)
-        quantise_out(2)
-        nc.scalar.activation(o_bf[LAST][:, :, :2], low[:].rearrange("p e j -> p j e"), RELU)
+        nc.vector.tensor_scalar_max(last_bf[:, :, 2:], high[:].rearrange("p e j -> p j e"), 0.0)
+        quantise_out(1, block_cols(0))
+        nc.scalar.activation(last_bf[:, :, :2], low[:].rearrange("p e j -> p j e"), RELU)
         nc.vector.tensor_scalar_max(last_f32[1][:], high[:], 0.0)
         nc.sync.dma_start(out=out_rows[:, 2:, block_cols(LAST)], in_=last_f32[1][:])
-        quantise_out(LAST)
+        quantise_out(1, block_cols(1))
 
         for q, queue in enumerate((nc.sync, nc.scalar, nc.sync, nc.scalar)):
             queue.dma_start(

@@ -64,8 +64,8 @@ def tile_picked_ngcf8_relu_po_kernel(
         w1_raw = keep.tile([P, PACK, H], F32, name="w1_raw", align_bytes=64)
         w_tags = ("w2_raw", "w3_raw", "h1_0")
         w_raw = [keep.tile([P, H], I32, name=f"w_raw{i}", tag=w_tags[i], align_bytes=64) for i in range(3)]
-        w_scales_room = late.tile([P, 3 * 4 * HALF], U8, name="w_scales_room", align_bytes=64, offset=0)
-        w_scales_raw = w_scales_room[:, :H]
+        w_scales_room = late.tile([P, H], U8, name="w_scales_room", align_bytes=64, offset=0)
+        w_scales_raw = w_scales_room[:]
 
         nc.gpsimd.memset(x_scale_table[:].bitcast(I32), 0)
         nc.gpsimd.memset(w_scales_raw.bitcast(I32), 0)
@@ -159,9 +159,9 @@ def tile_picked_ngcf8_relu_po_kernel(
         for t in range(PACK):
             nc.scalar.copy(out=y_plain[:, t, :], in_=y_window[t][:, half_cols(1)])
 
-        h_sum = {0: keep.tile([P, PACK, HALF], F32, name="h_sum0")}
+        h_sum = {}
         h1 = {}
-        z_early = [late.tile([P, HALF, PACK], BF16, name=f"z_early{w}", align_bytes=64, offset=4 * HALF * (3 + 2 * w)) for w in (Z, Z2)]
+        z_early = [late.tile([P, HALF, PACK], BF16, name=f"z_early{w}", align_bytes=64, offset=4 * HALF * (4 + 2 * w)) for w in (Z, Z2)]
         z_block = {b: keep.tile([P, 2, BLK, PACK], BF16, name=f"z_block{b}", align_bytes=64) for b in (2, 3)}
         by_lines = "p t (c i) -> p c t i"
 
@@ -185,9 +185,11 @@ def tile_picked_ngcf8_relu_po_kernel(
                 MULT if which == Z2 else ADD,
             )
 
-        slots = [dict(offset=4 * HALF * i) for i in range(3)]
-        gather_h1(0, 0, keep)
-        deal("scales", w_scales_raw, U8, keep)
+        for t in range(PACK):
+            gather_h1(t, 0, keep, tag=f"h1_of_{t}")
+        dealt["scales"] = keep.tile([P, H], U8, name="dealt_scales", align_bytes=64)
+        nc.gpsimd.tensor_copy(out=dealt["scales"][:].rearrange("p (t m) -> p t m", t=PACK), in_=w_scales_raw.rearrange("p (m t) -> p t m", t=PACK))
+        h_sum[0] = late.tile([P, PACK, HALF], F32, name="h_sum0", align_bytes=64, offset=0)
         c_bank = [psum.tile([P, PACK, BLK], F32, name=f"c_bank{b}", tag=f"bank{PACK + b}") for b in range(BLOCKS)]
         for b in range(BLOCKS):
             for t in range(PACK):
@@ -201,16 +203,13 @@ def tile_picked_ngcf8_relu_po_kernel(
                 )
         c_first = keep.tile([P, PACK, BLK], F32, name="c_first")
         nc.scalar.copy(out=c_first[:], in_=c_bank[0][:])
-        gather_h1(1, 0, late, **slots[0])
         gather_h2(0, 0)
-        gather_h1(2, 0, late, **slots[1])
         gather_h2(1, 0)
         low_bf = keep.tile([P, 2, P, 2], BF16, name="low_bf", tag="low_bf", align_bytes=64)
         nc.scalar.copy(out=low_bf[:], in_=turned_low[:].rearrange("j i e p -> j i p e"))
         back = [psum.tile([P, 2, BLK], F32, name=f"back{i}", tag=f"bank{i}") for i in range(2)]
         for i in range(2):
             nc.tensor.transpose(back[i][:, 0, :], low_bf[:, i].rearrange("j p e -> j (p e)").bitcast(F32), identity[:])
-        gather_h1(3, 0, late, **slots[2])
         gather_h2(2, 0)
         gather_h2(3, 0)
         for i in range(2):
@@ -263,8 +262,8 @@ def tile_picked_ngcf8_relu_po_kernel(
                 nc.sync.dma_start(out=out_words[:, half_cols(h)], in_=out_codes[h][:].bitcast(I32))
 
         flat = "p j t -> p (j t)"
-        gather_h1(0, 1, late, **slots[1])
-        gather_h1(1, 1, late, **slots[2])
+        gather_h1(0, 1, keep, tag="h1_of_2")
+        gather_h1(1, 1, keep, tag="h1_of_3")
         gather_h1(2, 1, reuse, offset=4 * H * W2)
         mix(nc.vector, 1, c_bank[1][:], Z2, LINE)
         gather_h1(3, 1, reuse, offset=4 * H * W2 + 4 * HALF)
@@ -273,7 +272,7 @@ def tile_picked_ngcf8_relu_po_kernel(
         empty_early(0)
         empty_early(1)
         nc.sync.dma_start(out=out_rows[:, :, half_cols(0)], in_=early_f32[:])
-        h_sum[1] = late.tile([P, PACK, HALF], F32, name="h_sum1", align_bytes=64, offset=4 * HALF * 3)
+        h_sum[1] = late.tile([P, PACK, HALF], F32, name="h_sum1", align_bytes=64, offset=4 * HALF * 4)
         for t in range(PACK):
             gather_h2(t, 1)
         mix(nc.vector, 2, c_bank[2][:], Z2, LINE)

@@ -28,6 +28,8 @@ BLOCKS = S // BLK
 LAST = BLOCKS - 1
 LINE = 2
 W1_SPLIT = 60
+POOL_COLS = 160
+POOL_LAST = 64
 W2, W3, W4 = 0, 1, 2
 Z, Z2 = 0, 1
 
@@ -155,9 +157,6 @@ def tile_picked_ngcf8_relu_po_kernel(
 
         for t in range(PACK):
             turn(y_window[t], t, 0)
-        y_plain = keep.tile([P, PACK, HALF], F32, name="y_plain")
-        for t in range(PACK):
-            nc.scalar.copy(out=y_plain[:, t, :], in_=y_window[t][:, half_cols(1)])
 
         h_sum = {}
         h1 = {}
@@ -177,10 +176,10 @@ def tile_picked_ngcf8_relu_po_kernel(
             if h == 0:
                 turn(h_sum[0][:, t, :], t, 1)
 
-        def mix(engine, b, other, which, line):
+        def mix(engine, out, h, cols, other, which, line):
             engine.tensor_tensor(
-                z_values(b, which).rearrange("p (c i) t -> p c t i", i=line),
-                h_sum[b // 2][:, :, block_cols(b % 2)].rearrange(by_lines, i=line),
+                out.rearrange("p (c i) t -> p c t i", i=line),
+                h_sum[h][:, :, cols].rearrange(by_lines, i=line),
                 other.rearrange(by_lines, i=line),
                 MULT if which == Z2 else ADD,
             )
@@ -201,8 +200,11 @@ def tile_picked_ngcf8_relu_po_kernel(
                     start=True,
                     stop=True,
                 )
-        c_first = keep.tile([P, PACK, BLK], F32, name="c_first")
-        nc.scalar.copy(out=c_first[:], in_=c_bank[0][:])
+        c_first = keep.tile([P, PACK, POOL_COLS], F32, name="c_first")
+        nc.scalar.copy(out=c_first[:, :, :BLK], in_=c_bank[0][:])
+        nc.scalar.copy(out=c_first[:, :, BLK:], in_=c_bank[1][:, :, : POOL_COLS - BLK])
+        c_last = keep.tile([P, PACK, POOL_LAST], F32, name="c_last")
+        nc.scalar.copy(out=c_last[:], in_=c_bank[LAST][:, :, :POOL_LAST])
         gather_h2(0, 0)
         gather_h2(1, 0)
         low_bf = keep.tile([P, 2, P, 2], BF16, name="low_bf", tag="low_bf", align_bytes=64)
@@ -219,7 +221,7 @@ def tile_picked_ngcf8_relu_po_kernel(
         for i in range(2):
             z_words = z_values(i, Z).rearrange("p j t -> p (j t)").bitcast(F32).rearrange("p (j u) -> p j u", u=2)
             nc.scalar.copy(out=z_words, in_=back[i][:].rearrange("p u j -> p j u"))
-        mix(nc.gpsimd, 0, c_first[:], Z2, 4)
+        mix(nc.gpsimd, z_early[Z2][:, :POOL_COLS, :], 0, slice(0, POOL_COLS), c_first[:], Z2, 4)
 
         out_scales = keep.tile([P, S], U8, name="out_scales", align_bytes=64)
         out_rows = out_0.rearrange("(p t) j -> p t j", t=PACK)
@@ -265,26 +267,39 @@ def tile_picked_ngcf8_relu_po_kernel(
         gather_h1(0, 1, keep, tag="h1_of_2")
         gather_h1(1, 1, keep, tag="h1_of_3")
         gather_h1(2, 1, reuse, offset=4 * H * W2)
-        mix(nc.vector, 1, c_bank[1][:], Z2, LINE)
+        mix(nc.vector, z_early[Z2][:, POOL_COLS:, :], 0, slice(POOL_COLS, HALF), c_bank[1][:, :, POOL_COLS - BLK :], Z2, LINE)
         gather_h1(3, 1, reuse, offset=4 * H * W2 + 4 * HALF)
         quantise(z_early[Z2][:].rearrange(flat), [(0, Z2), (1, Z2)], tag="high_bf1")
         quantise(z_early[Z][:].rearrange(flat), [(0, Z), (1, Z)])
         empty_early(0)
         empty_early(1)
         nc.sync.dma_start(out=out_rows[:, :, half_cols(0)], in_=early_f32[:])
+        y_again = {b: psum.tile([P, PACK, BLK], F32, name=f"y_again{b}", tag=f"bank{PACK + b - 2}") for b in (2, 3)}
+        for b in (2, 3):
+            for t in range(PACK):
+                nc.tensor.matmul_mx(
+                    out=y_again[b][:, t, :],
+                    lhsT=w1_codes[:, block_cols(t)].bitcast(FP8X4),
+                    lhsT_scale=w1_scales[:, block_cols(t)],
+                    rhs=x_picked[:, block_cols(b)].bitcast(FP8X4),
+                    rhs_scale=x_scale_picked[:, block_cols(b)],
+                    start=True,
+                    stop=True,
+                )
         h_sum[1] = late.tile([P, PACK, HALF], F32, name="h_sum1", align_bytes=64, offset=4 * HALF * 4)
         for t in range(PACK):
             gather_h2(t, 1)
-        mix(nc.vector, 2, c_bank[2][:], Z2, LINE)
-        mix(nc.vector, 2, y_plain[:, :, block_cols(0)], Z, LINE)
+        mix(nc.gpsimd, z_values(3, Z2)[:, :POOL_LAST, :], 1, slice(BLK, BLK + POOL_LAST), c_last[:], Z2, 4)
+        mix(nc.vector, z_values(2, Z2), 1, block_cols(0), c_bank[2][:], Z2, LINE)
+        mix(nc.vector, z_values(2, Z), 1, block_cols(0), y_again[2][:], Z, LINE)
         quantise(z_values(2, Z2).rearrange(flat), [(2, Z2)])
-        mix(nc.vector, 3, c_bank[3][:], Z2, LINE)
+        mix(nc.vector, z_values(3, Z2)[:, POOL_LAST:, :], 1, slice(BLK + POOL_LAST, HALF), c_bank[3][:, :, POOL_LAST:], Z2, LINE)
         quantise(z_values(2, Z).rearrange(flat), [(2, Z)])
         third_f32 = keep.tile([P, PACK, BLK], F32, name="third_f32")
         nc.scalar.activation(third_f32[:], o_bank[2][0][:], RELU)
         nc.sync.dma_start(out=out_rows[:, :, block_cols(2)], in_=third_f32[:])
         quantise(z_values(3, Z2).rearrange(flat), [(3, Z2)])
-        mix(nc.vector, 3, y_plain[:, :, block_cols(1)], Z, LINE)
+        mix(nc.vector, z_values(3, Z), 1, block_cols(1), y_again[3][:], Z, LINE)
         quantise_out(0, half_cols(0))
         quantise(z_values(3, Z).rearrange(flat), [(3, Z)])
         nc.vector.tensor_copy(out=out_bf[1][:, block_cols(0), :].rearrange("p (c i) t -> p c t i", i=4), in_=third_f32[:].rearrange(by_lines, i=4))

@@ -69,8 +69,8 @@ def tile_picked_ngcf8_relu_po_kernel(
         w_scales_room = late.tile([P, H], U8, name="w_scales_room", align_bytes=64, offset=0)
         w_scales_raw = w_scales_room[:]
 
-        nc.gpsimd.memset(x_scale_table[:].bitcast(I32), 0)
-        nc.gpsimd.memset(w_scales_raw.bitcast(I32), 0)
+        nc.vector.memset(x_scale_table[:].bitcast(I32), 0)
+        nc.vector.memset(w_scales_raw.bitcast(I32), 0)
         y_window = [keep.tile([P, S], F32, name=f"y_window{t}") for t in range(PACK)]
         identity = keep.tile([P, P], F32, name="identity")
         make_identity(nc, identity[:])
@@ -84,7 +84,7 @@ def tile_picked_ngcf8_relu_po_kernel(
         for i, words in enumerate((w2_words, w3_words, w4_words)):
             nc.sync.dma_start(out=w_raw[i][:], in_=words_of(words))
         for i, scales in enumerate((w2_scales, w3_scales, w4_scales)):
-            load_scale_rows(nc.gpsimd if i == W4 else nc.sync, w_scales_raw, SCALE_ROWS * i, scales)
+            load_scale_rows(nc.sync, w_scales_raw, SCALE_ROWS * i, scales)
 
         def half_cols(h):
             return slice(h * HALF, (h + 1) * HALF)

@@ -28,7 +28,7 @@ BLOCKS = S // BLK
 LAST = BLOCKS - 1
 LINE = 2
 W1_SPLIT = 60
-POOL_COLS = 160
+POOL_COLS = 192
 POOL_LAST = 64
 W2, W3, W4 = 0, 1, 2
 Z, Z2 = 0, 1
@@ -73,11 +73,14 @@ def tile_picked_ngcf8_relu_po_kernel(
         nc.vector.memset(w_scales_raw.bitcast(I32), 0)
         y_window = [keep.tile([P, S], F32, name=f"y_window{t}") for t in range(PACK)]
         identity = keep.tile([P, P], F32, name="identity")
-        make_identity(nc, identity[:])
+        nc.vector.memset(identity[:], 0.0)
 
         nc.sync.dma_start(offs_sb[:], offs)
         nc.sync.dma_start(out=w1_raw[:], in_=w1.rearrange("(p j) c -> p j c", j=PACK))
         load_scale_rows(nc.scalar, x_scale_table, 0, x_scales)
+        warm = keep.tile([P, 1], F32, name="warm")
+        nc.scalar.activation(warm[:], identity[:, 0:1], RELU)
+        make_identity(nc, identity[:], nomemset=True)
         nc.sync.dma_start(p1_sb[:], p1)
         nc.sync.dma_start(p2_sb[:], p2)
         nc.sync.dma_start(out=x_table[:].bitcast(I32), in_=words_of(x_words))
@@ -184,6 +187,9 @@ def tile_picked_ngcf8_relu_po_kernel(
                 MULT if which == Z2 else ADD,
             )
 
+        def pool_product(out, h, cols, c_words):
+            nc.gpsimd.tensor_tensor(out, h_sum[h][:, :, cols].rearrange("p t j -> p j t"), c_words, MULT)
+
         for t in range(PACK):
             gather_h1(t, 0, keep, tag=f"h1_of_{t}")
         dealt["scales"] = keep.tile([P, H], U8, name="dealt_scales", align_bytes=64)
@@ -200,11 +206,11 @@ def tile_picked_ngcf8_relu_po_kernel(
                     start=True,
                     stop=True,
                 )
-        c_first = keep.tile([P, PACK, POOL_COLS], F32, name="c_first")
-        nc.scalar.copy(out=c_first[:, :, :BLK], in_=c_bank[0][:])
-        nc.scalar.copy(out=c_first[:, :, BLK:], in_=c_bank[1][:, :, : POOL_COLS - BLK])
-        c_last = keep.tile([P, PACK, POOL_LAST], F32, name="c_last")
-        nc.scalar.copy(out=c_last[:], in_=c_bank[LAST][:, :, :POOL_LAST])
+        c_first = keep.tile([P, POOL_COLS, PACK], F32, name="c_first")
+        nc.scalar.copy(out=c_first[:, :BLK, :], in_=c_bank[0][:].rearrange("p t j -> p j t"))
+        nc.scalar.copy(out=c_first[:, BLK:, :], in_=c_bank[1][:, :, : POOL_COLS - BLK].rearrange("p t j -> p j t"))
+        c_last = keep.tile([P, POOL_LAST, PACK], F32, name="c_last")
+        nc.scalar.copy(out=c_last[:], in_=c_bank[LAST][:, :, :POOL_LAST].rearrange("p t j -> p j t"))
         gather_h2(0, 0)
         gather_h2(1, 0)
         low_bf = keep.tile([P, 2, P, 2], BF16, name="low_bf", tag="low_bf", align_bytes=64)
@@ -221,7 +227,7 @@ def tile_picked_ngcf8_relu_po_kernel(
         for i in range(2):
             z_words = z_values(i, Z).rearrange("p j t -> p (j t)").bitcast(F32).rearrange("p (j u) -> p j u", u=2)
             nc.scalar.copy(out=z_words, in_=back[i][:].rearrange("p u j -> p j u"))
-        mix(nc.gpsimd, z_early[Z2][:, :POOL_COLS, :], 0, slice(0, POOL_COLS), c_first[:], Z2, 4)
+        pool_product(z_early[Z2][:, :POOL_COLS, :], 0, slice(0, POOL_COLS), c_first[:])
 
         out_scales = keep.tile([P, S], U8, name="out_scales", align_bytes=64)
         out_rows = out_0.rearrange("(p t) j -> p t j", t=PACK)
@@ -289,7 +295,7 @@ def tile_picked_ngcf8_relu_po_kernel(
         h_sum[1] = late.tile([P, PACK, HALF], F32, name="h_sum1", align_bytes=64, offset=4 * HALF * 4)
         for t in range(PACK):
             gather_h2(t, 1)
-        mix(nc.gpsimd, z_values(3, Z2)[:, :POOL_LAST, :], 1, slice(BLK, BLK + POOL_LAST), c_last[:], Z2, 4)
+        pool_product(z_values(3, Z2)[:, :POOL_LAST, :], 1, slice(BLK, BLK + POOL_LAST), c_last[:])
         mix(nc.vector, z_values(2, Z2), 1, block_cols(0), c_bank[2][:], Z2, LINE)
         mix(nc.vector, z_values(2, Z), 1, block_cols(0), y_again[2][:], Z, LINE)
         quantise(z_values(2, Z2).rearrange(flat), [(2, Z2)])

@@ -64,13 +64,15 @@ def tile_picked_ngcf8_relu_po_kernel(
         x_table = reuse.tile([P, T], U32, name="x_table", align_bytes=64, offset=0)
         x_scale_table = keep.tile([P, T], U8, name="x_scale_table", align_bytes=64)
         w1_raw = keep.tile([P, PACK, H], F32, name="w1_raw", align_bytes=64)
-        w_tags = ("w2_raw", "w3_raw", "h1_0")
+        w_tags = ("w2_raw", "w3_raw", "w4_raw")
         w_raw = [keep.tile([P, H], I32, name=f"w_raw{i}", tag=w_tags[i], align_bytes=64) for i in range(3)]
         w_scales_room = late.tile([P, H], U8, name="w_scales_room", align_bytes=64, offset=0)
         w_scales_raw = w_scales_room[:]
+        w34_scales_raw = keep.tile([P, H], U8, name="w34_scales_raw", align_bytes=64)
 
         nc.vector.memset(x_scale_table[:].bitcast(I32), 0)
         nc.vector.memset(w_scales_raw.bitcast(I32), 0)
+        nc.vector.memset(w34_scales_raw[:].bitcast(I32), 0)
         y_window = [keep.tile([P, S], F32, name=f"y_window{t}") for t in range(PACK)]
         identity = keep.tile([P, P], F32, name="identity")
         nc.vector.memset(identity[:], 0.0)
@@ -86,8 +88,9 @@ def tile_picked_ngcf8_relu_po_kernel(
         nc.sync.dma_start(out=x_table[:].bitcast(I32), in_=words_of(x_words))
         for i, words in enumerate((w2_words, w3_words, w4_words)):
             nc.sync.dma_start(out=w_raw[i][:], in_=words_of(words))
-        for i, scales in enumerate((w2_scales, w3_scales, w4_scales)):
-            load_scale_rows(nc.sync, w_scales_raw, SCALE_ROWS * i, scales)
+        load_scale_rows(nc.sync, w_scales_raw, 0, w2_scales)
+        for i, scales in enumerate((w3_scales, w4_scales)):
+            load_scale_rows(nc.sync, w34_scales_raw, SCALE_ROWS * i, scales)
 
         def half_cols(h):
             return slice(h * HALF, (h + 1) * HALF)
@@ -141,9 +144,9 @@ def tile_picked_ngcf8_relu_po_kernel(
 
         def weight(i, t):
             cols = slice(t * P, (t + 1) * P)
-            return dict(lhsT=dealt[i][:, cols].bitcast(FP8X4), lhsT_scale=dealt["scales"][SCALE_ROWS * i :, cols])
+            return dict(lhsT=dealt[i][:, cols].bitcast(FP8X4), lhsT_scale=dealt_scales[i][:, cols])
 
-        for i in (W2, W3, W4):
+        for i in (W2, W3):
             deal(i, w_raw[i][:], I32, reuse, offset=4 * H * i)
 
         turned_low = psum.tile([P, 2, 2, P], F32, name="turned_low", tag="bank0")
@@ -192,8 +195,12 @@ def tile_picked_ngcf8_relu_po_kernel(
 
         for t in range(PACK):
             gather_h1(t, 0, keep, tag=f"h1_of_{t}")
-        dealt["scales"] = keep.tile([P, H], U8, name="dealt_scales", align_bytes=64)
-        nc.gpsimd.tensor_copy(out=dealt["scales"][:].rearrange("p (t m) -> p t m", t=PACK), in_=w_scales_raw.rearrange("p (m t) -> p t m", t=PACK))
+        w2_scales_dealt = keep.tile([P, H], U8, name="w2_scales_dealt", tag="w3_raw", align_bytes=64)
+        w34_scales_dealt = keep.tile([P, H], U8, name="w34_scales_dealt", align_bytes=64)
+        dealt[W4] = reuse.tile([P, H], I32, name="dealt_w4", align_bytes=64, offset=4 * H * W4)
+        for out, raw in ((w2_scales_dealt, w_scales_raw), (dealt[W4], w_raw[W4][:]), (w34_scales_dealt, w34_scales_raw[:])):
+            nc.gpsimd.tensor_copy(out=out[:].rearrange("p (t m) -> p t m", t=PACK), in_=raw.rearrange("p (m t) -> p t m", t=PACK))
+        dealt_scales = {W2: w2_scales_dealt[:], W3: w34_scales_dealt[:], W4: w34_scales_dealt[SCALE_ROWS:, :]}
         h_sum[0] = late.tile([P, PACK, HALF], F32, name="h_sum0", align_bytes=64, offset=0)
         c_bank = [psum.tile([P, PACK, BLK], F32, name=f"c_bank{b}", tag=f"bank{PACK + b}") for b in range(BLOCKS)]
         for b in range(BLOCKS):
@@ -261,7 +268,6 @@ def tile_picked_ngcf8_relu_po_kernel(
 
         def empty_early(b):
             nc.scalar.activation(early_f32[:, :, block_cols(b)], o_bank[b][0][:], RELU)
-            nc.scalar.activation(out_bf[0][:, block_cols(b), :], o_bank[b][0][:].rearrange("p t j -> p j t"), RELU)
 
         def quantise_out(h, inner):
             cols = slice(h * HALF + inner.start, h * HALF + inner.stop)
@@ -280,6 +286,7 @@ def tile_picked_ngcf8_relu_po_kernel(
         empty_early(0)
         empty_early(1)
         nc.sync.dma_start(out=out_rows[:, :, half_cols(0)], in_=early_f32[:])
+        nc.scalar.copy(out=out_bf[0][:].rearrange("p (c i) t -> p c t i", i=LINE), in_=early_f32[:].rearrange(by_lines, i=LINE))
         y_again = {b: psum.tile([P, PACK, BLK], F32, name=f"y_again{b}", tag=f"bank{PACK + b - 2}") for b in (2, 3)}
         for b in (2, 3):
             for t in range(PACK):

@@ -29,7 +29,7 @@ LAST = BLOCKS - 1
 LINE = 2
 W1_SPLIT = 60
 POOL_COLS = 192
-POOL_LAST = 64
+POOL_LAST = 96
 W2, W3, W4 = 0, 1, 2
 Z, Z2 = 0, 1
 
@@ -264,16 +264,17 @@ def tile_picked_ngcf8_relu_po_kernel(
 
         early_f32 = keep.tile([P, PACK, HALF], F32, name="early_f32")
         out_bf = [keep.tile([P, HALF, PACK], BF16, name=f"out_bf{h}", align_bytes=64) for h in range(2)]
-        out_codes = [keep.tile([P, HALF], U32, name=f"out_codes{h}", align_bytes=64) for h in range(2)]
+        out_codes = keep.tile([P, S], U32, name="out_codes", align_bytes=64)
 
         def empty_early(b):
             nc.scalar.activation(early_f32[:, :, block_cols(b)], o_bank[b][0][:], RELU)
 
         def quantise_out(h, inner):
             cols = slice(h * HALF + inner.start, h * HALF + inner.stop)
-            nc.vector.quantize_mx(out=out_codes[h][:, inner].bitcast(FP8X4), scales=out_scales[:, cols], in_=out_bf[h][:, inner, :].rearrange("p j t -> p (j t)"))
-            if inner.stop == HALF:
-                nc.sync.dma_start(out=out_words[:, half_cols(h)], in_=out_codes[h][:].bitcast(I32))
+            nc.vector.quantize_mx(out=out_codes[:, cols].bitcast(FP8X4), scales=out_scales[:, cols], in_=out_bf[h][:, inner, :].rearrange("p j t -> p (j t)"))
+            if h == 1:
+                stored = slice(0 if inner.start == 0 else cols.start, cols.stop)
+                nc.sync.dma_start(out=out_words[:, stored], in_=out_codes[:, stored].bitcast(I32))
 
         flat = "p j t -> p (j t)"
         gather_h1(0, 1, keep, tag="h1_of_2")
@@ -287,7 +288,7 @@ def tile_picked_ngcf8_relu_po_kernel(
         empty_early(1)
         nc.sync.dma_start(out=out_rows[:, :, half_cols(0)], in_=early_f32[:])
         nc.scalar.copy(out=out_bf[0][:].rearrange("p (c i) t -> p c t i", i=LINE), in_=early_f32[:].rearrange(by_lines, i=LINE))
-        y_again = {b: psum.tile([P, PACK, BLK], F32, name=f"y_again{b}", tag=f"bank{PACK + b - 2}") for b in (2, 3)}
+        y_again = {b: psum.tile([P, PACK, BLK], F32, name=f"y_again{b}", tag=f"bank{PACK * (b - 2)}") for b in (2, 3)}
         for b in (2, 3):
             for t in range(PACK):
                 nc.tensor.matmul_mx(
@@ -311,21 +312,20 @@ def tile_picked_ngcf8_relu_po_kernel(
         third_f32 = keep.tile([P, PACK, BLK], F32, name="third_f32")
         nc.scalar.activation(third_f32[:], o_bank[2][0][:], RELU)
         nc.sync.dma_start(out=out_rows[:, :, block_cols(2)], in_=third_f32[:])
+        nc.scalar.activation(out_bf[1][:, block_cols(0), :], o_bank[2][0][:].rearrange("p t j -> p j t"), RELU)
         quantise(z_values(3, Z2).rearrange(flat), [(3, Z2)])
         mix(nc.vector, z_values(3, Z), 1, block_cols(1), y_again[3][:], Z, LINE)
-        quantise_out(0, half_cols(0))
         quantise(z_values(3, Z).rearrange(flat), [(3, Z)])
-        nc.vector.tensor_copy(out=out_bf[1][:, block_cols(0), :].rearrange("p (c i) t -> p c t i", i=4), in_=third_f32[:].rearrange(by_lines, i=4))
+        quantise_out(0, half_cols(0))
         low, high = o_bank[LAST]
-        last_f32 = [keep.tile([P, 2, BLK], F32, name=f"last_f32{u}") for u in range(2)]
+        last_f32 = keep.tile([P, PACK, BLK], F32, name="last_f32")
         last_bf = out_bf[1][:, block_cols(1), :]
-        nc.scalar.activation(last_f32[0][:], low[:], RELU)
-        nc.sync.dma_start(out=out_rows[:, 0:2, block_cols(LAST)], in_=last_f32[0][:])
-        nc.vector.tensor_scalar_max(last_bf[:, :, 2:], high[:].rearrange("p e j -> p j e"), 0.0)
         quantise_out(1, block_cols(0))
+        nc.scalar.activation(last_f32[:, :2, :], low[:], RELU)
+        nc.vector.tensor_scalar_max(last_f32[:, 2:, :], high[:], 0.0)
+        nc.sync.dma_start(out=out_rows[:, :, block_cols(LAST)], in_=last_f32[:])
         nc.scalar.activation(last_bf[:, :, :2], low[:].rearrange("p e j -> p j e"), RELU)
-        nc.vector.tensor_scalar_max(last_f32[1][:], high[:], 0.0)
-        nc.sync.dma_start(out=out_rows[:, 2:, block_cols(LAST)], in_=last_f32[1][:])
+        nc.vector.tensor_scalar_max(last_bf[:, :, 2:], high[:].rearrange("p e j -> p j e"), 0.0)
         quantise_out(1, block_cols(1))
 
         for q, queue in enumerate((nc.sync, nc.scalar, nc.sync, nc.scalar)):

@@ -28,8 +28,8 @@ BLOCKS = S // BLK
 LAST = BLOCKS - 1
 LINE = 2
 W1_SPLIT = 60
-POOL_COLS = 192
-POOL_LAST = 96
+POOL_COLS = 160
+POOL_LAST = 64
 W2, W3, W4 = 0, 1, 2
 Z, Z2 = 0, 1
 

@@ -28,8 +28,8 @@ BLOCKS = S // BLK
 LAST = BLOCKS - 1
 LINE = 2
 W1_SPLIT = 60
-POOL_COLS = 160
-POOL_LAST = 64
+POOL_COLS = 128
+POOL_LAST = 48
 W2, W3, W4 = 0, 1, 2
 Z, Z2 = 0, 1
 
@@ -146,7 +146,7 @@ def tile_picked_ngcf8_relu_po_kernel(
             cols = slice(t * P, (t + 1) * P)
             return dict(lhsT=dealt[i][:, cols].bitcast(FP8X4), lhsT_scale=dealt_scales[i][:, cols])
 
-        for i in (W2, W3):
+        for i in (W2, W3, W4):
             deal(i, w_raw[i][:], I32, reuse, offset=4 * H * i)
 
         turned_low = psum.tile([P, 2, 2, P], F32, name="turned_low", tag="bank0")
@@ -197,8 +197,7 @@ def tile_picked_ngcf8_relu_po_kernel(
             gather_h1(t, 0, keep, tag=f"h1_of_{t}")
         w2_scales_dealt = keep.tile([P, H], U8, name="w2_scales_dealt", tag="w3_raw", align_bytes=64)
         w34_scales_dealt = keep.tile([P, H], U8, name="w34_scales_dealt", align_bytes=64)
-        dealt[W4] = reuse.tile([P, H], I32, name="dealt_w4", align_bytes=64, offset=4 * H * W4)
-        for out, raw in ((w2_scales_dealt, w_scales_raw), (dealt[W4], w_raw[W4][:]), (w34_scales_dealt, w34_scales_raw[:])):
+        for out, raw in ((w2_scales_dealt, w_scales_raw), (w34_scales_dealt, w34_scales_raw[:])):
             nc.gpsimd.tensor_copy(out=out[:].rearrange("p (t m) -> p t m", t=PACK), in_=raw.rearrange("p (m t) -> p t m", t=PACK))
         dealt_scales = {W2: w2_scales_dealt[:], W3: w34_scales_dealt[:], W4: w34_scales_dealt[SCALE_ROWS:, :]}
         h_sum[0] = late.tile([P, PACK, HALF], F32, name="h_sum0", align_bytes=64, offset=0)
@@ -215,7 +214,6 @@ def tile_picked_ngcf8_relu_po_kernel(
                 )
         c_first = keep.tile([P, POOL_COLS, PACK], F32, name="c_first")
         nc.scalar.copy(out=c_first[:, :BLK, :], in_=c_bank[0][:].rearrange("p t j -> p j t"))
-        nc.scalar.copy(out=c_first[:, BLK:, :], in_=c_bank[1][:, :, : POOL_COLS - BLK].rearrange("p t j -> p j t"))
         c_last = keep.tile([P, POOL_LAST, PACK], F32, name="c_last")
         nc.scalar.copy(out=c_last[:], in_=c_bank[LAST][:, :, :POOL_LAST].rearrange("p t j -> p j t"))
         gather_h2(0, 0)

@@ -1,7 +1,6 @@
 from contextlib import ExitStack
 
 import concourse.mybir as mybir
-from concourse.masks import make_identity
 
 K, T, S, N, H = 512, 2048, 512, 512, 512
 FLOPS = 2 * S * (2 * K * H + 2 * H * N)
@@ -16,6 +15,7 @@ FP8X4 = mybir.dt.float8_e4m3fn_x4
 ADD = mybir.AluOpType.add
 MULT = mybir.AluOpType.mult
 RELU = mybir.ActivationFunctionType.Relu
+COPY = mybir.ActivationFunctionType.Copy
 
 P = 128
 PACK = 4
@@ -28,8 +28,6 @@ BLOCKS = S // BLK
 LAST = BLOCKS - 1
 LINE = 2
 W1_SPLIT = 60
-POOL_COLS = 128
-POOL_LAST = 48
 W2, W3, W4 = 0, 1, 2
 Z, Z2 = 0, 1
 
@@ -40,9 +38,6 @@ def tile_picked_ngcf8_relu_po_kernel(
     nc = tc.nc
     with ExitStack() as ctx:
         keep = ctx.enter_context(tc.tile_pool(name="keep", bufs=1))
-        ring = ctx.enter_context(tc.tile_pool(name="ring", bufs=BLOCKS))
-        reuse = ctx.enter_context(tc.tile_pool(name="reuse", bufs=1))
-        late = ctx.enter_context(tc.tile_pool(name="late", bufs=1))
         psum = ctx.enter_context(tc.psum_pool(name="psum", bufs=1))
 
         def words_of(dram):
@@ -58,54 +53,51 @@ def tile_picked_ngcf8_relu_po_kernel(
         def block_cols(b):
             return slice(b * BLK, (b + 1) * BLK)
 
-        offs_sb = keep.tile([P, S // LIST_ROWS], U16, name="offs_sb")
-        p1_sb = keep.tile([P, S // LIST_ROWS], U16, name="p1_sb")
-        p2_sb = keep.tile([P, S // LIST_ROWS], U16, name="p2_sb")
-        x_table = reuse.tile([P, T], U32, name="x_table", align_bytes=64, offset=0)
-        x_scale_table = keep.tile([P, T], U8, name="x_scale_table", align_bytes=64)
-        w1_raw = keep.tile([P, PACK, H], F32, name="w1_raw", align_bytes=64)
-        w_tags = ("w2_raw", "w3_raw", "w4_raw")
-        w_raw = [keep.tile([P, H], I32, name=f"w_raw{i}", tag=w_tags[i], align_bytes=64) for i in range(3)]
-        w_scales_room = late.tile([P, H], U8, name="w_scales_room", align_bytes=64, offset=0)
-        w_scales_raw = w_scales_room[:]
-        w34_scales_raw = keep.tile([P, H], U8, name="w34_scales_raw", align_bytes=64)
-
-        nc.vector.memset(x_scale_table[:].bitcast(I32), 0)
-        nc.vector.memset(w_scales_raw.bitcast(I32), 0)
-        nc.vector.memset(w34_scales_raw[:].bitcast(I32), 0)
-        y_window = [keep.tile([P, S], F32, name=f"y_window{t}") for t in range(PACK)]
-        identity = keep.tile([P, P], F32, name="identity")
-        nc.vector.memset(identity[:], 0.0)
-
-        nc.sync.dma_start(offs_sb[:], offs)
-        nc.sync.dma_start(out=w1_raw[:], in_=w1.rearrange("(p j) c -> p j c", j=PACK))
-        load_scale_rows(nc.scalar, x_scale_table, 0, x_scales)
-        warm = keep.tile([P, 1], F32, name="warm")
-        nc.scalar.activation(warm[:], identity[:, 0:1], RELU)
-        make_identity(nc, identity[:], nomemset=True)
-        nc.sync.dma_start(p1_sb[:], p1)
-        nc.sync.dma_start(p2_sb[:], p2)
-        nc.sync.dma_start(out=x_table[:].bitcast(I32), in_=words_of(x_words))
-        for i, words in enumerate((w2_words, w3_words, w4_words)):
-            nc.sync.dma_start(out=w_raw[i][:], in_=words_of(words))
-        load_scale_rows(nc.sync, w_scales_raw, 0, w2_scales)
-        for i, scales in enumerate((w3_scales, w4_scales)):
-            load_scale_rows(nc.sync, w34_scales_raw, SCALE_ROWS * i, scales)
-
         def half_cols(h):
             return slice(h * HALF, (h + 1) * HALF)
 
         def entries(tile, h):
             return tile[:, h * HALF // LIST_ROWS : (h + 1) * HALF // LIST_ROWS]
 
+        offs_sb = keep.tile([P, S // LIST_ROWS], U16, name="offs_sb")
+        p1_sb = keep.tile([P, S // LIST_ROWS], U16, name="p1_sb")
+        p2_sb = keep.tile([P, S // LIST_ROWS], U16, name="p2_sb")
+        x_table = keep.tile([P, T], U32, name="x_table", align_bytes=64)
+        x_scale_table = keep.tile([P, T], U8, name="x_scale_table", align_bytes=64)
+        w1_raw = keep.tile([P, PACK, H], F32, name="w1_raw", tag="w1_raw", align_bytes=64)
+        w_raw = [keep.tile([P, H], I32, name=f"w_raw{i}", align_bytes=64) for i in range(3)]
+        w2_scales_raw = keep.tile([P, H], U8, name="w2_scales_raw", align_bytes=64)
+        w34_scales_raw = keep.tile([P, H], U8, name="w34_scales_raw", align_bytes=64)
+
+        nc.vector.memset(x_scale_table[:].bitcast(I32), 0)
+        nc.vector.memset(w2_scales_raw[:].bitcast(I32), 0)
+        nc.vector.memset(w34_scales_raw[:].bitcast(I32), 0)
+
+        nc.sync.dma_start(offs_sb[:], offs)
+        nc.sync.dma_start(out=w1_raw[:], in_=w1.rearrange("(p j) c -> p j c", j=PACK))
+        load_scale_rows(nc.scalar, x_scale_table, 0, x_scales)
+        nc.sync.dma_start(p1_sb[:], p1)
+        nc.sync.dma_start(p2_sb[:], p2)
+        nc.sync.dma_start(out=x_table[:].bitcast(I32), in_=words_of(x_words))
+        nc.sync.dma_start(out=w_raw[W2][:], in_=words_of(w2_words))
+        load_scale_rows(nc.sync, w2_scales_raw, 0, w2_scales)
+        nc.sync.dma_start(out=w_raw[W3][:], in_=words_of(w3_words))
+        nc.sync.dma_start(out=w_raw[W4][:], in_=words_of(w4_words))
+        for i, scales in enumerate((w3_scales, w4_scales)):
+            load_scale_rows(nc.sync, w34_scales_raw, SCALE_ROWS * i, scales)
+
         x_scale_picked = keep.tile([P, S], U8, name="x_scale_picked", align_bytes=64)
         nc.vector.tensor_copy(out=x_scale_picked[:], in_=x_scale_table[:].indirect(offs_sb[:]))
         w1_bf = keep.tile([P, PACK, P, PACK], BF16, name="w1_bf", align_bytes=64)
-        for copy, lo, hi in ((nc.vector.tensor_copy, 0, W1_SPLIT), (nc.scalar.copy, W1_SPLIT, P)):
-            copy(
-                out=w1_bf[:, :, lo:hi, :].rearrange("p t m j -> p m j t"),
-                in_=w1_raw[:, :, PACK * lo : PACK * hi].rearrange("p j (m t) -> p m j t", t=PACK),
+
+        def w1_part(lo, hi):
+            return (
+                w1_bf[:, :, lo:hi, :].rearrange("p t m j -> p m j t"),
+                w1_raw[:, :, PACK * lo : PACK * hi].rearrange("p j (m t) -> p m j t", t=PACK),
             )
+
+        nc.vector.tensor_copy(*w1_part(0, W1_SPLIT))
+        nc.scalar.activation(*w1_part(W1_SPLIT, P), COPY)
         w1_codes = keep.tile([P, H], U32, name="w1_codes", align_bytes=64)
         w1_scales = keep.tile([P, H], U8, name="w1_scales", align_bytes=64)
 
@@ -119,137 +111,111 @@ def tile_picked_ngcf8_relu_po_kernel(
             nc.vector.tensor_copy(out=x_picked[:, half_cols(h)], in_=x_table[:].indirect(entries(offs_sb, h)))
         quantise_w1(slice(2, PACK))
 
-        y_bank = [psum.tile([P, S], F32, name=f"y_bank{t}", tag=f"bank{t}") for t in range(PACK)]
-        y_first = psum.tile([P, HALF], F32, name="y_first", tag=f"bank{PACK}")
-        for t in range(PACK):
-            for h in range(2) if t == 0 else (None,):
-                cols = slice(0, S) if h is None else half_cols(h)
-                bank = y_first[:] if h == 0 else y_bank[t][:, cols]
-                nc.tensor.matmul_mx(
-                    out=bank,
-                    lhsT=w1_codes[:, block_cols(t)].bitcast(FP8X4),
-                    lhsT_scale=w1_scales[:, block_cols(t)],
-                    rhs=x_picked[:, cols].bitcast(FP8X4),
-                    rhs_scale=x_scale_picked[:, cols],
-                    start=True,
-                    stop=True,
-                )
-                nc.scalar.copy(out=y_window[t][:, cols], in_=bank)
+        def bank(k, shape, name):
+            return psum.tile([P] + shape, F32, name=name, tag=f"bank{k}")
+
+        def times_x(out, weights, cols):
+            nc.tensor.matmul_mx(out=out, **weights, rhs=x_picked[:, cols].bitcast(FP8X4), rhs_scale=x_scale_picked[:, cols], start=True, stop=True)
+
+        def w1_plane(t):
+            return dict(lhsT=w1_codes[:, block_cols(t)].bitcast(FP8X4), lhsT_scale=w1_scales[:, block_cols(t)])
 
         dealt = {}
 
-        def deal(key, raw, dtype, pool, **place):
-            dealt[key] = pool.tile([P, H], dtype, name=f"dealt_{key}", align_bytes=64, **place)
-            nc.vector.tensor_copy(out=dealt[key][:].rearrange("p (t m) -> p m t", t=PACK), in_=raw.rearrange("p (m t) -> p m t", t=PACK))
+        def deal(engine, key, raw, dtype, **place):
+            dealt[key] = keep.tile([P, H], dtype, name=f"dealt_{key}", align_bytes=64, **place)
+            order = "p m t" if engine is nc.vector else "p t m"
+            engine.tensor_copy(out=dealt[key][:].rearrange(f"p (t m) -> {order}", t=PACK), in_=raw.rearrange(f"p (m t) -> {order}", t=PACK))
 
         def weight(i, t):
-            cols = slice(t * P, (t + 1) * P)
-            return dict(lhsT=dealt[i][:, cols].bitcast(FP8X4), lhsT_scale=dealt_scales[i][:, cols])
+            cols = block_cols(t)
+            scales = dealt["s2"][:] if i == W2 else dealt["s34"][SCALE_ROWS * (i - W3) :, :]
+            return dict(lhsT=dealt[i][:, cols].bitcast(FP8X4), lhsT_scale=scales[:, cols])
 
-        for i in (W2, W3, W4):
-            deal(i, w_raw[i][:], I32, reuse, offset=4 * H * i)
+        y_window = [keep.tile([P, S], F32, name=f"y_window{t}") for t in range(PACK)]
+        y_part = {}
+        for k, (t, h) in enumerate(((0, 0), (1, 0), (0, 1), (1, 1))):
+            y_part[t, h] = bank(k, [HALF], f"y_part{t}{h}")
+            times_x(y_part[t, h][:], w1_plane(t), half_cols(h))
+        y_whole = {}
+        for t in (2, 3):
+            y_whole[t] = bank(2 + t, [S], f"y_whole{t}")
+            times_x(y_whole[t][:], w1_plane(t), slice(0, S))
+        deal(nc.vector, W2, w_raw[W2][:], I32)
+        deal(nc.gpsimd, "s2", w2_scales_raw[:], U8)
+        deal(nc.vector, W3, w_raw[W3][:], I32)
+        deal(nc.gpsimd, W4, w_raw[W4][:], I32)
+        deal(nc.gpsimd, "s34", w34_scales_raw[:], U8)
+        for h in range(2):
+            nc.scalar.copy(out=y_window[0][:, half_cols(h)], in_=y_part[0, h][:])
+            nc.vector.tensor_copy(out=y_window[1][:, half_cols(h)], in_=y_part[1, h][:])
+        for t in (2, 3):
+            nc.vector.tensor_copy(out=y_window[t][:], in_=y_whole[t][:])
 
-        turned_low = psum.tile([P, 2, 2, P], F32, name="turned_low", tag="bank0")
-        turned_high = [psum.tile([P, 2, P], F32, name=f"turned_high{i}", tag=f"bank{2 + i}") for i in range(2)]
+        slots = keep.tile([P, 8, HALF], F32, name="slots", align_bytes=64)
+        h_rows = keep.tile([P, 6, HALF], F32, name="h_rows", align_bytes=64)
+        h_sum = [h_rows[:, 0:4, :], h_rows[:, 2:6, :]]
 
-        def turn(source, t, last):
-            u, e = divmod(t, 2)
-            for i in range(2):
-                edge = e == last and (u == 1 or i == last)
-                nc.tensor.matmul(
-                    turned_high[i][:, e, :] if u else turned_low[:, i, e, :], source[:, block_cols(i)], identity[:],
-                    is_transpose=True, start=edge and not last, stop=edge and bool(last),
-                )
+        def fetch(slot, t, lists, h):
+            nc.scalar.activation(slots[:, slot, :], y_window[t][:].indirect(entries(lists, h)), COPY)
+
+        def fetch_add(t, h, slot):
+            nc.vector.tensor_tensor(h_sum[h][:, t, :], y_window[t][:].indirect(entries(p2_sb, h)), slots[:, slot, :], ADD)
 
         for t in range(PACK):
-            turn(y_window[t], t, 0)
+            fetch(t, t, p1_sb, 0)
+        for t in range(PACK):
+            fetch_add(t, 0, t)
 
-        h_sum = {}
-        h1 = {}
-        z_early = [late.tile([P, HALF, PACK], BF16, name=f"z_early{w}", align_bytes=64, offset=4 * HALF * (4 + 2 * w)) for w in (Z, Z2)]
-        z_block = {b: keep.tile([P, 2, BLK, PACK], BF16, name=f"z_block{b}", align_bytes=64) for b in (2, 3)}
+        side = {}
+
+        def side_products(b):
+            for which, k, weights in ((Z, (6, 0)[b % 2], w1_plane), (Z2, (7, 1)[b % 2], lambda t: weight(W2, t))):
+                side[b, which] = bank(k, [PACK, BLK], f"side{b}{which}")
+                for t in range(PACK):
+                    times_x(side[b, which][:, t, :], weights(t), block_cols(b))
+
+        side_products(0)
+        side_products(1)
+
+        for t in (2, 3):
+            fetch(2 * t, t, p1_sb, 1)
+            fetch(2 * t + 1, t, p2_sb, 1)
+            nc.gpsimd.tensor_tensor(h_sum[1][:, t, :], slots[:, 2 * t, :], slots[:, 2 * t + 1, :], ADD)
+        fetch(0, 0, p1_sb, 1)
+        fetch(1, 1, p1_sb, 1)
+        fetch(2, 1, p2_sb, 1)
+
+        z_bf = [keep.tile([P, 2, BLK, PACK], BF16, name=f"z_bf{b}", align_bytes=64) for b in range(BLOCKS)]
         by_lines = "p t (c i) -> p c t i"
+        flat = "p j t -> p (j t)"
 
-        def z_values(b, which):
-            return z_early[which][:, block_cols(b), :] if b < 2 else z_block[b][:, which]
-
-        def gather_h1(t, h, pool, **place):
-            h1[t, h] = pool.tile([P, HALF], F32, name=f"h1_{t}{h}", align_bytes=64, **place)
-            nc.vector.tensor_copy(out=h1[t, h][:], in_=y_window[t][:].indirect(entries(p1_sb, h)))
-
-        def gather_h2(t, h):
-            nc.vector.tensor_tensor(h_sum[h][:, t, :], y_window[t][:].indirect(entries(p2_sb, h)), h1[t, h][:], ADD)
-            if h == 0:
-                turn(h_sum[0][:, t, :], t, 1)
-
-        def mix(engine, out, h, cols, other, which, line):
-            engine.tensor_tensor(
-                out.rearrange("p (c i) t -> p c t i", i=line),
-                h_sum[h][:, :, cols].rearrange(by_lines, i=line),
-                other.rearrange(by_lines, i=line),
+        def mix(b, which):
+            h, inner = divmod(b, 2)
+            nc.vector.tensor_tensor(
+                z_bf[b][:, which].rearrange("p (c i) t -> p c t i", i=LINE),
+                h_sum[h][:, :, block_cols(inner)].rearrange(by_lines, i=LINE),
+                side[b, which][:].rearrange(by_lines, i=LINE),
                 MULT if which == Z2 else ADD,
             )
-
-        def pool_product(out, h, cols, c_words):
-            nc.gpsimd.tensor_tensor(out, h_sum[h][:, :, cols].rearrange("p t j -> p j t"), c_words, MULT)
-
-        for t in range(PACK):
-            gather_h1(t, 0, keep, tag=f"h1_of_{t}")
-        w2_scales_dealt = keep.tile([P, H], U8, name="w2_scales_dealt", tag="w3_raw", align_bytes=64)
-        w34_scales_dealt = keep.tile([P, H], U8, name="w34_scales_dealt", align_bytes=64)
-        for out, raw in ((w2_scales_dealt, w_scales_raw), (w34_scales_dealt, w34_scales_raw[:])):
-            nc.gpsimd.tensor_copy(out=out[:].rearrange("p (t m) -> p t m", t=PACK), in_=raw.rearrange("p (m t) -> p t m", t=PACK))
-        dealt_scales = {W2: w2_scales_dealt[:], W3: w34_scales_dealt[:], W4: w34_scales_dealt[SCALE_ROWS:, :]}
-        h_sum[0] = late.tile([P, PACK, HALF], F32, name="h_sum0", align_bytes=64, offset=0)
-        c_bank = [psum.tile([P, PACK, BLK], F32, name=f"c_bank{b}", tag=f"bank{PACK + b}") for b in range(BLOCKS)]
-        for b in range(BLOCKS):
-            for t in range(PACK):
-                nc.tensor.matmul_mx(
-                    out=c_bank[b][:, t, :],
-                    **weight(W2, t),
-                    rhs=x_picked[:, block_cols(b)].bitcast(FP8X4),
-                    rhs_scale=x_scale_picked[:, block_cols(b)],
-                    start=True,
-                    stop=True,
-                )
-        c_first = keep.tile([P, POOL_COLS, PACK], F32, name="c_first")
-        nc.scalar.copy(out=c_first[:, :BLK, :], in_=c_bank[0][:].rearrange("p t j -> p j t"))
-        c_last = keep.tile([P, POOL_LAST, PACK], F32, name="c_last")
-        nc.scalar.copy(out=c_last[:], in_=c_bank[LAST][:, :, :POOL_LAST].rearrange("p t j -> p j t"))
-        gather_h2(0, 0)
-        gather_h2(1, 0)
-        low_bf = keep.tile([P, 2, P, 2], BF16, name="low_bf", tag="low_bf", align_bytes=64)
-        nc.scalar.copy(out=low_bf[:], in_=turned_low[:].rearrange("j i e p -> j i p e"))
-        back = [psum.tile([P, 2, BLK], F32, name=f"back{i}", tag=f"bank{i}") for i in range(2)]
-        for i in range(2):
-            nc.tensor.transpose(back[i][:, 0, :], low_bf[:, i].rearrange("j p e -> j (p e)").bitcast(F32), identity[:])
-        gather_h2(2, 0)
-        gather_h2(3, 0)
-        for i in range(2):
-            high_bf = keep.tile([P, P, 2], BF16, name=f"high_bf{i}", tag=f"high_bf{i}", align_bytes=64)
-            nc.scalar.copy(out=high_bf[:], in_=turned_high[i][:].rearrange("j e p -> j p e"))
-            nc.tensor.transpose(back[i][:, 1, :], high_bf[:].rearrange("j p e -> j (p e)").bitcast(F32), identity[:])
-        for i in range(2):
-            z_words = z_values(i, Z).rearrange("p j t -> p (j t)").bitcast(F32).rearrange("p (j u) -> p j u", u=2)
-            nc.scalar.copy(out=z_words, in_=back[i][:].rearrange("p u j -> p j u"))
-        pool_product(z_early[Z2][:, :POOL_COLS, :], 0, slice(0, POOL_COLS), c_first[:])
 
         out_scales = keep.tile([P, S], U8, name="out_scales", align_bytes=64)
         out_rows = out_0.rearrange("(p t) j -> p t j", t=PACK)
         out_words = words_of(out_1)
         o_bank = {}
+        o_tags = {0: (2,), 1: (3,), 2: (4,), 3: (5, 2)}
 
-        def quantise(values, parts, **place):
+        def quantise(b, parts):
             width = BLK * len(parts)
-            codes = keep.tile([P, width], U32, name=f"codes{parts[0][0]}{parts[0][1]}", align_bytes=64, **place)
-            scales = keep.tile([P, width], U8, name=f"scales{parts[0][0]}{parts[0][1]}", align_bytes=64)
+            codes = keep.tile([P, width], U32, name=f"codes{b}{parts[0]}", align_bytes=64)
+            scales = keep.tile([P, width], U8, name=f"scales{b}{parts[0]}", align_bytes=64)
+            values = z_bf[b][:, parts[0] : parts[-1] + 1].rearrange("p w j t -> p (w j t)")
             nc.vector.quantize_mx(out=codes[:].bitcast(FP8X4), scales=scales[:], in_=values)
-            for i, (b, which) in sorted(enumerate(parts), key=lambda part: part[1][0]):
+            for i, which in enumerate(parts):
                 first = b not in o_bank
-                group = 2 if b == LAST else PACK
+                group = PACK // len(o_tags[b])
                 if first:
-                    tags = (2, 3) if b == LAST else (PACK + b,)
-                    o_bank[b] = [psum.tile([P, group, BLK], F32, name=f"o_bank{b}{k}", tag=f"bank{k}") for k in tags]
+                    o_bank[b] = [bank(k, [group, BLK], f"o_bank{b}{k}") for k in o_tags[b]]
                 for t in range(PACK):
                     nc.tensor.matmul_mx(
                         out=o_bank[b][t // group][:, t % group, :],
@@ -264,57 +230,38 @@ def tile_picked_ngcf8_relu_po_kernel(
         out_bf = [keep.tile([P, HALF, PACK], BF16, name=f"out_bf{h}", align_bytes=64) for h in range(2)]
         out_codes = keep.tile([P, S], U32, name="out_codes", align_bytes=64)
 
-        def empty_early(b):
-            nc.scalar.activation(early_f32[:, :, block_cols(b)], o_bank[b][0][:], RELU)
-
         def quantise_out(h, inner):
             cols = slice(h * HALF + inner.start, h * HALF + inner.stop)
-            nc.vector.quantize_mx(out=out_codes[:, cols].bitcast(FP8X4), scales=out_scales[:, cols], in_=out_bf[h][:, inner, :].rearrange("p j t -> p (j t)"))
+            nc.vector.quantize_mx(out=out_codes[:, cols].bitcast(FP8X4), scales=out_scales[:, cols], in_=out_bf[h][:, inner, :].rearrange(flat))
             if h == 1:
                 stored = slice(0 if inner.start == 0 else cols.start, cols.stop)
                 nc.sync.dma_start(out=out_words[:, stored], in_=out_codes[:, stored].bitcast(I32))
 
-        flat = "p j t -> p (j t)"
-        gather_h1(0, 1, keep, tag="h1_of_2")
-        gather_h1(1, 1, keep, tag="h1_of_3")
-        gather_h1(2, 1, reuse, offset=4 * H * W2)
-        mix(nc.vector, z_early[Z2][:, POOL_COLS:, :], 0, slice(POOL_COLS, HALF), c_bank[1][:, :, POOL_COLS - BLK :], Z2, LINE)
-        gather_h1(3, 1, reuse, offset=4 * H * W2 + 4 * HALF)
-        quantise(z_early[Z2][:].rearrange(flat), [(0, Z2), (1, Z2)], tag="high_bf1")
-        quantise(z_early[Z][:].rearrange(flat), [(0, Z), (1, Z)])
-        empty_early(0)
-        empty_early(1)
+        for b in range(2):
+            mix(b, Z)
+            mix(b, Z2)
+            side_products(2 + b)
+        quantise(0, (Z, Z2))
+        fetch_add(0, 1, 0)
+        quantise(1, (Z, Z2))
+        nc.vector.tensor_tensor(h_sum[1][:, 1, :], slots[:, 1, :], slots[:, 2, :], ADD)
+        for b in range(2):
+            nc.scalar.activation(early_f32[:, :, block_cols(b)], o_bank[b][0][:], RELU)
         nc.sync.dma_start(out=out_rows[:, :, half_cols(0)], in_=early_f32[:])
         nc.scalar.copy(out=out_bf[0][:].rearrange("p (c i) t -> p c t i", i=LINE), in_=early_f32[:].rearrange(by_lines, i=LINE))
-        y_again = {b: psum.tile([P, PACK, BLK], F32, name=f"y_again{b}", tag=f"bank{PACK * (b - 2)}") for b in (2, 3)}
-        for b in (2, 3):
-            for t in range(PACK):
-                nc.tensor.matmul_mx(
-                    out=y_again[b][:, t, :],
-                    lhsT=w1_codes[:, block_cols(t)].bitcast(FP8X4),
-                    lhsT_scale=w1_scales[:, block_cols(t)],
-                    rhs=x_picked[:, block_cols(b)].bitcast(FP8X4),
-                    rhs_scale=x_scale_picked[:, block_cols(b)],
-                    start=True,
-                    stop=True,
-                )
-        h_sum[1] = late.tile([P, PACK, HALF], F32, name="h_sum1", align_bytes=64, offset=4 * HALF * 4)
-        for t in range(PACK):
-            gather_h2(t, 1)
-        pool_product(z_values(3, Z2)[:, :POOL_LAST, :], 1, slice(BLK, BLK + POOL_LAST), c_last[:])
-        mix(nc.vector, z_values(2, Z2), 1, block_cols(0), c_bank[2][:], Z2, LINE)
-        mix(nc.vector, z_values(2, Z), 1, block_cols(0), y_again[2][:], Z, LINE)
-        quantise(z_values(2, Z2).rearrange(flat), [(2, Z2)])
-        mix(nc.vector, z_values(3, Z2)[:, POOL_LAST:, :], 1, slice(BLK + POOL_LAST, HALF), c_bank[3][:, :, POOL_LAST:], Z2, LINE)
-        quantise(z_values(2, Z).rearrange(flat), [(2, Z)])
+        mix(2, Z)
+        mix(2, Z2)
+        quantise(2, (Z,))
+        mix(3, Z)
+        quantise(2, (Z2,))
         third_f32 = keep.tile([P, PACK, BLK], F32, name="third_f32")
         nc.scalar.activation(third_f32[:], o_bank[2][0][:], RELU)
         nc.sync.dma_start(out=out_rows[:, :, block_cols(2)], in_=third_f32[:])
         nc.scalar.activation(out_bf[1][:, block_cols(0), :], o_bank[2][0][:].rearrange("p t j -> p j t"), RELU)
-        quantise(z_values(3, Z2).rearrange(flat), [(3, Z2)])
-        mix(nc.vector, z_values(3, Z), 1, block_cols(1), y_again[3][:], Z, LINE)
-        quantise(z_values(3, Z).rearrange(flat), [(3, Z)])
+        mix(3, Z2)
+        quantise(3, (Z,))
         quantise_out(0, half_cols(0))
+        quantise(3, (Z2,))
         low, high = o_bank[LAST]
         last_f32 = keep.tile([P, PACK, BLK], F32, name="last_f32")
         last_bf = out_bf[1][:, block_cols(1), :]

@@ -38,6 +38,7 @@ def tile_picked_ngcf8_relu_po_kernel(
     nc = tc.nc
     with ExitStack() as ctx:
         keep = ctx.enter_context(tc.tile_pool(name="keep", bufs=1))
+        reuse = ctx.enter_context(tc.tile_pool(name="reuse", bufs=1))
         psum = ctx.enter_context(tc.psum_pool(name="psum", bufs=1))
 
         def words_of(dram):
@@ -64,7 +65,7 @@ def tile_picked_ngcf8_relu_po_kernel(
         p2_sb = keep.tile([P, S // LIST_ROWS], U16, name="p2_sb")
         x_table = keep.tile([P, T], U32, name="x_table", align_bytes=64)
         x_scale_table = keep.tile([P, T], U8, name="x_scale_table", align_bytes=64)
-        w1_raw = keep.tile([P, PACK, H], F32, name="w1_raw", tag="w1_raw", align_bytes=64)
+        w1_raw = reuse.tile([P, PACK, H], F32, name="w1_raw", align_bytes=64, offset=0)
         w_raw = [keep.tile([P, H], I32, name=f"w_raw{i}", align_bytes=64) for i in range(3)]
         w2_scales_raw = keep.tile([P, H], U8, name="w2_scales_raw", align_bytes=64)
         w34_scales_raw = keep.tile([P, H], U8, name="w34_scales_raw", align_bytes=64)
@@ -105,11 +106,10 @@ def tile_picked_ngcf8_relu_po_kernel(
             cols = slice(planes.start * P, planes.stop * P)
             nc.vector.quantize_mx(out=w1_codes[:, cols].bitcast(FP8X4), scales=w1_scales[:, cols], in_=w1_bf[:, planes].rearrange("p t m j -> p (t m j)"))
 
-        quantise_w1(slice(0, 2))
+        quantise_w1(slice(0, PACK))
         x_picked = keep.tile([P, S], U32, name="x_picked", align_bytes=64)
         for h in range(2):
             nc.vector.tensor_copy(out=x_picked[:, half_cols(h)], in_=x_table[:].indirect(entries(offs_sb, h)))
-        quantise_w1(slice(2, PACK))
 
         def bank(k, shape, name):
             return psum.tile([P] + shape, F32, name=name, tag=f"bank{k}")
@@ -122,17 +122,16 @@ def tile_picked_ngcf8_relu_po_kernel(
 
         dealt = {}
 
-        def deal(engine, key, raw, dtype, **place):
-            dealt[key] = keep.tile([P, H], dtype, name=f"dealt_{key}", align_bytes=64, **place)
-            order = "p m t" if engine is nc.vector else "p t m"
-            engine.tensor_copy(out=dealt[key][:].rearrange(f"p (t m) -> {order}", t=PACK), in_=raw.rearrange(f"p (m t) -> {order}", t=PACK))
+        def deal(engine, key, raw, dtype, pool, **place):
+            dealt[key] = pool.tile([P, H], dtype, name=f"dealt_{key}", align_bytes=64, **place)
+            copy, order = (nc.scalar.copy, "p m t") if engine is nc.scalar else (nc.gpsimd.tensor_copy, "p t m")
+            copy(out=dealt[key][:].rearrange(f"p (t m) -> {order}", t=PACK), in_=raw.rearrange(f"p (m t) -> {order}", t=PACK))
 
         def weight(i, t):
             cols = block_cols(t)
             scales = dealt["s2"][:] if i == W2 else dealt["s34"][SCALE_ROWS * (i - W3) :, :]
             return dict(lhsT=dealt[i][:, cols].bitcast(FP8X4), lhsT_scale=scales[:, cols])
 
-        y_window = [keep.tile([P, S], F32, name=f"y_window{t}") for t in range(PACK)]
         y_part = {}
         for k, (t, h) in enumerate(((0, 0), (1, 0), (0, 1), (1, 1))):
             y_part[t, h] = bank(k, [HALF], f"y_part{t}{h}")
@@ -141,36 +140,35 @@ def tile_picked_ngcf8_relu_po_kernel(
         for t in (2, 3):
             y_whole[t] = bank(2 + t, [S], f"y_whole{t}")
             times_x(y_whole[t][:], w1_plane(t), slice(0, S))
-        deal(nc.vector, W2, w_raw[W2][:], I32)
-        deal(nc.gpsimd, "s2", w2_scales_raw[:], U8)
-        deal(nc.vector, W3, w_raw[W3][:], I32)
-        deal(nc.gpsimd, W4, w_raw[W4][:], I32)
-        deal(nc.gpsimd, "s34", w34_scales_raw[:], U8)
+        deal(nc.scalar, W2, w_raw[W2][:].bitcast(U32), U32, keep)
+        deal(nc.gpsimd, "s2", w2_scales_raw[:], U8, keep)
+        for i in (W3, W4):
+            deal(nc.gpsimd, i, w_raw[i][:], I32, keep)
+        y_window = [keep.tile([P, S], F32, name=f"y_window{t}") for t in range(PACK)]
         for h in range(2):
             nc.scalar.copy(out=y_window[0][:, half_cols(h)], in_=y_part[0, h][:])
             nc.vector.tensor_copy(out=y_window[1][:, half_cols(h)], in_=y_part[1, h][:])
         for t in (2, 3):
             nc.vector.tensor_copy(out=y_window[t][:], in_=y_whole[t][:])
 
-        slots = keep.tile([P, 8, HALF], F32, name="slots", align_bytes=64)
-        h_rows = keep.tile([P, 6, HALF], F32, name="h_rows", align_bytes=64)
-        h_sum = [h_rows[:, 0:4, :], h_rows[:, 2:6, :]]
+        h1 = keep.tile([P, PACK, HALF], F32, name="h1", align_bytes=64)
+        h_sum = keep.tile([P, PACK, HALF], F32, name="h_sum", align_bytes=64)
 
-        def fetch(slot, t, lists, h):
-            nc.scalar.activation(slots[:, slot, :], y_window[t][:].indirect(entries(lists, h)), COPY)
+        def fetch(out, t, lists, h):
+            nc.scalar.activation(out, y_window[t][:].indirect(entries(lists, h)), COPY)
 
-        def fetch_add(t, h, slot):
-            nc.vector.tensor_tensor(h_sum[h][:, t, :], y_window[t][:].indirect(entries(p2_sb, h)), slots[:, slot, :], ADD)
-
+        first_h1 = [h1[:, 0, :], h1[:, 1, :], h1[:, 2, :], w1_raw[:, 0, :HALF]]
         for t in range(PACK):
-            fetch(t, t, p1_sb, 0)
+            fetch(first_h1[t], t, p1_sb, 0)
         for t in range(PACK):
-            fetch_add(t, 0, t)
+            nc.vector.tensor_tensor(h_sum[:, t, :], y_window[t][:].indirect(entries(p2_sb, 0)), first_h1[t], ADD)
+        deal(nc.gpsimd, "s34", w34_scales_raw[:], U8, reuse, offset=0)
+        h2 = reuse.tile([P, PACK - 1, HALF], F32, name="h2", align_bytes=64, offset=1024)
 
         side = {}
 
         def side_products(b):
-            for which, k, weights in ((Z, (6, 0)[b % 2], w1_plane), (Z2, (7, 1)[b % 2], lambda t: weight(W2, t))):
+            for which, k, weights in ((Z, (6, 0, 7, 1)[b], w1_plane), (Z2, (7, 1, 6, 0)[b], lambda t: weight(W2, t))):
                 side[b, which] = bank(k, [PACK, BLK], f"side{b}{which}")
                 for t in range(PACK):
                     times_x(side[b, which][:, t, :], weights(t), block_cols(b))
@@ -178,23 +176,19 @@ def tile_picked_ngcf8_relu_po_kernel(
         side_products(0)
         side_products(1)
 
-        for t in (2, 3):
-            fetch(2 * t, t, p1_sb, 1)
-            fetch(2 * t + 1, t, p2_sb, 1)
-            nc.gpsimd.tensor_tensor(h_sum[1][:, t, :], slots[:, 2 * t, :], slots[:, 2 * t + 1, :], ADD)
-        fetch(0, 0, p1_sb, 1)
-        fetch(1, 1, p1_sb, 1)
-        fetch(2, 1, p2_sb, 1)
+        for out, lists in ((h1, p1_sb), (h2, p2_sb)):
+            for t in range(out.shape[1]):
+                fetch(out[:, t, :], t, lists, 1)
 
         z_bf = [keep.tile([P, 2, BLK, PACK], BF16, name=f"z_bf{b}", align_bytes=64) for b in range(BLOCKS)]
         by_lines = "p t (c i) -> p c t i"
         flat = "p j t -> p (j t)"
 
         def mix(b, which):
-            h, inner = divmod(b, 2)
+            inner = b % 2
             nc.vector.tensor_tensor(
                 z_bf[b][:, which].rearrange("p (c i) t -> p c t i", i=LINE),
-                h_sum[h][:, :, block_cols(inner)].rearrange(by_lines, i=LINE),
+                h_sum[:, :, block_cols(inner)].rearrange(by_lines, i=LINE),
                 side[b, which][:].rearrange(by_lines, i=LINE),
                 MULT if which == Z2 else ADD,
             )
@@ -227,51 +221,48 @@ def tile_picked_ngcf8_relu_po_kernel(
                     )
 
         early_f32 = keep.tile([P, PACK, HALF], F32, name="early_f32")
-        out_bf = [keep.tile([P, HALF, PACK], BF16, name=f"out_bf{h}", align_bytes=64) for h in range(2)]
+        out_bf = [keep.tile([P, HALF, PACK], BF16, name=f"out_bf{h}", tag=f"out_bf{h}", align_bytes=64) for h in range(2)]
         out_codes = keep.tile([P, S], U32, name="out_codes", align_bytes=64)
 
-        def quantise_out(h, inner):
-            cols = slice(h * HALF + inner.start, h * HALF + inner.stop)
-            nc.vector.quantize_mx(out=out_codes[:, cols].bitcast(FP8X4), scales=out_scales[:, cols], in_=out_bf[h][:, inner, :].rearrange(flat))
-            if h == 1:
-                stored = slice(0 if inner.start == 0 else cols.start, cols.stop)
-                nc.sync.dma_start(out=out_words[:, stored], in_=out_codes[:, stored].bitcast(I32))
+        def quantise_out(h):
+            cols = half_cols(h)
+            nc.vector.quantize_mx(out=out_codes[:, cols].bitcast(FP8X4), scales=out_scales[:, cols], in_=out_bf[h][:].rearrange(flat))
+            nc.sync.dma_start(out=out_words[:, cols], in_=out_codes[:, cols].bitcast(I32))
 
         for b in range(2):
             mix(b, Z)
             mix(b, Z2)
             side_products(2 + b)
         quantise(0, (Z, Z2))
-        fetch_add(0, 1, 0)
+        nc.vector.tensor_tensor(h_sum[:, 3, :], y_window[3][:].indirect(entries(p2_sb, 1)), h1[:, 3, :], ADD)
+        nc.vector.tensor_tensor(h_sum[:, :3, :], h1[:, :3, :], h2[:], ADD)
         quantise(1, (Z, Z2))
-        nc.vector.tensor_tensor(h_sum[1][:, 1, :], slots[:, 1, :], slots[:, 2, :], ADD)
         for b in range(2):
             nc.scalar.activation(early_f32[:, :, block_cols(b)], o_bank[b][0][:], RELU)
+            nc.scalar.activation(out_bf[0][:, block_cols(b), :], o_bank[b][0][:].rearrange("p t j -> p j t"), RELU)
         nc.sync.dma_start(out=out_rows[:, :, half_cols(0)], in_=early_f32[:])
-        nc.scalar.copy(out=out_bf[0][:].rearrange("p (c i) t -> p c t i", i=LINE), in_=early_f32[:].rearrange(by_lines, i=LINE))
         mix(2, Z)
         mix(2, Z2)
         quantise(2, (Z,))
-        mix(3, Z)
         quantise(2, (Z2,))
+        mix(3, Z)
         third_f32 = keep.tile([P, PACK, BLK], F32, name="third_f32")
         nc.scalar.activation(third_f32[:], o_bank[2][0][:], RELU)
         nc.sync.dma_start(out=out_rows[:, :, block_cols(2)], in_=third_f32[:])
         nc.scalar.activation(out_bf[1][:, block_cols(0), :], o_bank[2][0][:].rearrange("p t j -> p j t"), RELU)
         mix(3, Z2)
         quantise(3, (Z,))
-        quantise_out(0, half_cols(0))
         quantise(3, (Z2,))
+        quantise_out(0)
         low, high = o_bank[LAST]
-        last_f32 = keep.tile([P, PACK, BLK], F32, name="last_f32")
+        last_f32 = keep.tile([P, PACK, BLK], F32, name="last_f32", tag="out_bf0", align_bytes=64)
         last_bf = out_bf[1][:, block_cols(1), :]
-        quantise_out(1, block_cols(0))
         nc.scalar.activation(last_f32[:, :2, :], low[:], RELU)
         nc.vector.tensor_scalar_max(last_f32[:, 2:, :], high[:], 0.0)
         nc.sync.dma_start(out=out_rows[:, :, block_cols(LAST)], in_=last_f32[:])
         nc.scalar.activation(last_bf[:, :, :2], low[:].rearrange("p e j -> p j e"), RELU)
         nc.vector.tensor_scalar_max(last_bf[:, :, 2:], high[:].rearrange("p e j -> p j e"), 0.0)
-        quantise_out(1, block_cols(1))
+        quantise_out(1)
 
         for q, queue in enumerate((nc.sync, nc.scalar, nc.sync, nc.scalar)):
             queue.dma_start(

@@ -142,8 +142,6 @@ def tile_picked_ngcf8_relu_po_kernel(
             times_x(y_whole[t][:], w1_plane(t), slice(0, S))
         deal(nc.scalar, W2, w_raw[W2][:].bitcast(U32), U32, keep)
         deal(nc.gpsimd, "s2", w2_scales_raw[:], U8, keep)
-        for i in (W3, W4):
-            deal(nc.gpsimd, i, w_raw[i][:], I32, keep)
         y_window = [keep.tile([P, S], F32, name=f"y_window{t}") for t in range(PACK)]
         for h in range(2):
             nc.scalar.copy(out=y_window[0][:, half_cols(h)], in_=y_part[0, h][:])
@@ -162,6 +160,7 @@ def tile_picked_ngcf8_relu_po_kernel(
             fetch(first_h1[t], t, p1_sb, 0)
         for t in range(PACK):
             nc.vector.tensor_tensor(h_sum[:, t, :], y_window[t][:].indirect(entries(p2_sb, 0)), first_h1[t], ADD)
+        deal(nc.gpsimd, W3, w_raw[W3][:], I32, reuse, offset=6144)
         deal(nc.gpsimd, "s34", w34_scales_raw[:], U8, reuse, offset=0)
         h2 = reuse.tile([P, PACK - 1, HALF], F32, name="h2", align_bytes=64, offset=1024)
 
@@ -179,15 +178,19 @@ def tile_picked_ngcf8_relu_po_kernel(
         for out, lists in ((h1, p1_sb), (h2, p2_sb)):
             for t in range(out.shape[1]):
                 fetch(out[:, t, :], t, lists, 1)
+        deal(nc.scalar, W4, w_raw[W4][:].bitcast(U32), U32, reuse, offset=4096)
 
-        z_bf = [keep.tile([P, 2, BLK, PACK], BF16, name=f"z_bf{b}", align_bytes=64) for b in range(BLOCKS)]
+        z_bf = [keep.tile([P, 2, BLK, PACK], BF16, name=f"z_bf{b}", align_bytes=64) for b in range(LAST)]
+
+        def z_values(b, which):
+            return z_bf[min(b, LAST - 1)][:, which]
         by_lines = "p t (c i) -> p c t i"
         flat = "p j t -> p (j t)"
 
         def mix(b, which):
             inner = b % 2
             nc.vector.tensor_tensor(
-                z_bf[b][:, which].rearrange("p (c i) t -> p c t i", i=LINE),
+                z_values(b, which).rearrange("p (c i) t -> p c t i", i=LINE),
                 h_sum[:, :, block_cols(inner)].rearrange(by_lines, i=LINE),
                 side[b, which][:].rearrange(by_lines, i=LINE),
                 MULT if which == Z2 else ADD,
@@ -203,7 +206,7 @@ def tile_picked_ngcf8_relu_po_kernel(
             width = BLK * len(parts)
             codes = keep.tile([P, width], U32, name=f"codes{b}{parts[0]}", align_bytes=64)
             scales = keep.tile([P, width], U8, name=f"scales{b}{parts[0]}", align_bytes=64)
-            values = z_bf[b][:, parts[0] : parts[-1] + 1].rearrange("p w j t -> p (w j t)")
+            values = z_bf[b][:].rearrange("p w j t -> p (w j t)") if len(parts) == 2 else z_values(b, parts[0]).rearrange(flat)
             nc.vector.quantize_mx(out=codes[:].bitcast(FP8X4), scales=scales[:], in_=values)
             for i, which in enumerate(parts):
                 first = b not in o_bank
@@ -221,12 +224,14 @@ def tile_picked_ngcf8_relu_po_kernel(
                     )
 
         early_f32 = keep.tile([P, PACK, HALF], F32, name="early_f32")
-        out_bf = [keep.tile([P, HALF, PACK], BF16, name=f"out_bf{h}", tag=f"out_bf{h}", align_bytes=64) for h in range(2)]
+        early_bf = keep.tile([P, LAST * BLK, PACK], BF16, name="early_bf", tag="early_bf", align_bytes=64)
+        last_bf = keep.tile([P, BLK, PACK], BF16, name="last_bf", align_bytes=64)
         out_codes = keep.tile([P, S], U32, name="out_codes", align_bytes=64)
 
-        def quantise_out(h):
-            cols = half_cols(h)
-            nc.vector.quantize_mx(out=out_codes[:, cols].bitcast(FP8X4), scales=out_scales[:, cols], in_=out_bf[h][:].rearrange(flat))
+        def quantise_out(values, cols):
+            nc.vector.quantize_mx(out=out_codes[:, cols].bitcast(FP8X4), scales=out_scales[:, cols], in_=values.rearrange(flat))
+
+        def store_words(cols):
             nc.sync.dma_start(out=out_words[:, cols], in_=out_codes[:, cols].bitcast(I32))
 
         for b in range(2):
@@ -239,7 +244,7 @@ def tile_picked_ngcf8_relu_po_kernel(
         quantise(1, (Z, Z2))
         for b in range(2):
             nc.scalar.activation(early_f32[:, :, block_cols(b)], o_bank[b][0][:], RELU)
-            nc.scalar.activation(out_bf[0][:, block_cols(b), :], o_bank[b][0][:].rearrange("p t j -> p j t"), RELU)
+            nc.scalar.activation(early_bf[:, block_cols(b), :], o_bank[b][0][:].rearrange("p t j -> p j t"), RELU)
         nc.sync.dma_start(out=out_rows[:, :, half_cols(0)], in_=early_f32[:])
         mix(2, Z)
         mix(2, Z2)
@@ -247,22 +252,24 @@ def tile_picked_ngcf8_relu_po_kernel(
         quantise(2, (Z2,))
         mix(3, Z)
         third_f32 = keep.tile([P, PACK, BLK], F32, name="third_f32")
+        nc.scalar.activation(early_bf[:, block_cols(2), :], o_bank[2][0][:].rearrange("p t j -> p j t"), RELU)
         nc.scalar.activation(third_f32[:], o_bank[2][0][:], RELU)
         nc.sync.dma_start(out=out_rows[:, :, block_cols(2)], in_=third_f32[:])
-        nc.scalar.activation(out_bf[1][:, block_cols(0), :], o_bank[2][0][:].rearrange("p t j -> p j t"), RELU)
         mix(3, Z2)
         quantise(3, (Z,))
         quantise(3, (Z2,))
-        quantise_out(0)
+        quantise_out(early_bf[:, half_cols(0), :], half_cols(0))
+        quantise_out(early_bf[:, block_cols(2), :], block_cols(2))
+        store_words(slice(0, LAST * BLK))
         low, high = o_bank[LAST]
-        last_f32 = keep.tile([P, PACK, BLK], F32, name="last_f32", tag="out_bf0", align_bytes=64)
-        last_bf = out_bf[1][:, block_cols(1), :]
+        last_f32 = keep.tile([P, PACK, BLK], F32, name="last_f32", tag="early_bf", align_bytes=64)
         nc.scalar.activation(last_f32[:, :2, :], low[:], RELU)
         nc.vector.tensor_scalar_max(last_f32[:, 2:, :], high[:], 0.0)
         nc.sync.dma_start(out=out_rows[:, :, block_cols(LAST)], in_=last_f32[:])
         nc.scalar.activation(last_bf[:, :, :2], low[:].rearrange("p e j -> p j e"), RELU)
         nc.vector.tensor_scalar_max(last_bf[:, :, 2:], high[:].rearrange("p e j -> p j e"), 0.0)
-        quantise_out(1)
+        quantise_out(last_bf[:], block_cols(LAST))
+        store_words(block_cols(LAST))
 
         for q, queue in enumerate((nc.sync, nc.scalar, nc.sync, nc.scalar)):
             queue.dma_start(

@@ -57,8 +57,8 @@ def tile_picked_ngcf8_relu_po_kernel(
         def half_cols(h):
             return slice(h * HALF, (h + 1) * HALF)
 
-        def entries(tile, h):
-            return tile[:, h * HALF // LIST_ROWS : (h + 1) * HALF // LIST_ROWS]
+        def entries(tile, cols):
+            return tile[:, cols.start // LIST_ROWS : cols.stop // LIST_ROWS]
 
         offs_sb = keep.tile([P, S // LIST_ROWS], U16, name="offs_sb")
         p1_sb = keep.tile([P, S // LIST_ROWS], U16, name="p1_sb")
@@ -108,8 +108,8 @@ def tile_picked_ngcf8_relu_po_kernel(
 
         quantise_w1(slice(0, PACK))
         x_picked = keep.tile([P, S], U32, name="x_picked", align_bytes=64)
-        for h in range(2):
-            nc.vector.tensor_copy(out=x_picked[:, half_cols(h)], in_=x_table[:].indirect(entries(offs_sb, h)))
+        for cols in (block_cols(0), block_cols(1), half_cols(1)):
+            nc.vector.tensor_copy(out=x_picked[:, cols], in_=x_table[:].indirect(entries(offs_sb, cols)))
 
         def bank(k, shape, name):
             return psum.tile([P] + shape, F32, name=name, tag=f"bank{k}")
@@ -132,34 +132,37 @@ def tile_picked_ngcf8_relu_po_kernel(
             scales = dealt["s2"][:] if i == W2 else dealt["s34"][SCALE_ROWS * (i - W3) :, :]
             return dict(lhsT=dealt[i][:, cols].bitcast(FP8X4), lhsT_scale=scales[:, cols])
 
-        y_part = {}
-        for k, (t, h) in enumerate(((0, 0), (1, 0), (0, 1), (1, 1))):
-            y_part[t, h] = bank(k, [HALF], f"y_part{t}{h}")
-            times_x(y_part[t, h][:], w1_plane(t), half_cols(h))
-        y_whole = {}
-        for t in (2, 3):
-            y_whole[t] = bank(2 + t, [S], f"y_whole{t}")
-            times_x(y_whole[t][:], w1_plane(t), slice(0, S))
+        y_part = {(t, h): bank(PACK * h + t, [HALF], f"y_part{t}{h}") for h in range(2) for t in range(PACK)}
+        for t in range(PACK):
+            times_x(y_part[t, 0][:, block_cols(0)], w1_plane(t), block_cols(0))
+        for t in range(PACK - 1):
+            times_x(y_part[t, 0][:, block_cols(1)], w1_plane(t), block_cols(1))
+        for t in range(PACK):
+            if t == 2:
+                times_x(y_part[3, 0][:, block_cols(1)], w1_plane(3), block_cols(1))
+            times_x(y_part[t, 1][:], w1_plane(t), half_cols(1))
         deal(nc.scalar, W2, w_raw[W2][:].bitcast(U32), U32, keep)
         deal(nc.gpsimd, "s2", w2_scales_raw[:], U8, keep)
         y_window = [keep.tile([P, S], F32, name=f"y_window{t}") for t in range(PACK)]
         for h in range(2):
             nc.scalar.copy(out=y_window[0][:, half_cols(h)], in_=y_part[0, h][:])
-            nc.vector.tensor_copy(out=y_window[1][:, half_cols(h)], in_=y_part[1, h][:])
-        for t in (2, 3):
-            nc.vector.tensor_copy(out=y_window[t][:], in_=y_whole[t][:])
+        for t, h in ((1, 0), (2, 0), (1, 1), (3, 0), (2, 1), (3, 1)):
+            nc.vector.tensor_copy(out=y_window[t][:, half_cols(h)], in_=y_part[t, h][:])
 
         h1 = keep.tile([P, PACK, HALF], F32, name="h1", align_bytes=64)
         h_sum = keep.tile([P, PACK, HALF], F32, name="h_sum", align_bytes=64)
 
         def fetch(out, t, lists, h):
-            nc.scalar.activation(out, y_window[t][:].indirect(entries(lists, h)), COPY)
+            nc.scalar.activation(out, y_window[t][:].indirect(entries(lists, half_cols(h))), COPY)
 
         first_h1 = [h1[:, 0, :], h1[:, 1, :], h1[:, 2, :], w1_raw[:, 0, :HALF]]
         for t in range(PACK):
             fetch(first_h1[t], t, p1_sb, 0)
-        for t in range(PACK):
-            nc.vector.tensor_tensor(h_sum[:, t, :], y_window[t][:].indirect(entries(p2_sb, 0)), first_h1[t], ADD)
+        for t in range(PACK - 1):
+            nc.vector.tensor_tensor(h_sum[:, t, :], y_window[t][:].indirect(entries(p2_sb, half_cols(0))), first_h1[t], ADD)
+        for b in range(2):
+            offsets = entries(p2_sb, block_cols(b))
+            nc.vector.tensor_tensor(h_sum[:, 3, block_cols(b)], y_window[3][:].indirect(offsets), first_h1[3][:, block_cols(b)], ADD)
         deal(nc.gpsimd, W3, w_raw[W3][:], I32, reuse, offset=6144)
         deal(nc.gpsimd, "s34", w34_scales_raw[:], U8, reuse, offset=0)
         h2 = reuse.tile([P, PACK - 1, HALF], F32, name="h2", align_bytes=64, offset=1024)
@@ -167,7 +170,7 @@ def tile_picked_ngcf8_relu_po_kernel(
         side = {}
 
         def side_products(b):
-            for which, k, weights in ((Z, (6, 0, 7, 1)[b], w1_plane), (Z2, (7, 1, 6, 0)[b], lambda t: weight(W2, t))):
+            for which, k, weights in ((Z, (0, 2, 1, 4)[b], w1_plane), (Z2, (1, 4, 0, 2)[b], lambda t: weight(W2, t))):
                 side[b, which] = bank(k, [PACK, BLK], f"side{b}{which}")
                 for t in range(PACK):
                     times_x(side[b, which][:, t, :], weights(t), block_cols(b))
@@ -200,7 +203,7 @@ def tile_picked_ngcf8_relu_po_kernel(
         out_rows = out_0.rearrange("(p t) j -> p t j", t=PACK)
         out_words = words_of(out_1)
         o_bank = {}
-        o_tags = {0: (2,), 1: (3,), 2: (4,), 3: (5, 2)}
+        o_tags = {0: (3,), 1: (5,), 2: (6,), 3: (7, 3)}
 
         def quantise(b, parts):
             width = BLK * len(parts)
@@ -239,9 +242,10 @@ def tile_picked_ngcf8_relu_po_kernel(
             mix(b, Z2)
             side_products(2 + b)
         quantise(0, (Z, Z2))
-        nc.vector.tensor_tensor(h_sum[:, 3, :], y_window[3][:].indirect(entries(p2_sb, 1)), h1[:, 3, :], ADD)
-        nc.vector.tensor_tensor(h_sum[:, :3, :], h1[:, :3, :], h2[:], ADD)
+        nc.vector.tensor_tensor(h_sum[:, 3, :], y_window[3][:].indirect(entries(p2_sb, half_cols(1))), h1[:, 3, :], ADD)
         quantise(1, (Z, Z2))
+        for b in range(2):
+            nc.vector.tensor_tensor(h_sum[:, :3, block_cols(b)], h1[:, :3, block_cols(b)], h2[:, :, block_cols(b)], ADD)
         for b in range(2):
             nc.scalar.activation(early_f32[:, :, block_cols(b)], o_bank[b][0][:], RELU)
             nc.scalar.activation(early_bf[:, block_cols(b), :], o_bank[b][0][:].rearrange("p t j -> p j t"), RELU)

@@ -27,7 +27,7 @@ BLK = 128
 BLOCKS = S // BLK
 LAST = BLOCKS - 1
 LINE = 2
-W1_SPLIT = 60
+W1_SPLIT = 88
 W2, W3, W4 = 0, 1, 2
 Z, Z2 = 0, 1
 
@@ -87,26 +87,23 @@ def tile_picked_ngcf8_relu_po_kernel(
         for i, scales in enumerate((w3_scales, w4_scales)):
             load_scale_rows(nc.sync, w34_scales_raw, SCALE_ROWS * i, scales)
 
-        x_scale_picked = keep.tile([P, S], U8, name="x_scale_picked", align_bytes=64)
-        nc.vector.tensor_copy(out=x_scale_picked[:], in_=x_scale_table[:].indirect(offs_sb[:]))
-        w1_bf = keep.tile([P, PACK, P, PACK], BF16, name="w1_bf", align_bytes=64)
+        w1_bf = [keep.tile([P, 2, P, PACK], BF16, name=f"w1_bf{u}", tag=f"w1_bf{u}", align_bytes=64) for u in range(2)]
 
-        def w1_part(lo, hi):
+        def w1_part(u, lo, hi):
             return (
-                w1_bf[:, :, lo:hi, :].rearrange("p t m j -> p m j t"),
-                w1_raw[:, :, PACK * lo : PACK * hi].rearrange("p j (m t) -> p m j t", t=PACK),
+                w1_bf[u][:, :, lo:hi, :].rearrange("p e m j -> p m j e"),
+                w1_raw[:, :, PACK * lo : PACK * hi].rearrange("p j (m t) -> p m j t", t=PACK)[:, :, :, 2 * u : 2 * u + 2],
             )
 
-        nc.vector.tensor_copy(*w1_part(0, W1_SPLIT))
-        nc.scalar.activation(*w1_part(W1_SPLIT, P), COPY)
+        for u in range(2):
+            nc.vector.tensor_copy(*w1_part(u, 0, W1_SPLIT))
+            nc.scalar.activation(*w1_part(u, W1_SPLIT, P), COPY)
         w1_codes = keep.tile([P, H], U32, name="w1_codes", align_bytes=64)
         w1_scales = keep.tile([P, H], U8, name="w1_scales", align_bytes=64)
-
-        def quantise_w1(planes):
-            cols = slice(planes.start * P, planes.stop * P)
-            nc.vector.quantize_mx(out=w1_codes[:, cols].bitcast(FP8X4), scales=w1_scales[:, cols], in_=w1_bf[:, planes].rearrange("p t m j -> p (t m j)"))
-
-        quantise_w1(slice(0, PACK))
+        for u in range(2):
+            nc.vector.quantize_mx(out=w1_codes[:, half_cols(u)].bitcast(FP8X4), scales=w1_scales[:, half_cols(u)], in_=w1_bf[u][:].rearrange("p e m j -> p (e m j)"))
+        x_scale_picked = keep.tile([P, S], U8, name="x_scale_picked", tag="w1_bf0", align_bytes=64)
+        nc.vector.tensor_copy(out=x_scale_picked[:], in_=x_scale_table[:].indirect(offs_sb[:]))
         x_picked = keep.tile([P, S], U32, name="x_picked", align_bytes=64)
         for cols in (block_cols(0), block_cols(1), half_cols(1)):
             nc.vector.tensor_copy(out=x_picked[:, cols], in_=x_table[:].indirect(entries(offs_sb, cols)))

@@ -27,7 +27,6 @@ BLK = 128
 BLOCKS = S // BLK
 LAST = BLOCKS - 1
 LINE = 2
-W1_SPLIT = 88
 W2, W3, W4 = 0, 1, 2
 Z, Z2 = 0, 1
 
@@ -44,8 +43,8 @@ def tile_picked_ngcf8_relu_po_kernel(
         def words_of(dram):
             return dram[0].rearrange("p n t -> p (n t)").bitcast(I32)
 
-        def load_scale_rows(queue, tile, shift, dram):
-            for q in range(P // QUADRANT):
+        def load_scale_rows(queue, tile, shift, dram, quadrants=range(P // QUADRANT)):
+            for q in quadrants:
                 queue.dma_start(
                     out=tile[QUADRANT * q + shift : QUADRANT * q + shift + SCALE_ROWS, :].bitcast(I32),
                     in_=dram[0, SCALE_ROWS * q : SCALE_ROWS * (q + 1), :].bitcast(I32),
@@ -68,18 +67,19 @@ def tile_picked_ngcf8_relu_po_kernel(
         w1_raw = reuse.tile([P, PACK, H], F32, name="w1_raw", align_bytes=64, offset=0)
         w_raw = [keep.tile([P, H], I32, name=f"w_raw{i}", align_bytes=64) for i in range(3)]
         w2_scales_raw = keep.tile([P, H], U8, name="w2_scales_raw", align_bytes=64)
-        w34_scales_raw = keep.tile([P, H], U8, name="w34_scales_raw", align_bytes=64)
+        w34_scales_raw = reuse.tile([P, H], U8, name="w34_scales_raw", align_bytes=64, offset=12288)
 
-        nc.vector.memset(x_scale_table[:].bitcast(I32), 0)
+        nc.gpsimd.memset(x_scale_table[:].bitcast(I32), 0)
         nc.vector.memset(w2_scales_raw[:].bitcast(I32), 0)
         nc.vector.memset(w34_scales_raw[:].bitcast(I32), 0)
 
-        nc.sync.dma_start(offs_sb[:], offs)
         nc.sync.dma_start(out=w1_raw[:], in_=w1.rearrange("(p j) c -> p j c", j=PACK))
-        load_scale_rows(nc.scalar, x_scale_table, 0, x_scales)
+        nc.sync.dma_start(offs_sb[:], offs)
+        load_scale_rows(nc.scalar, x_scale_table, 0, x_scales, range(2))
+        load_scale_rows(nc.sync, x_scale_table, 0, x_scales, range(2, 4))
+        nc.sync.dma_start(out=x_table[:].bitcast(I32), in_=words_of(x_words))
         nc.sync.dma_start(p1_sb[:], p1)
         nc.sync.dma_start(p2_sb[:], p2)
-        nc.sync.dma_start(out=x_table[:].bitcast(I32), in_=words_of(x_words))
         nc.sync.dma_start(out=w_raw[W2][:], in_=words_of(w2_words))
         load_scale_rows(nc.sync, w2_scales_raw, 0, w2_scales)
         nc.sync.dma_start(out=w_raw[W3][:], in_=words_of(w3_words))
@@ -87,23 +87,21 @@ def tile_picked_ngcf8_relu_po_kernel(
         for i, scales in enumerate((w3_scales, w4_scales)):
             load_scale_rows(nc.sync, w34_scales_raw, SCALE_ROWS * i, scales)
 
-        w1_bf = [keep.tile([P, 2, P, PACK], BF16, name=f"w1_bf{u}", tag=f"w1_bf{u}", align_bytes=64) for u in range(2)]
+        w1_bf = keep.tile([P, PACK, P, PACK], BF16, name="w1_bf", align_bytes=64)
 
-        def w1_part(u, lo, hi):
+        def w1_part(u):
             return (
-                w1_bf[u][:, :, lo:hi, :].rearrange("p e m j -> p m j e"),
-                w1_raw[:, :, PACK * lo : PACK * hi].rearrange("p j (m t) -> p m j t", t=PACK)[:, :, :, 2 * u : 2 * u + 2],
+                w1_bf[:, 2 * u : 2 * u + 2].rearrange("p e m j -> p m j e"),
+                w1_raw[:].rearrange("p j (m t) -> p m j t", t=PACK)[:, :, :, 2 * u : 2 * u + 2],
             )
 
-        for u in range(2):
-            nc.vector.tensor_copy(*w1_part(u, 0, W1_SPLIT))
-            nc.scalar.activation(*w1_part(u, W1_SPLIT, P), COPY)
+        nc.vector.tensor_copy(*w1_part(0))
+        nc.scalar.activation(*w1_part(1), COPY)
+        x_scale_picked = keep.tile([P, S], U8, name="x_scale_picked", align_bytes=64)
+        nc.vector.tensor_copy(out=x_scale_picked[:], in_=x_scale_table[:].indirect(offs_sb[:]))
         w1_codes = keep.tile([P, H], U32, name="w1_codes", align_bytes=64)
         w1_scales = keep.tile([P, H], U8, name="w1_scales", align_bytes=64)
-        for u in range(2):
-            nc.vector.quantize_mx(out=w1_codes[:, half_cols(u)].bitcast(FP8X4), scales=w1_scales[:, half_cols(u)], in_=w1_bf[u][:].rearrange("p e m j -> p (e m j)"))
-        x_scale_picked = keep.tile([P, S], U8, name="x_scale_picked", tag="w1_bf0", align_bytes=64)
-        nc.vector.tensor_copy(out=x_scale_picked[:], in_=x_scale_table[:].indirect(offs_sb[:]))
+        nc.vector.quantize_mx(out=w1_codes[:].bitcast(FP8X4), scales=w1_scales[:], in_=w1_bf[:].rearrange("p t m j -> p (t m j)"))
         x_picked = keep.tile([P, S], U32, name="x_picked", align_bytes=64)
         for cols in (block_cols(0), block_cols(1), half_cols(1)):
             nc.vector.tensor_copy(out=x_picked[:, cols], in_=x_table[:].indirect(entries(offs_sb, cols)))
@@ -121,8 +119,7 @@ def tile_picked_ngcf8_relu_po_kernel(
 
         def deal(engine, key, raw, dtype, pool, **place):
             dealt[key] = pool.tile([P, H], dtype, name=f"dealt_{key}", align_bytes=64, **place)
-            copy, order = (nc.scalar.copy, "p m t") if engine is nc.scalar else (nc.gpsimd.tensor_copy, "p t m")
-            copy(out=dealt[key][:].rearrange(f"p (t m) -> {order}", t=PACK), in_=raw.rearrange(f"p (m t) -> {order}", t=PACK))
+            engine.tensor_copy(out=dealt[key][:].rearrange("p (t m) -> p t m", t=PACK), in_=raw.rearrange("p (m t) -> p t m", t=PACK))
 
         def weight(i, t):
             cols = block_cols(t)
@@ -138,8 +135,9 @@ def tile_picked_ngcf8_relu_po_kernel(
             if t == 2:
                 times_x(y_part[3, 0][:, block_cols(1)], w1_plane(3), block_cols(1))
             times_x(y_part[t, 1][:], w1_plane(t), half_cols(1))
-        deal(nc.scalar, W2, w_raw[W2][:].bitcast(U32), U32, keep)
+        deal(nc.gpsimd, W2, w_raw[W2][:], I32, keep)
         deal(nc.gpsimd, "s2", w2_scales_raw[:], U8, keep)
+        deal(nc.gpsimd, W3, w_raw[W3][:], I32, keep, tag="w2_scales_raw")
         y_window = [keep.tile([P, S], F32, name=f"y_window{t}") for t in range(PACK)]
         for h in range(2):
             nc.scalar.copy(out=y_window[0][:, half_cols(h)], in_=y_part[0, h][:])
@@ -149,20 +147,22 @@ def tile_picked_ngcf8_relu_po_kernel(
         h1 = keep.tile([P, PACK, HALF], F32, name="h1", align_bytes=64)
         h_sum = keep.tile([P, PACK, HALF], F32, name="h_sum", align_bytes=64)
 
-        def fetch(out, t, lists, h):
-            nc.scalar.activation(out, y_window[t][:].indirect(entries(lists, half_cols(h))), COPY)
+        def fetch(out, t, lists, cols):
+            nc.scalar.activation(out, y_window[t][:].indirect(entries(lists, cols)), COPY)
 
         first_h1 = [h1[:, 0, :], h1[:, 1, :], h1[:, 2, :], w1_raw[:, 0, :HALF]]
         for t in range(PACK):
-            fetch(first_h1[t], t, p1_sb, 0)
+            fetch(first_h1[t], t, p1_sb, half_cols(0))
         for t in range(PACK - 1):
             nc.vector.tensor_tensor(h_sum[:, t, :], y_window[t][:].indirect(entries(p2_sb, half_cols(0))), first_h1[t], ADD)
         for b in range(2):
             offsets = entries(p2_sb, block_cols(b))
             nc.vector.tensor_tensor(h_sum[:, 3, block_cols(b)], y_window[3][:].indirect(offsets), first_h1[3][:, block_cols(b)], ADD)
-        deal(nc.gpsimd, W3, w_raw[W3][:], I32, reuse, offset=6144)
         deal(nc.gpsimd, "s34", w34_scales_raw[:], U8, reuse, offset=0)
-        h2 = reuse.tile([P, PACK - 1, HALF], F32, name="h2", align_bytes=64, offset=1024)
+        deal(nc.gpsimd, W4, w_raw[W4][:], I32, reuse, offset=12544)
+        late = reuse.tile([P, PACK, HALF], F32, name="late", align_bytes=64, offset=8448)
+        h2 = late[:, : PACK - 1, :]
+        sums = [h_sum[:, :, block_cols(0)], h_sum[:, :, block_cols(1)], h_sum[:, :, block_cols(0)], late[:, :, block_cols(0)]]
 
         side = {}
 
@@ -175,10 +175,11 @@ def tile_picked_ngcf8_relu_po_kernel(
         side_products(0)
         side_products(1)
 
-        for out, lists in ((h1, p1_sb), (h2, p2_sb)):
-            for t in range(out.shape[1]):
-                fetch(out[:, t, :], t, lists, 1)
-        deal(nc.scalar, W4, w_raw[W4][:].bitcast(U32), U32, reuse, offset=4096)
+        for t in range(PACK):
+            fetch(h1[:, t, :], t, p1_sb, half_cols(1))
+        for b in range(2):
+            for t in range(PACK - 1):
+                fetch(h2[:, t, block_cols(b)], t, p2_sb, block_cols(2 + b))
 
         z_bf = [keep.tile([P, 2, BLK, PACK], BF16, name=f"z_bf{b}", align_bytes=64) for b in range(LAST)]
 
@@ -188,10 +189,9 @@ def tile_picked_ngcf8_relu_po_kernel(
         flat = "p j t -> p (j t)"
 
         def mix(b, which):
-            inner = b % 2
             nc.vector.tensor_tensor(
                 z_values(b, which).rearrange("p (c i) t -> p c t i", i=LINE),
-                h_sum[:, :, block_cols(inner)].rearrange(by_lines, i=LINE),
+                sums[b].rearrange(by_lines, i=LINE),
                 side[b, which][:].rearrange(by_lines, i=LINE),
                 MULT if which == Z2 else ADD,
             )
@@ -226,7 +226,6 @@ def tile_picked_ngcf8_relu_po_kernel(
         early_f32 = keep.tile([P, PACK, HALF], F32, name="early_f32")
         early_bf = keep.tile([P, LAST * BLK, PACK], BF16, name="early_bf", tag="early_bf", align_bytes=64)
         last_bf = keep.tile([P, BLK, PACK], BF16, name="last_bf", align_bytes=64)
-        out_codes = keep.tile([P, S], U32, name="out_codes", align_bytes=64)
 
         def quantise_out(values, cols):
             nc.vector.quantize_mx(out=out_codes[:, cols].bitcast(FP8X4), scales=out_scales[:, cols], in_=values.rearrange(flat))
@@ -239,10 +238,18 @@ def tile_picked_ngcf8_relu_po_kernel(
             mix(b, Z2)
             side_products(2 + b)
         quantise(0, (Z, Z2))
-        nc.vector.tensor_tensor(h_sum[:, 3, :], y_window[3][:].indirect(entries(p2_sb, half_cols(1))), h1[:, 3, :], ADD)
+
+        def fetch_and_add_last_plane(b):
+            nc.vector.tensor_tensor(sums[b][:, 3], y_window[3][:].indirect(entries(p2_sb, block_cols(b))), h1[:, 3, block_cols(b - 2)], ADD)
+
+        def add_pairs(engine, b):
+            engine.tensor_tensor(sums[b][:, :3], h1[:, :3, block_cols(b - 2)], h2[:, :, block_cols(b - 2)], ADD)
+
+        fetch_and_add_last_plane(2)
+        add_pairs(nc.vector, 2)
+        fetch_and_add_last_plane(3)
         quantise(1, (Z, Z2))
-        for b in range(2):
-            nc.vector.tensor_tensor(h_sum[:, :3, block_cols(b)], h1[:, :3, block_cols(b)], h2[:, :, block_cols(b)], ADD)
+        add_pairs(nc.gpsimd, 3)
         for b in range(2):
             nc.scalar.activation(early_f32[:, :, block_cols(b)], o_bank[b][0][:], RELU)
             nc.scalar.activation(early_bf[:, block_cols(b), :], o_bank[b][0][:].rearrange("p t j -> p j t"), RELU)
@@ -259,6 +266,7 @@ def tile_picked_ngcf8_relu_po_kernel(
         mix(3, Z2)
         quantise(3, (Z,))
         quantise(3, (Z2,))
+        out_codes = keep.tile([P, S], U32, name="out_codes", tag="z_bf2", align_bytes=64)
         quantise_out(early_bf[:, half_cols(0), :], half_cols(0))
         quantise_out(early_bf[:, block_cols(2), :], block_cols(2))
         store_words(slice(0, LAST * BLK))

@@ -65,7 +65,9 @@ def tile_picked_ngcf8_relu_po_kernel(
         x_table = keep.tile([P, T], U32, name="x_table", align_bytes=64)
         x_scale_table = keep.tile([P, T], U8, name="x_scale_table", align_bytes=64)
         w1_raw = reuse.tile([P, PACK, H], F32, name="w1_raw", align_bytes=64, offset=0)
-        w_raw = [keep.tile([P, H], I32, name=f"w_raw{i}", align_bytes=64) for i in range(3)]
+        w_raw = {i: keep.tile([P, H], I32, name=f"w_raw{i}", align_bytes=64)[:] for i in (W2, W4)}
+        w3_raw = reuse.tile([P, PACK * S], I32, name="w3_raw", align_bytes=64, offset=16384)
+        w_raw = [w_raw[W2], w3_raw[:, :H], w_raw[W4]]
         w2_scales_raw = keep.tile([P, H], U8, name="w2_scales_raw", align_bytes=64)
         w34_scales_raw = reuse.tile([P, H], U8, name="w34_scales_raw", align_bytes=64, offset=12288)
 
@@ -80,10 +82,10 @@ def tile_picked_ngcf8_relu_po_kernel(
         nc.sync.dma_start(out=x_table[:].bitcast(I32), in_=words_of(x_words))
         nc.sync.dma_start(p1_sb[:], p1)
         nc.sync.dma_start(p2_sb[:], p2)
-        nc.sync.dma_start(out=w_raw[W2][:], in_=words_of(w2_words))
+        nc.sync.dma_start(out=w_raw[W2], in_=words_of(w2_words))
+        nc.sync.dma_start(out=w_raw[W3], in_=words_of(w3_words))
         load_scale_rows(nc.sync, w2_scales_raw, 0, w2_scales)
-        nc.sync.dma_start(out=w_raw[W3][:], in_=words_of(w3_words))
-        nc.sync.dma_start(out=w_raw[W4][:], in_=words_of(w4_words))
+        nc.sync.dma_start(out=w_raw[W4], in_=words_of(w4_words))
         for i, scales in enumerate((w3_scales, w4_scales)):
             load_scale_rows(nc.sync, w34_scales_raw, SCALE_ROWS * i, scales)
 
@@ -119,7 +121,8 @@ def tile_picked_ngcf8_relu_po_kernel(
 
         def deal(engine, key, raw, dtype, pool, **place):
             dealt[key] = pool.tile([P, H], dtype, name=f"dealt_{key}", align_bytes=64, **place)
-            engine.tensor_copy(out=dealt[key][:].rearrange("p (t m) -> p t m", t=PACK), in_=raw.rearrange("p (m t) -> p t m", t=PACK))
+            copy, order = (nc.scalar.copy, "p m t") if engine is nc.scalar else (nc.gpsimd.tensor_copy, "p t m")
+            copy(out=dealt[key][:].rearrange(f"p (t m) -> {order}", t=PACK), in_=raw.rearrange(f"p (m t) -> {order}", t=PACK))
 
         def weight(i, t):
             cols = block_cols(t)
@@ -135,10 +138,10 @@ def tile_picked_ngcf8_relu_po_kernel(
             if t == 2:
                 times_x(y_part[3, 0][:, block_cols(1)], w1_plane(3), block_cols(1))
             times_x(y_part[t, 1][:], w1_plane(t), half_cols(1))
-        deal(nc.gpsimd, W2, w_raw[W2][:], I32, keep)
+        for i in (W2, W3):
+            deal(nc.scalar, i, w_raw[i].bitcast(U32), U32, keep)
         deal(nc.gpsimd, "s2", w2_scales_raw[:], U8, keep)
-        deal(nc.gpsimd, W3, w_raw[W3][:], I32, keep, tag="w2_scales_raw")
-        y_window = [keep.tile([P, S], F32, name=f"y_window{t}") for t in range(PACK)]
+        y_window = [reuse.tile([P, S], F32, name=f"y_window{t}", align_bytes=64, offset=16384 + 2048 * t) for t in range(PACK)]
         for h in range(2):
             nc.scalar.copy(out=y_window[0][:, half_cols(h)], in_=y_part[0, h][:])
         for t, h in ((1, 0), (2, 0), (1, 1), (3, 0), (2, 1), (3, 1)):
@@ -159,7 +162,7 @@ def tile_picked_ngcf8_relu_po_kernel(
             offsets = entries(p2_sb, block_cols(b))
             nc.vector.tensor_tensor(h_sum[:, 3, block_cols(b)], y_window[3][:].indirect(offsets), first_h1[3][:, block_cols(b)], ADD)
         deal(nc.gpsimd, "s34", w34_scales_raw[:], U8, reuse, offset=0)
-        deal(nc.gpsimd, W4, w_raw[W4][:], I32, reuse, offset=12544)
+        deal(nc.gpsimd, W4, w_raw[W4], I32, reuse, offset=12544)
         late = reuse.tile([P, PACK, HALF], F32, name="late", align_bytes=64, offset=8448)
         h2 = late[:, : PACK - 1, :]
         sums = [h_sum[:, :, block_cols(0)], h_sum[:, :, block_cols(1)], h_sum[:, :, block_cols(0)], late[:, :, block_cols(0)]]

@@ -43,8 +43,8 @@ def tile_picked_ngcf8_relu_po_kernel(
         def words_of(dram):
             return dram[0].rearrange("p n t -> p (n t)").bitcast(I32)
 
-        def load_scale_rows(queue, tile, shift, dram, quadrants=range(P // QUADRANT)):
-            for q in quadrants:
+        def load_scale_rows(queue, tile, shift, dram):
+            for q in range(P // QUADRANT):
                 queue.dma_start(
                     out=tile[QUADRANT * q + shift : QUADRANT * q + shift + SCALE_ROWS, :].bitcast(I32),
                     in_=dram[0, SCALE_ROWS * q : SCALE_ROWS * (q + 1), :].bitcast(I32),
@@ -77,8 +77,7 @@ def tile_picked_ngcf8_relu_po_kernel(
 
         nc.sync.dma_start(out=w1_raw[:], in_=w1.rearrange("(p j) c -> p j c", j=PACK))
         nc.sync.dma_start(offs_sb[:], offs)
-        load_scale_rows(nc.scalar, x_scale_table, 0, x_scales, range(2))
-        load_scale_rows(nc.sync, x_scale_table, 0, x_scales, range(2, 4))
+        load_scale_rows(nc.sync, x_scale_table, 0, x_scales)
         nc.sync.dma_start(out=x_table[:].bitcast(I32), in_=words_of(x_words))
         nc.sync.dma_start(p1_sb[:], p1)
         nc.sync.dma_start(p2_sb[:], p2)
@@ -101,7 +100,7 @@ def tile_picked_ngcf8_relu_po_kernel(
         nc.scalar.activation(*w1_part(1), COPY)
         x_scale_picked = keep.tile([P, S], U8, name="x_scale_picked", align_bytes=64)
         nc.vector.tensor_copy(out=x_scale_picked[:], in_=x_scale_table[:].indirect(offs_sb[:]))
-        w1_codes = keep.tile([P, H], U32, name="w1_codes", align_bytes=64)
+        w1_codes = keep.tile([P, H], U32, name="w1_codes", tag="x_scale_table", align_bytes=64)
         w1_scales = keep.tile([P, H], U8, name="w1_scales", align_bytes=64)
         nc.vector.quantize_mx(out=w1_codes[:].bitcast(FP8X4), scales=w1_scales[:], in_=w1_bf[:].rearrange("p t m j -> p (t m j)"))
         x_picked = keep.tile([P, S], U32, name="x_picked", align_bytes=64)

@@ -177,11 +177,15 @@ def tile_picked_ngcf8_relu_po_kernel(
         side_products(0)
         side_products(1)
 
-        for t in range(PACK):
+        for t in range(PACK - 1):
             fetch(h1[:, t, :], t, p1_sb, half_cols(1))
-        for b in range(2):
-            for t in range(PACK - 1):
-                fetch(h2[:, t, block_cols(b)], t, p2_sb, block_cols(2 + b))
+        last_plane_h1 = {2: h1[:, 3, block_cols(0)], 3: late[:, 3, block_cols(1)]}
+        fetch(last_plane_h1[2], 3, p1_sb, block_cols(2))
+        for t in range(PACK - 1):
+            fetch(h2[:, t, block_cols(0)], t, p2_sb, block_cols(2))
+        fetch(last_plane_h1[3], 3, p1_sb, block_cols(3))
+        for t in range(PACK - 1):
+            fetch(h2[:, t, block_cols(1)], t, p2_sb, block_cols(3))
 
         z_bf = [keep.tile([P, 2, BLK, PACK], BF16, name=f"z_bf{b}", align_bytes=64) for b in range(LAST)]
 
@@ -242,15 +246,15 @@ def tile_picked_ngcf8_relu_po_kernel(
         quantise(0, (Z, Z2))
 
         def fetch_and_add_last_plane(b):
-            nc.vector.tensor_tensor(sums[b][:, 3], y_window[3][:].indirect(entries(p2_sb, block_cols(b))), h1[:, 3, block_cols(b - 2)], ADD)
+            nc.vector.tensor_tensor(sums[b][:, 3], y_window[3][:].indirect(entries(p2_sb, block_cols(b))), last_plane_h1[b], ADD)
 
         def add_pairs(engine, b):
             engine.tensor_tensor(sums[b][:, :3], h1[:, :3, block_cols(b - 2)], h2[:, :, block_cols(b - 2)], ADD)
 
         fetch_and_add_last_plane(2)
+        quantise(1, (Z, Z2))
         add_pairs(nc.vector, 2)
         fetch_and_add_last_plane(3)
-        quantise(1, (Z, Z2))
         add_pairs(nc.gpsimd, 3)
         for b in range(2):
             nc.scalar.activation(early_f32[:, :, block_cols(b)], o_bank[b][0][:], RELU)

@@ -27,6 +27,7 @@ BLK = 128
 BLOCKS = S // BLK
 LAST = BLOCKS - 1
 LINE = 2
+W1_SPLIT = 88
 W2, W3, W4 = 0, 1, 2
 Z, Z2 = 0, 1
 
@@ -90,14 +91,15 @@ def tile_picked_ngcf8_relu_po_kernel(
 
         w1_bf = keep.tile([P, PACK, P, PACK], BF16, name="w1_bf", align_bytes=64)
 
-        def w1_part(u):
+        def w1_part(u, m):
             return (
-                w1_bf[:, 2 * u : 2 * u + 2].rearrange("p e m j -> p m j e"),
-                w1_raw[:].rearrange("p j (m t) -> p m j t", t=PACK)[:, :, :, 2 * u : 2 * u + 2],
+                w1_bf[:, 2 * u : 2 * u + 2, m].rearrange("p e m j -> p m j e"),
+                w1_raw[:].rearrange("p j (m t) -> p m j t", t=PACK)[:, m, :, 2 * u : 2 * u + 2],
             )
 
-        nc.vector.tensor_copy(*w1_part(0))
-        nc.scalar.activation(*w1_part(1), COPY)
+        nc.vector.tensor_copy(*w1_part(0, slice(0, W1_SPLIT)))
+        nc.scalar.activation(*w1_part(1, slice(0, P)), COPY)
+        nc.scalar.activation(*w1_part(0, slice(W1_SPLIT, P)), COPY)
         x_scale_picked = keep.tile([P, S], U8, name="x_scale_picked", align_bytes=64)
         nc.vector.tensor_copy(out=x_scale_picked[:], in_=x_scale_table[:].indirect(offs_sb[:]))
         w1_codes = keep.tile([P, H], U32, name="w1_codes", tag="x_scale_table", align_bytes=64)
@@ -187,10 +189,12 @@ def tile_picked_ngcf8_relu_po_kernel(
         for t in range(PACK - 1):
             fetch(h2[:, t, block_cols(1)], t, p2_sb, block_cols(3))
 
-        z_bf = [keep.tile([P, 2, BLK, PACK], BF16, name=f"z_bf{b}", align_bytes=64) for b in range(LAST)]
+        z_bf = [keep.tile([P, 2, BLK, PACK], BF16, name=f"z_bf{b}", align_bytes=64) for b in range(2)]
+        late_z = reuse.tile([P, 5, BLK, PACK], BF16, name="late_z", align_bytes=64, offset=24576)
+        late_z2 = keep.tile([P, BLK, PACK], BF16, name="late_z2", align_bytes=64)
 
         def z_values(b, which):
-            return z_bf[min(b, LAST - 1)][:, which]
+            return z_bf[b][:, which] if b < 2 else (late_z[:, 0], late_z2[:])[which]
         by_lines = "p t (c i) -> p c t i"
         flat = "p j t -> p (j t)"
 
@@ -230,7 +234,7 @@ def tile_picked_ngcf8_relu_po_kernel(
                     )
 
         early_f32 = keep.tile([P, PACK, HALF], F32, name="early_f32")
-        early_bf = keep.tile([P, LAST * BLK, PACK], BF16, name="early_bf", tag="early_bf", align_bytes=64)
+        early_bf = keep.tile([P, HALF, PACK], BF16, name="early_bf", tag="early_bf", align_bytes=64)
         last_bf = keep.tile([P, BLK, PACK], BF16, name="last_bf", align_bytes=64)
 
         def quantise_out(values, cols):
@@ -266,25 +270,26 @@ def tile_picked_ngcf8_relu_po_kernel(
         quantise(2, (Z2,))
         mix(3, Z)
         third_f32 = keep.tile([P, PACK, BLK], F32, name="third_f32")
-        nc.scalar.activation(early_bf[:, block_cols(2), :], o_bank[2][0][:].rearrange("p t j -> p j t"), RELU)
         nc.scalar.activation(third_f32[:], o_bank[2][0][:], RELU)
         nc.sync.dma_start(out=out_rows[:, :, block_cols(2)], in_=third_f32[:])
         mix(3, Z2)
         quantise(3, (Z,))
         quantise(3, (Z2,))
-        out_codes = keep.tile([P, S], U32, name="out_codes", tag="z_bf2", align_bytes=64)
-        quantise_out(early_bf[:, half_cols(0), :], half_cols(0))
-        quantise_out(early_bf[:, block_cols(2), :], block_cols(2))
-        store_words(slice(0, LAST * BLK))
+        out_codes = reuse.tile([P, S], U32, name="out_codes", align_bytes=64, offset=24576)
+        third_bf = reuse.tile([P, BLK, PACK], BF16, name="third_bf", align_bytes=64, offset=24576 + 2048)
+        quantise_out(early_bf[:], half_cols(0))
+        store_words(half_cols(0))
+        nc.vector.tensor_copy(out=third_bf[:].rearrange("p (c i) t -> p c t i", i=PACK), in_=third_f32[:].rearrange(by_lines, i=PACK))
         low, high = o_bank[LAST]
-        last_f32 = keep.tile([P, PACK, BLK], F32, name="last_f32", tag="early_bf", align_bytes=64)
+        last_f32 = reuse.tile([P, PACK, BLK], F32, name="last_f32", align_bytes=64, offset=24576 + 3072)
         nc.scalar.activation(last_f32[:, :2, :], low[:], RELU)
         nc.vector.tensor_scalar_max(last_f32[:, 2:, :], high[:], 0.0)
         nc.sync.dma_start(out=out_rows[:, :, block_cols(LAST)], in_=last_f32[:])
         nc.scalar.activation(last_bf[:, :, :2], low[:].rearrange("p e j -> p j e"), RELU)
         nc.vector.tensor_scalar_max(last_bf[:, :, 2:], high[:].rearrange("p e j -> p j e"), 0.0)
+        quantise_out(third_bf[:], block_cols(2))
         quantise_out(last_bf[:], block_cols(LAST))
-        store_words(block_cols(LAST))
+        store_words(half_cols(1))
 
         for q, queue in enumerate((nc.sync, nc.scalar, nc.sync, nc.scalar)):
             queue.dma_start(

@@ -66,11 +66,10 @@ def tile_picked_ngcf8_relu_po_kernel(
         x_table = keep.tile([P, T], U32, name="x_table", align_bytes=64)
         x_scale_table = keep.tile([P, T], U8, name="x_scale_table", align_bytes=64)
         w1_raw = reuse.tile([P, PACK, H], F32, name="w1_raw", align_bytes=64, offset=0)
-        w_raw = {i: keep.tile([P, H], I32, name=f"w_raw{i}", align_bytes=64)[:] for i in (W2, W4)}
-        w3_raw = reuse.tile([P, PACK * S], I32, name="w3_raw", align_bytes=64, offset=16384)
-        w_raw = [w_raw[W2], w3_raw[:, :H], w_raw[W4]]
+        w2_raw = reuse.tile([P, PACK * S], I32, name="w2_raw", align_bytes=64, offset=16384)
+        w_raw = [w2_raw[:, :H]] + [keep.tile([P, H], I32, name=f"w_raw{i}", align_bytes=64)[:] for i in (W3, W4)]
         w2_scales_raw = keep.tile([P, H], U8, name="w2_scales_raw", align_bytes=64)
-        w34_scales_raw = reuse.tile([P, H], U8, name="w34_scales_raw", align_bytes=64, offset=12288)
+        w34_scales_raw = reuse.tile([P, 6656], U8, name="w34_scales_raw", align_bytes=64, offset=8448)[:, :H]
 
         nc.gpsimd.memset(x_scale_table[:].bitcast(I32), 0)
         nc.vector.memset(w2_scales_raw[:].bitcast(I32), 0)
@@ -131,16 +130,16 @@ def tile_picked_ngcf8_relu_po_kernel(
             return dict(lhsT=dealt[i][:, cols].bitcast(FP8X4), lhsT_scale=scales[:, cols])
 
         y_part = {(t, h): bank(PACK * h + t, [HALF], f"y_part{t}{h}") for h in range(2) for t in range(PACK)}
-        for t in range(PACK):
-            times_x(y_part[t, 0][:, block_cols(0)], w1_plane(t), block_cols(0))
-        for t in range(PACK - 1):
-            times_x(y_part[t, 0][:, block_cols(1)], w1_plane(t), block_cols(1))
+        for b in range(2):
+            for t in (1, 2, 0):
+                times_x(y_part[t, 0][:, block_cols(b)], w1_plane(t), block_cols(b))
         for t in range(PACK):
             if t == 2:
-                times_x(y_part[3, 0][:, block_cols(1)], w1_plane(3), block_cols(1))
+                for b in range(2):
+                    times_x(y_part[3, 0][:, block_cols(b)], w1_plane(3), block_cols(b))
             times_x(y_part[t, 1][:], w1_plane(t), half_cols(1))
-        for i in (W2, W3):
-            deal(nc.scalar, i, w_raw[i].bitcast(U32), U32, keep)
+        deal(nc.scalar, W2, w_raw[W2].bitcast(U32), U32, keep)
+        deal(nc.gpsimd, W3, w_raw[W3], I32, keep)
         deal(nc.gpsimd, "s2", w2_scales_raw[:], U8, keep)
         y_window = [reuse.tile([P, S], F32, name=f"y_window{t}", align_bytes=64, offset=16384 + 2048 * t) for t in range(PACK)]
         for h in range(2):
@@ -154,19 +153,25 @@ def tile_picked_ngcf8_relu_po_kernel(
         def fetch(out, t, lists, cols):
             nc.scalar.activation(out, y_window[t][:].indirect(entries(lists, cols)), COPY)
 
-        first_h1 = [h1[:, 0, :], h1[:, 1, :], h1[:, 2, :], w1_raw[:, 0, :HALF]]
-        for t in range(PACK):
-            fetch(first_h1[t], t, p1_sb, half_cols(0))
+        plane3_h1 = [w1_raw[:, 0, :BLK], h1[:, 3, block_cols(1)]]
         for t in range(PACK - 1):
-            nc.vector.tensor_tensor(h_sum[:, t, :], y_window[t][:].indirect(entries(p2_sb, half_cols(0))), first_h1[t], ADD)
+            fetch(h1[:, t, :], t, p1_sb, half_cols(0))
+        for b in range(2):
+            fetch(plane3_h1[b], 3, p1_sb, block_cols(b))
+        for t in range(PACK - 1):
+            nc.vector.tensor_tensor(h_sum[:, t, :], y_window[t][:].indirect(entries(p2_sb, half_cols(0))), h1[:, t, :], ADD)
         for b in range(2):
             offsets = entries(p2_sb, block_cols(b))
-            nc.vector.tensor_tensor(h_sum[:, 3, block_cols(b)], y_window[3][:].indirect(offsets), first_h1[3][:, block_cols(b)], ADD)
+            nc.vector.tensor_tensor(h_sum[:, 3, block_cols(b)], y_window[3][:].indirect(offsets), plane3_h1[b], ADD)
         deal(nc.gpsimd, "s34", w34_scales_raw[:], U8, reuse, offset=0)
-        deal(nc.gpsimd, W4, w_raw[W4], I32, reuse, offset=12544)
-        late = reuse.tile([P, PACK, HALF], F32, name="late", align_bytes=64, offset=8448)
-        h2 = late[:, : PACK - 1, :]
-        sums = [h_sum[:, :, block_cols(0)], h_sum[:, :, block_cols(1)], h_sum[:, :, block_cols(0)], late[:, :, block_cols(0)]]
+        deal(nc.gpsimd, W4, w_raw[W4], I32, reuse, offset=8960)
+        late = reuse.tile([P, PACK, BLK], F32, name="late", align_bytes=64, offset=512)
+        third_h2 = late[:, : PACK - 1, :]
+        last_h1 = reuse.tile([P, BLK], F32, name="last_h1", align_bytes=64, offset=13056)
+        last_h2 = reuse.tile([P, PACK - 1, BLK], F32, name="last_h2", align_bytes=64, offset=13568)
+        h2 = {2: third_h2, 3: last_h2[:]}
+        third_sum = reuse.tile([P, PACK, BLK], F32, name="third_sum", align_bytes=64, offset=11008)
+        sums = [h_sum[:, :, block_cols(0)], h_sum[:, :, block_cols(1)], third_sum[:], late[:]]
 
         side = {}
 
@@ -181,13 +186,13 @@ def tile_picked_ngcf8_relu_po_kernel(
 
         for t in range(PACK - 1):
             fetch(h1[:, t, :], t, p1_sb, half_cols(1))
-        last_plane_h1 = {2: h1[:, 3, block_cols(0)], 3: late[:, 3, block_cols(1)]}
+        last_plane_h1 = {2: h1[:, 3, block_cols(0)], 3: last_h1[:]}
         fetch(last_plane_h1[2], 3, p1_sb, block_cols(2))
         for t in range(PACK - 1):
-            fetch(h2[:, t, block_cols(0)], t, p2_sb, block_cols(2))
+            fetch(h2[2][:, t, :], t, p2_sb, block_cols(2))
         fetch(last_plane_h1[3], 3, p1_sb, block_cols(3))
         for t in range(PACK - 1):
-            fetch(h2[:, t, block_cols(1)], t, p2_sb, block_cols(3))
+            fetch(h2[3][:, t, :], t, p2_sb, block_cols(3))
 
         z_bf = [keep.tile([P, 2, BLK, PACK], BF16, name=f"z_bf{b}", align_bytes=64) for b in range(2)]
         late_z = reuse.tile([P, 5, BLK, PACK], BF16, name="late_z", align_bytes=64, offset=24576)
@@ -253,10 +258,10 @@ def tile_picked_ngcf8_relu_po_kernel(
             nc.vector.tensor_tensor(sums[b][:, 3], y_window[3][:].indirect(entries(p2_sb, block_cols(b))), last_plane_h1[b], ADD)
 
         def add_pairs(engine, b):
-            engine.tensor_tensor(sums[b][:, :3], h1[:, :3, block_cols(b - 2)], h2[:, :, block_cols(b - 2)], ADD)
+            engine.tensor_tensor(sums[b][:, :3], h1[:, :3, block_cols(b - 2)], h2[b], ADD)
 
-        fetch_and_add_last_plane(2)
         quantise(1, (Z, Z2))
+        fetch_and_add_last_plane(2)
         add_pairs(nc.vector, 2)
         fetch_and_add_last_plane(3)
         add_pairs(nc.gpsimd, 3)

@@ -69,7 +69,7 @@ def tile_picked_ngcf8_relu_po_kernel(
         w2_raw = reuse.tile([P, PACK * S], I32, name="w2_raw", align_bytes=64, offset=16384)
         w_raw = [w2_raw[:, :H]] + [keep.tile([P, H], I32, name=f"w_raw{i}", align_bytes=64)[:] for i in (W3, W4)]
         w2_scales_raw = keep.tile([P, H], U8, name="w2_scales_raw", align_bytes=64)
-        w34_scales_raw = reuse.tile([P, 6656], U8, name="w34_scales_raw", align_bytes=64, offset=8448)[:, :H]
+        w34_scales_raw = reuse.tile([P, 7936], U8, name="w34_scales_raw", align_bytes=64, offset=8448)[:, :H]
 
         nc.gpsimd.memset(x_scale_table[:].bitcast(I32), 0)
         nc.vector.memset(w2_scales_raw[:].bitcast(I32), 0)
@@ -153,22 +153,21 @@ def tile_picked_ngcf8_relu_po_kernel(
         def fetch(out, t, lists, cols):
             nc.scalar.activation(out, y_window[t][:].indirect(entries(lists, cols)), COPY)
 
-        plane3_h1 = [w1_raw[:, 0, :BLK], h1[:, 3, block_cols(1)]]
-        for t in range(PACK - 1):
-            fetch(h1[:, t, :], t, p1_sb, half_cols(0))
-        for b in range(2):
-            fetch(plane3_h1[b], 3, p1_sb, block_cols(b))
+        first_h1 = [h1[:, 0, :], h1[:, 1, :], h1[:, 2, :], w1_raw[:, 0, :HALF]]
+        for t in range(PACK):
+            fetch(first_h1[t], t, p1_sb, half_cols(0))
         for t in range(PACK - 1):
             nc.vector.tensor_tensor(h_sum[:, t, :], y_window[t][:].indirect(entries(p2_sb, half_cols(0))), h1[:, t, :], ADD)
         for b in range(2):
             offsets = entries(p2_sb, block_cols(b))
-            nc.vector.tensor_tensor(h_sum[:, 3, block_cols(b)], y_window[3][:].indirect(offsets), plane3_h1[b], ADD)
+            nc.vector.tensor_tensor(h_sum[:, 3, block_cols(b)], y_window[3][:].indirect(offsets), first_h1[3][:, block_cols(b)], ADD)
         deal(nc.gpsimd, "s34", w34_scales_raw[:], U8, reuse, offset=0)
         deal(nc.gpsimd, W4, w_raw[W4], I32, reuse, offset=8960)
         late = reuse.tile([P, PACK, BLK], F32, name="late", align_bytes=64, offset=512)
         third_h2 = late[:, : PACK - 1, :]
         last_h1 = reuse.tile([P, BLK], F32, name="last_h1", align_bytes=64, offset=13056)
         last_h2 = reuse.tile([P, PACK - 1, BLK], F32, name="last_h2", align_bytes=64, offset=13568)
+        last_plane_h2 = reuse.tile([P, BLK], F32, name="last_plane_h2", align_bytes=64, offset=8448)
         h2 = {2: third_h2, 3: last_h2[:]}
         third_sum = reuse.tile([P, PACK, BLK], F32, name="third_sum", align_bytes=64, offset=11008)
         sums = [h_sum[:, :, block_cols(0)], h_sum[:, :, block_cols(1)], third_sum[:], late[:]]
@@ -190,9 +189,10 @@ def tile_picked_ngcf8_relu_po_kernel(
         fetch(last_plane_h1[2], 3, p1_sb, block_cols(2))
         for t in range(PACK - 1):
             fetch(h2[2][:, t, :], t, p2_sb, block_cols(2))
-        fetch(last_plane_h1[3], 3, p1_sb, block_cols(3))
         for t in range(PACK - 1):
             fetch(h2[3][:, t, :], t, p2_sb, block_cols(3))
+        fetch(last_plane_h1[3], 3, p1_sb, block_cols(3))
+        fetch(last_plane_h2[:], 3, p2_sb, block_cols(3))
 
         z_bf = [keep.tile([P, 2, BLK, PACK], BF16, name=f"z_bf{b}", align_bytes=64) for b in range(2)]
         late_z = reuse.tile([P, 5, BLK, PACK], BF16, name="late_z", align_bytes=64, offset=24576)
@@ -219,8 +219,12 @@ def tile_picked_ngcf8_relu_po_kernel(
 
         def quantise(b, parts):
             width = BLK * len(parts)
-            codes = keep.tile([P, width], U32, name=f"codes{b}{parts[0]}", align_bytes=64)
-            scales = keep.tile([P, width], U8, name=f"scales{b}{parts[0]}", align_bytes=64)
+            if b == 1:
+                codes = reuse.tile([P, width], U32, name="codes1", align_bytes=64, offset=15104)
+                scales = reuse.tile([P, width], U8, name="scales1", align_bytes=64, offset=16128)
+            else:
+                codes = keep.tile([P, width], U32, name=f"codes{b}{parts[0]}", align_bytes=64)
+                scales = keep.tile([P, width], U8, name=f"scales{b}{parts[0]}", align_bytes=64)
             values = z_bf[b][:].rearrange("p w j t -> p (w j t)") if len(parts) == 2 else z_values(b, parts[0]).rearrange(flat)
             nc.vector.quantize_mx(out=codes[:].bitcast(FP8X4), scales=scales[:], in_=values)
             for i, which in enumerate(parts):
@@ -260,10 +264,9 @@ def tile_picked_ngcf8_relu_po_kernel(
         def add_pairs(engine, b):
             engine.tensor_tensor(sums[b][:, :3], h1[:, :3, block_cols(b - 2)], h2[b], ADD)
 
-        quantise(1, (Z, Z2))
         fetch_and_add_last_plane(2)
         add_pairs(nc.vector, 2)
-        fetch_and_add_last_plane(3)
+        quantise(1, (Z, Z2))
         add_pairs(nc.gpsimd, 3)
         for b in range(2):
             nc.scalar.activation(early_f32[:, :, block_cols(b)], o_bank[b][0][:], RELU)
@@ -271,6 +274,7 @@ def tile_picked_ngcf8_relu_po_kernel(
         nc.sync.dma_start(out=out_rows[:, :, half_cols(0)], in_=early_f32[:])
         mix(2, Z)
         mix(2, Z2)
+        nc.vector.tensor_tensor(late[:, 3, :], last_plane_h2[:], last_h1[:], ADD)
         quantise(2, (Z,))
         quantise(2, (Z2,))
         mix(3, Z)

@@ -28,6 +28,7 @@ BLOCKS = S // BLK
 LAST = BLOCKS - 1
 LINE = 2
 W1_SPLIT = 88
+POOL_SHARE = 64
 W2, W3, W4 = 0, 1, 2
 Z, Z2 = 0, 1
 
@@ -197,9 +198,10 @@ def tile_picked_ngcf8_relu_po_kernel(
         z_bf = [keep.tile([P, 2, BLK, PACK], BF16, name=f"z_bf{b}", align_bytes=64) for b in range(2)]
         late_z = reuse.tile([P, 5, BLK, PACK], BF16, name="late_z", align_bytes=64, offset=24576)
         late_z2 = keep.tile([P, BLK, PACK], BF16, name="late_z2", align_bytes=64)
+        third_z = reuse.tile([P, BLK, PACK], BF16, name="third_z", align_bytes=64, offset=30720)
 
         def z_values(b, which):
-            return z_bf[b][:, which] if b < 2 else (late_z[:, 0], late_z2[:])[which]
+            return z_bf[b][:, which] if b < 2 else (third_z[:] if b == 2 else late_z[:, 0], late_z2[:])[which]
         by_lines = "p t (c i) -> p c t i"
         flat = "p j t -> p (j t)"
 
@@ -270,13 +272,17 @@ def tile_picked_ngcf8_relu_po_kernel(
         add_pairs(nc.gpsimd, 3)
         for b in range(2):
             nc.scalar.activation(early_f32[:, :, block_cols(b)], o_bank[b][0][:], RELU)
-            nc.scalar.activation(early_bf[:, block_cols(b), :], o_bank[b][0][:].rearrange("p t j -> p j t"), RELU)
+            skip = POOL_SHARE if b == 0 else 0
+            out = early_bf[:, b * BLK + skip : (b + 1) * BLK, :]
+            nc.scalar.activation(out, o_bank[b][0][:, :, skip:].rearrange("p t j -> p j t"), RELU)
         nc.sync.dma_start(out=out_rows[:, :, half_cols(0)], in_=early_f32[:])
         mix(2, Z)
         mix(2, Z2)
         nc.vector.tensor_tensor(late[:, 3, :], last_plane_h2[:], last_h1[:], ADD)
         quantise(2, (Z,))
         quantise(2, (Z2,))
+        first_bf = reuse.tile([P, POOL_SHARE, PACK], BF16, name="first_bf", align_bytes=64, offset=30720)
+        nc.gpsimd.tensor_copy(out=first_bf[:], in_=early_f32[:, :, :POOL_SHARE].rearrange("p t j -> p j t"))
         mix(3, Z)
         third_f32 = keep.tile([P, PACK, BLK], F32, name="third_f32")
         nc.scalar.activation(third_f32[:], o_bank[2][0][:], RELU)
@@ -286,7 +292,9 @@ def tile_picked_ngcf8_relu_po_kernel(
         quantise(3, (Z2,))
         out_codes = reuse.tile([P, S], U32, name="out_codes", align_bytes=64, offset=24576)
         third_bf = reuse.tile([P, BLK, PACK], BF16, name="third_bf", align_bytes=64, offset=24576 + 2048)
-        quantise_out(early_bf[:], half_cols(0))
+        quantise_out(early_bf[:, block_cols(1), :], block_cols(1))
+        quantise_out(early_bf[:, POOL_SHARE:BLK, :], slice(POOL_SHARE, BLK))
+        quantise_out(first_bf[:], slice(0, POOL_SHARE))
         store_words(half_cols(0))
         nc.vector.tensor_copy(out=third_bf[:].rearrange("p (c i) t -> p c t i", i=PACK), in_=third_f32[:].rearrange(by_lines, i=PACK))
         low, high = o_bank[LAST]

from contextlib import ExitStack

import concourse.mybir as mybir

K, T, S, N, H = 512, 2048, 512, 512, 512
FLOPS = 2 * S * (2 * K * H + 2 * H * N)

F32 = mybir.dt.float32
BF16 = mybir.dt.bfloat16
I32 = mybir.dt.int32
U32 = mybir.dt.uint32
U16 = mybir.dt.uint16
U8 = mybir.dt.uint8
FP8X4 = mybir.dt.float8_e4m3fn_x4
ADD = mybir.AluOpType.add
MULT = mybir.AluOpType.mult
RELU = mybir.ActivationFunctionType.Relu
COPY = mybir.ActivationFunctionType.Copy

P = 128
PACK = 4
QUADRANT = 32
SCALE_ROWS = 4
LIST_ROWS = 16
HALF = S // 2
BLK = 128
BLOCKS = S // BLK
LAST = BLOCKS - 1
LINE = 2
W1_SPLIT = 88
POOL_SHARE = 64
W2, W3, W4 = 0, 1, 2
Z, Z2 = 0, 1


def tile_picked_ngcf8_relu_po_kernel(
    tc, x_words, x_scales, w1, w2_words, w2_scales, w3_words, w3_scales, w4_words, w4_scales, offs, p1, p2, out_0, out_1, out_2
):
    nc = tc.nc
    with ExitStack() as ctx:
        keep = ctx.enter_context(tc.tile_pool(name="keep", bufs=1))
        reuse = ctx.enter_context(tc.tile_pool(name="reuse", bufs=1))
        psum = ctx.enter_context(tc.psum_pool(name="psum", bufs=1))

        def words_of(dram):
            return dram[0].rearrange("p n t -> p (n t)").bitcast(I32)

        def load_scale_rows(queue, tile, shift, dram):
            for q in range(P // QUADRANT):
                queue.dma_start(
                    out=tile[QUADRANT * q + shift : QUADRANT * q + shift + SCALE_ROWS, :].bitcast(I32),
                    in_=dram[0, SCALE_ROWS * q : SCALE_ROWS * (q + 1), :].bitcast(I32),
                )

        def block_cols(b):
            return slice(b * BLK, (b + 1) * BLK)

        def half_cols(h):
            return slice(h * HALF, (h + 1) * HALF)

        def entries(tile, cols):
            return tile[:, cols.start // LIST_ROWS : cols.stop // LIST_ROWS]

        offs_sb = keep.tile([P, S // LIST_ROWS], U16, name="offs_sb")
        p1_sb = keep.tile([P, S // LIST_ROWS], U16, name="p1_sb")
        p2_sb = keep.tile([P, S // LIST_ROWS], U16, name="p2_sb")
        x_table = keep.tile([P, T], U32, name="x_table", align_bytes=64)
        x_scale_table = keep.tile([P, T], U8, name="x_scale_table", align_bytes=64)
        w1_raw = reuse.tile([P, PACK, H], F32, name="w1_raw", align_bytes=64, offset=0)
        w2_raw = reuse.tile([P, PACK * S], I32, name="w2_raw", align_bytes=64, offset=16384)
        w_raw = [w2_raw[:, :H]] + [keep.tile([P, H], I32, name=f"w_raw{i}", align_bytes=64)[:] for i in (W3, W4)]
        w2_scales_raw = keep.tile([P, H], U8, name="w2_scales_raw", align_bytes=64)
        w34_scales_raw = reuse.tile([P, 7936], U8, name="w34_scales_raw", align_bytes=64, offset=8448)[:, :H]

        nc.gpsimd.memset(x_scale_table[:].bitcast(I32), 0)
        nc.vector.memset(w2_scales_raw[:].bitcast(I32), 0)
        nc.vector.memset(w34_scales_raw[:].bitcast(I32), 0)

        nc.sync.dma_start(out=w1_raw[:], in_=w1.rearrange("(p j) c -> p j c", j=PACK))
        nc.sync.dma_start(offs_sb[:], offs)
        load_scale_rows(nc.sync, x_scale_table, 0, x_scales)
        nc.sync.dma_start(out=x_table[:].bitcast(I32), in_=words_of(x_words))
        nc.sync.dma_start(p1_sb[:], p1)
        nc.sync.dma_start(p2_sb[:], p2)
        nc.sync.dma_start(out=w_raw[W2], in_=words_of(w2_words))
        nc.sync.dma_start(out=w_raw[W3], in_=words_of(w3_words))
        load_scale_rows(nc.sync, w2_scales_raw, 0, w2_scales)
        nc.sync.dma_start(out=w_raw[W4], in_=words_of(w4_words))
        for i, scales in enumerate((w3_scales, w4_scales)):
            load_scale_rows(nc.sync, w34_scales_raw, SCALE_ROWS * i, scales)

        w1_bf = keep.tile([P, PACK, P, PACK], BF16, name="w1_bf", align_bytes=64)

        def w1_part(u, m):
            return (
                w1_bf[:, 2 * u : 2 * u + 2, m].rearrange("p e m j -> p m j e"),
                w1_raw[:].rearrange("p j (m t) -> p m j t", t=PACK)[:, m, :, 2 * u : 2 * u + 2],
            )

        nc.vector.tensor_copy(*w1_part(0, slice(0, W1_SPLIT)))
        nc.scalar.activation(*w1_part(1, slice(0, P)), COPY)
        nc.scalar.activation(*w1_part(0, slice(W1_SPLIT, P)), COPY)
        x_scale_picked = keep.tile([P, S], U8, name="x_scale_picked", align_bytes=64)
        nc.vector.tensor_copy(out=x_scale_picked[:], in_=x_scale_table[:].indirect(offs_sb[:]))
        w1_codes = keep.tile([P, H], U32, name="w1_codes", tag="x_scale_table", align_bytes=64)
        w1_scales = keep.tile([P, H], U8, name="w1_scales", align_bytes=64)
        nc.vector.quantize_mx(out=w1_codes[:].bitcast(FP8X4), scales=w1_scales[:], in_=w1_bf[:].rearrange("p t m j -> p (t m j)"))
        x_picked = keep.tile([P, S], U32, name="x_picked", align_bytes=64)
        for cols in (block_cols(0), block_cols(1), half_cols(1)):
            nc.vector.tensor_copy(out=x_picked[:, cols], in_=x_table[:].indirect(entries(offs_sb, cols)))

        def bank(k, shape, name):
            return psum.tile([P] + shape, F32, name=name, tag=f"bank{k}")

        def times_x(out, weights, cols):
            nc.tensor.matmul_mx(out=out, **weights, rhs=x_picked[:, cols].bitcast(FP8X4), rhs_scale=x_scale_picked[:, cols], start=True, stop=True)

        def w1_plane(t):
            return dict(lhsT=w1_codes[:, block_cols(t)].bitcast(FP8X4), lhsT_scale=w1_scales[:, block_cols(t)])

        dealt = {}

        def deal(engine, key, raw, dtype, pool, **place):
            dealt[key] = pool.tile([P, H], dtype, name=f"dealt_{key}", align_bytes=64, **place)
            copy, order = (nc.scalar.copy, "p m t") if engine is nc.scalar else (nc.gpsimd.tensor_copy, "p t m")
            copy(out=dealt[key][:].rearrange(f"p (t m) -> {order}", t=PACK), in_=raw.rearrange(f"p (m t) -> {order}", t=PACK))

        def weight(i, t):
            cols = block_cols(t)
            scales = dealt["s2"][:] if i == W2 else dealt["s34"][SCALE_ROWS * (i - W3) :, :]
            return dict(lhsT=dealt[i][:, cols].bitcast(FP8X4), lhsT_scale=scales[:, cols])

        y_part = {(t, h): bank(PACK * h + t, [HALF], f"y_part{t}{h}") for h in range(2) for t in range(PACK)}
        for b in range(2):
            for t in (1, 2, 0):
                times_x(y_part[t, 0][:, block_cols(b)], w1_plane(t), block_cols(b))
        for t in range(PACK):
            if t == 2:
                for b in range(2):
                    times_x(y_part[3, 0][:, block_cols(b)], w1_plane(3), block_cols(b))
            times_x(y_part[t, 1][:], w1_plane(t), half_cols(1))
        deal(nc.scalar, W2, w_raw[W2].bitcast(U32), U32, keep)
        deal(nc.gpsimd, W3, w_raw[W3], I32, keep)
        deal(nc.gpsimd, "s2", w2_scales_raw[:], U8, keep)
        y_window = [reuse.tile([P, S], F32, name=f"y_window{t}", align_bytes=64, offset=16384 + 2048 * t) for t in range(PACK)]
        for h in range(2):
            nc.scalar.copy(out=y_window[0][:, half_cols(h)], in_=y_part[0, h][:])
        for t, h in ((1, 0), (2, 0), (1, 1), (3, 0), (2, 1), (3, 1)):
            nc.vector.tensor_copy(out=y_window[t][:, half_cols(h)], in_=y_part[t, h][:])

        h1 = keep.tile([P, PACK, HALF], F32, name="h1", align_bytes=64)
        h_sum = keep.tile([P, PACK, HALF], F32, name="h_sum", align_bytes=64)

        def fetch(out, t, lists, cols):
            nc.scalar.activation(out, y_window[t][:].indirect(entries(lists, cols)), COPY)

        first_h1 = [h1[:, 0, :], h1[:, 1, :], h1[:, 2, :], w1_raw[:, 0, :HALF]]
        for t in range(PACK):
            fetch(first_h1[t], t, p1_sb, half_cols(0))
        for t in range(PACK - 1):
            nc.vector.tensor_tensor(h_sum[:, t, :], y_window[t][:].indirect(entries(p2_sb, half_cols(0))), h1[:, t, :], ADD)
        for b in range(2):
            offsets = entries(p2_sb, block_cols(b))
            nc.vector.tensor_tensor(h_sum[:, 3, block_cols(b)], y_window[3][:].indirect(offsets), first_h1[3][:, block_cols(b)], ADD)
        deal(nc.gpsimd, "s34", w34_scales_raw[:], U8, reuse, offset=0)
        deal(nc.gpsimd, W4, w_raw[W4], I32, reuse, offset=8960)
        late = reuse.tile([P, PACK, BLK], F32, name="late", align_bytes=64, offset=512)
        third_h2 = late[:, : PACK - 1, :]
        last_h1 = reuse.tile([P, BLK], F32, name="last_h1", align_bytes=64, offset=13056)
        last_h2 = reuse.tile([P, PACK - 1, BLK], F32, name="last_h2", align_bytes=64, offset=13568)
        last_plane_h2 = reuse.tile([P, BLK], F32, name="last_plane_h2", align_bytes=64, offset=8448)
        h2 = {2: third_h2, 3: last_h2[:]}
        third_sum = reuse.tile([P, PACK, BLK], F32, name="third_sum", align_bytes=64, offset=11008)
        sums = [h_sum[:, :, block_cols(0)], h_sum[:, :, block_cols(1)], third_sum[:], late[:]]

        side = {}

        def side_products(b):
            for which, k, weights in ((Z, (0, 2, 1, 4)[b], w1_plane), (Z2, (1, 4, 0, 2)[b], lambda t: weight(W2, t))):
                side[b, which] = bank(k, [PACK, BLK], f"side{b}{which}")
                for t in range(PACK):
                    times_x(side[b, which][:, t, :], weights(t), block_cols(b))

        side_products(0)
        side_products(1)

        for t in range(PACK - 1):
            fetch(h1[:, t, :], t, p1_sb, half_cols(1))
        last_plane_h1 = {2: h1[:, 3, block_cols(0)], 3: last_h1[:]}
        fetch(last_plane_h1[2], 3, p1_sb, block_cols(2))
        for t in range(PACK - 1):
            fetch(h2[2][:, t, :], t, p2_sb, block_cols(2))
        for t in range(PACK - 1):
            fetch(h2[3][:, t, :], t, p2_sb, block_cols(3))
        fetch(last_plane_h1[3], 3, p1_sb, block_cols(3))
        fetch(last_plane_h2[:], 3, p2_sb, block_cols(3))

        z_bf = [keep.tile([P, 2, BLK, PACK], BF16, name=f"z_bf{b}", align_bytes=64) for b in range(2)]
        late_z = reuse.tile([P, 5, BLK, PACK], BF16, name="late_z", align_bytes=64, offset=24576)
        late_z2 = keep.tile([P, BLK, PACK], BF16, name="late_z2", align_bytes=64)
        third_z = reuse.tile([P, BLK, PACK], BF16, name="third_z", align_bytes=64, offset=30720)

        def z_values(b, which):
            return z_bf[b][:, which] if b < 2 else (third_z[:] if b == 2 else late_z[:, 0], late_z2[:])[which]
        by_lines = "p t (c i) -> p c t i"
        flat = "p j t -> p (j t)"

        def mix(b, which):
            nc.vector.tensor_tensor(
                z_values(b, which).rearrange("p (c i) t -> p c t i", i=LINE),
                sums[b].rearrange(by_lines, i=LINE),
                side[b, which][:].rearrange(by_lines, i=LINE),
                MULT if which == Z2 else ADD,
            )

        out_scales = keep.tile([P, S], U8, name="out_scales", align_bytes=64)
        out_rows = out_0.rearrange("(p t) j -> p t j", t=PACK)
        out_words = words_of(out_1)
        o_bank = {}
        o_tags = {0: (3,), 1: (5,), 2: (6,), 3: (7, 3)}

        def quantise(b, parts):
            width = BLK * len(parts)
            if b == 1:
                codes = reuse.tile([P, width], U32, name="codes1", align_bytes=64, offset=15104)
                scales = reuse.tile([P, width], U8, name="scales1", align_bytes=64, offset=16128)
            else:
                codes = keep.tile([P, width], U32, name=f"codes{b}{parts[0]}", align_bytes=64)
                scales = keep.tile([P, width], U8, name=f"scales{b}{parts[0]}", align_bytes=64)
            values = z_bf[b][:].rearrange("p w j t -> p (w j t)") if len(parts) == 2 else z_values(b, parts[0]).rearrange(flat)
            nc.vector.quantize_mx(out=codes[:].bitcast(FP8X4), scales=scales[:], in_=values)
            for i, which in enumerate(parts):
                first = b not in o_bank
                group = PACK // len(o_tags[b])
                if first:
                    o_bank[b] = [bank(k, [group, BLK], f"o_bank{b}{k}") for k in o_tags[b]]
                for t in range(PACK):
                    nc.tensor.matmul_mx(
                        out=o_bank[b][t // group][:, t % group, :],
                        **weight(W3 + which, t),
                        rhs=codes[:, block_cols(i)].bitcast(FP8X4),
                        rhs_scale=scales[:, block_cols(i)],
                        start=(first and t % group == 0),
                        stop=(not first and t % group == group - 1),
                    )

        early_f32 = keep.tile([P, PACK, HALF], F32, name="early_f32")
        early_bf = keep.tile([P, HALF, PACK], BF16, name="early_bf", tag="early_bf", align_bytes=64)
        last_bf = keep.tile([P, BLK, PACK], BF16, name="last_bf", align_bytes=64)

        def quantise_out(values, cols):
            nc.vector.quantize_mx(out=out_codes[:, cols].bitcast(FP8X4), scales=out_scales[:, cols], in_=values.rearrange(flat))

        def store_words(cols):
            nc.sync.dma_start(out=out_words[:, cols], in_=out_codes[:, cols].bitcast(I32))

        for b in range(2):
            mix(b, Z)
            mix(b, Z2)
            side_products(2 + b)
        quantise(0, (Z, Z2))

        def fetch_and_add_last_plane(b):
            nc.vector.tensor_tensor(sums[b][:, 3], y_window[3][:].indirect(entries(p2_sb, block_cols(b))), last_plane_h1[b], ADD)

        def add_pairs(engine, b):
            engine.tensor_tensor(sums[b][:, :3], h1[:, :3, block_cols(b - 2)], h2[b], ADD)

        fetch_and_add_last_plane(2)
        add_pairs(nc.vector, 2)
        quantise(1, (Z, Z2))
        add_pairs(nc.gpsimd, 3)
        for b in range(2):
            nc.scalar.activation(early_f32[:, :, block_cols(b)], o_bank[b][0][:], RELU)
            skip = POOL_SHARE if b == 0 else 0
            out = early_bf[:, b * BLK + skip : (b + 1) * BLK, :]
            nc.scalar.activation(out, o_bank[b][0][:, :, skip:].rearrange("p t j -> p j t"), RELU)
        nc.sync.dma_start(out=out_rows[:, :, half_cols(0)], in_=early_f32[:])
        mix(2, Z)
        mix(2, Z2)
        nc.vector.tensor_tensor(late[:, 3, :], last_plane_h2[:], last_h1[:], ADD)
        quantise(2, (Z,))
        quantise(2, (Z2,))
        first_bf = reuse.tile([P, POOL_SHARE, PACK], BF16, name="first_bf", align_bytes=64, offset=30720)
        nc.gpsimd.tensor_copy(out=first_bf[:], in_=early_f32[:, :, :POOL_SHARE].rearrange("p t j -> p j t"))
        mix(3, Z)
        third_f32 = keep.tile([P, PACK, BLK], F32, name="third_f32")
        nc.scalar.activation(third_f32[:], o_bank[2][0][:], RELU)
        nc.sync.dma_start(out=out_rows[:, :, block_cols(2)], in_=third_f32[:])
        mix(3, Z2)
        quantise(3, (Z,))
        quantise(3, (Z2,))
        out_codes = reuse.tile([P, S], U32, name="out_codes", align_bytes=64, offset=24576)
        third_bf = reuse.tile([P, BLK, PACK], BF16, name="third_bf", align_bytes=64, offset=24576 + 2048)
        quantise_out(early_bf[:, block_cols(1), :], block_cols(1))
        quantise_out(early_bf[:, POOL_SHARE:BLK, :], slice(POOL_SHARE, BLK))
        quantise_out(first_bf[:], slice(0, POOL_SHARE))
        store_words(half_cols(0))
        nc.vector.tensor_copy(out=third_bf[:].rearrange("p (c i) t -> p c t i", i=PACK), in_=third_f32[:].rearrange(by_lines, i=PACK))
        low, high = o_bank[LAST]
        last_f32 = reuse.tile([P, PACK, BLK], F32, name="last_f32", align_bytes=64, offset=24576 + 3072)
        nc.scalar.activation(last_f32[:, :2, :], low[:], RELU)
        nc.vector.tensor_scalar_max(last_f32[:, 2:, :], high[:], 0.0)
        nc.sync.dma_start(out=out_rows[:, :, block_cols(LAST)], in_=last_f32[:])
        nc.scalar.activation(last_bf[:, :, :2], low[:].rearrange("p e j -> p j e"), RELU)
        nc.vector.tensor_scalar_max(last_bf[:, :, 2:], high[:].rearrange("p e j -> p j e"), 0.0)
        quantise_out(third_bf[:], block_cols(2))
        quantise_out(last_bf[:], block_cols(LAST))
        store_words(half_cols(1))

        for q, queue in enumerate((nc.sync, nc.scalar, nc.sync, nc.scalar)):
            queue.dma_start(
                out=out_2[0, SCALE_ROWS * q : SCALE_ROWS * (q + 1), :].bitcast(I32),
                in_=out_scales[QUADRANT * q : QUADRANT * q + SCALE_ROWS, :].bitcast(I32),
            )
